import numpy as np
import ml_dtypes


def mxq(x, axis, fmt="e4m3"):
    dtype, down = {"e4m3": (ml_dtypes.float8_e4m3fn, 7), "e5m2": (ml_dtypes.float8_e5m2, 14)}[fmt]
    v = np.moveaxis(np.asarray(x, np.float32).astype(ml_dtypes.bfloat16).astype(np.float64), axis, -1)
    blocks = v.reshape(v.shape[:-1] + (-1, 32))
    amax = np.abs(blocks).max(-1, keepdims=True)
    byte = np.maximum(np.where(amax > 0, np.frexp(amax)[1] - 1 + 127, 0) - down, 1)
    scale = np.exp2(byte - 127.0)
    codes = (blocks / scale).astype(np.float32).astype(dtype).astype(np.float64)
    return np.moveaxis((codes * scale).reshape(v.shape), -1, axis)


WIDE = False


def mx_kscale(k):
    if not WIDE:
        return np.ones(k)
    levels = np.array([10, -10, 5, -5, 0])
    if k % 512:
        return np.exp2(np.random.permutation(np.resize(levels, k // 32))).repeat(32)
    a = np.empty((k // 512, 16))
    for p in range(k // 512):
        a[p, :8] = np.random.permutation(np.resize(levels, 8))
        for g in range(8):
            far = levels[np.abs(levels - a[p, g]) >= 10]
            a[p, g + 8] = far[np.random.randint(len(far))]
    return np.exp2(a.ravel()).repeat(32)


def f64(x):
    return np.asarray(x).astype(np.float64)


def striped(idx):
    return np.tile(idx.reshape(-1, 16).T, (8, 1)).astype(np.uint16)


def unstriped(offs):
    return offs[:16].T.reshape(-1).astype(np.int64)


E2M1 = np.array([0.0, 0.5, 1.0, 1.5, 2.0, 3.0, 4.0, 6.0, -0.0, -0.5, -1.0, -1.5, -2.0, -3.0, -4.0, -6.0])


def pack_weight(w, fmt):
    k, n = w.shape
    w = f64(np.asarray(w, np.float32).astype(ml_dtypes.bfloat16)).reshape(k // 32, 32, n)
    amax = np.abs(w).max(1)
    if fmt == "e4m3":
        byte = np.frexp(amax)[1] - 1 + 127 - 7
    else:
        mant, ex = np.frexp(amax / 6.0)
        byte = np.where(mant > 0.5, ex, ex - 1) + 127
    byte = np.clip(np.where(amax > 0, byte, 1), 1, 254)
    scaled = (w * np.exp2(127.0 - byte)[:, None, :]).reshape(k, n).astype(np.float32)
    by_word = np.ascontiguousarray(scaled.reshape(k // 512, 128, 4, n).transpose(0, 1, 3, 2))
    if fmt == "e4m3":
        words = by_word.astype(ml_dtypes.float8_e4m3fn).view(np.uint8)
    else:
        c = by_word.astype(ml_dtypes.float4_e2m1fn).view(np.uint8) & 0xF
        words = (c[..., 0::2] | (c[..., 1::2] << 4)).reshape(k // 512, 128, 2 * n)
    return np.ascontiguousarray(words), np.ascontiguousarray(byte.astype(np.uint8).reshape(k // 512, 16, n))


def unpack_weight(words, scales, fmt):
    g, _, n = scales.shape
    words = np.ascontiguousarray(words).reshape(g, 128, n, -1)
    if fmt == "e4m3":
        vals = words.view(ml_dtypes.float8_e4m3fn).astype(np.float64)
    else:
        nib = np.empty((g, 128, n, 4), np.uint8)
        nib[..., 0::2] = words & 0xF
        nib[..., 1::2] = words >> 4
        vals = E2M1[nib]
    vals = vals * np.repeat(np.exp2(scales.astype(np.float64) - 127.0), 8, axis=1)[..., None]
    return vals.transpose(0, 1, 3, 2).reshape(g * 512, n)


def gelu(v):
    return 0.5 * v * (1.0 + np.tanh(np.sqrt(2.0 / np.pi) * (v + 0.044715 * v**3)))


def bf(x):
    return np.asarray(x, np.float32).astype(ml_dtypes.bfloat16)

def planes(Y):
    n, m = Y.shape
    b = f64(bf(Y)).reshape(n // 32, 32, m)
    amax = np.abs(b).max(1)
    byte = np.clip(np.where(amax > 0, np.frexp(amax)[1] - 1 + 127 - 7, 1), 1, 254)
    codes = (b * np.exp2(127.0 - byte)[:, None, :]).reshape(n, m).astype(np.float32).astype(ml_dtypes.float8_e4m3fn).view(np.uint8)
    words = codes.reshape(n // 512, 128, 4, m).transpose(0, 1, 3, 2)
    return np.ascontiguousarray(words), np.ascontiguousarray(byte.astype(np.uint8).reshape(n // 512, 16, m))


K, H, T, S, T2, S2 = 1536, 1024, 2048, 512, 4096, 1536

def setup_inputs():
    n = np.random.standard_normal
    s = mx_kscale(K)[:, None]
    u = mx_kscale(H)[:, None]
    tab_words, tab_scales = pack_weight(n((K, T)) * s, "e4m3")
    tab2_words, tab2_scales = pack_weight(n((H, T2)) / np.sqrt(H) / u, "e4m3")
    ws_words, ws_scales = pack_weight(0.5 * n((K, H)) / np.sqrt(K) / s, "e2m1")
    return {
        "tab_words": tab_words, "tab_scales": tab_scales,
        "offs": striped(np.random.permutation(T)[:S]),
        "tab2_words": tab2_words, "tab2_scales": tab2_scales,
        "offs2": striped(np.random.permutation(T2)[:S2]),
        "wm": (n((K, H)) / np.sqrt(K) / s * u.T).astype(np.float32),
        "ws_words": ws_words, "ws_scales": ws_scales,
        "bs": (0.3 * n(H) - 0.4).astype(np.float32),
        "eps": (n((H, S)) * u).astype(np.float32),
        "pay": np.exp(0.8 * n(S2)).astype(np.float32),
    }

def reference(tab_words, tab_scales, offs, tab2_words, tab2_scales, offs2, wm, ws_words, ws_scales, bs, eps, pay):
    v = unpack_weight(tab_words, tab_scales, "e4m3")[:, unstriped(offs)]
    v2 = unpack_weight(tab2_words, tab2_scales, "e4m3")[:, unstriped(offs2)]
    ws = unpack_weight(ws_words, ws_scales, "e2m1")
    mean = mxq(f64(wm), 0, "e4m3").T @ v
    logsc = (ws.T @ v) + f64(bs)[:, None]
    h = mean + np.exp(logsc) * f64(eps)
    y = f64(pay)[:, None] * (v2.T @ mxq(h, 0, "e4m3"))
    words, scales = planes(y)
    return y, words, scales

@@ -1,0 +1,297 @@
+from contextlib import ExitStack
+
+import concourse.mybir as mybir
+
+K, H, T, S, T2, S2 = 1536, 1024, 2048, 512, 4096, 1536
+FLOPS = 2 * (2 * K * H * S + H * S2 * S)
+
+F32 = mybir.dt.float32
+BF16 = mybir.dt.bfloat16
+I32 = mybir.dt.int32
+U32 = mybir.dt.uint32
+U16 = mybir.dt.uint16
+U8 = mybir.dt.uint8
+FP8X4 = mybir.dt.float8_e4m3fn_x4
+FP4X4 = mybir.dt.float4_e2m1fn_x4
+ALU = mybir.AluOpType
+ACT = mybir.ActivationFunctionType
+
+P = 128
+PACK = 4
+PASS = P * PACK
+KA = K // PASS
+HB = H // PASS
+YG = S2 // PASS
+LIST_COLS = PASS // 16
+
+
+def tile_list_thompson_arm_rewards_kernel(
+    tc, tab_words, tab_scales, offs, tab2_words, tab2_scales, offs2, wm, ws_words, ws_scales, bs, eps, pay,
+    out_0, out_1, out_2,
+):
+    nc = tc.nc
+    with ExitStack() as ctx:
+        keep = ctx.enter_context(tc.tile_pool(name="keep", bufs=1))
+        ring = ctx.enter_context(tc.tile_pool(name="ring", bufs=1))
+        psum = ctx.enter_context(tc.psum_pool(name="psum", bufs=1))
+
+        def held(shape, dtype, name):
+            return keep.tile(shape, dtype, name=name, align_bytes=64)
+
+        def f32_block(name):
+            return ring.tile([P, PACK, PASS], F32, name=name, tag="f32_block", bufs=6, align_bytes=64)
+
+        idx = keep.tile([P, S // 16], U16, name="idx")
+        idx2 = keep.tile([P, S2 // 16], U16, name="idx2")
+        nc.sync.dma_start(idx[:], offs)
+        nc.sync.dma_start(idx2[:], offs2)
+
+        tab_sc = held([P, T], U8, "tab_sc")
+        ws_sc = held([P, H], U8, "ws_sc")
+        v_sc_low = [held([P, S], U8, "v_sc_low%d" % a) for a in range(1, KA)]
+        ws_sc_low = [held([P, H], U8, "ws_sc_low%d" % a) for a in range(1, KA)]
+        for plane in v_sc_low + ws_sc_low:
+            nc.gpsimd.memset(plane[:].bitcast(I32), 0)
+        tab2_sc = held([P, T2], U8, "tab2_sc")
+        for plane in (tab_sc, ws_sc, tab2_sc):
+            nc.vector.memset(plane[:].bitcast(I32), 0)
+
+        def load_scales(src, dst):
+            for q in range(4):
+                nc.sync.dma_start(
+                    out=dst[32 * q : 32 * q + 4 * KA, :].bitcast(I32), in_=src[:, 4 * q : 4 * q + 4, :].bitcast(I32)
+                )
+
+        def load_arm_scales(b, r):
+            rows = tab2_scales[b].rearrange("(q r) t -> r q t", r=4)
+            nc.sync.dma_start(out=tab2_sc[8 + 4 * b + r : P : 32, :].bitcast(I32), in_=rows[r].bitcast(I32))
+
+        wm_raw = {}
+        tab_w, eps_sb, tab2_w = [], [], []
+
+        def load_wm(b, a):
+            raw = f32_block("wm_raw%d%d" % (b, a))
+            nc.sync.dma_start(
+                out=raw[:],
+                in_=wm[a * PASS : (a + 1) * PASS, b * PASS : (b + 1) * PASS].rearrange("(p j) c -> p j c", j=PACK),
+            )
+            wm_raw[(b, a)] = raw
+
+        def load_words(src, a, width, name, into):
+            w = held([P, width], I32, name)
+            nc.sync.dma_start(out=w[:], in_=src[a].rearrange("p n t -> p (n t)").bitcast(I32))
+            into.append(w)
+
+        def load_eps(b):
+            e = held([P, PACK, S], F32, "eps%d" % b)
+            nc.sync.dma_start(out=e[:], in_=eps[b * PASS : (b + 1) * PASS, :].rearrange("(p t) j -> p t j", t=PACK))
+            eps_sb.append(e)
+
+        bs_sb = held([P, HB, PACK], F32, "bs_sb")
+        pay_sb = held([P, YG, PACK], F32, "pay_sb")
+        ws_w = held([P, KA, H // 2], I32, "ws_w")
+        load_wm(0, 0)
+        load_scales(tab_scales, tab_sc)
+        load_words(tab_words, 0, T, "tab_w0", tab_w)
+        load_scales(ws_scales, ws_sc)
+        nc.sync.dma_start(out=ws_w[:], in_=ws_words.rearrange("a p c -> p a c").bitcast(I32))
+        load_wm(0, 1)
+        for r in range(4):
+            load_arm_scales(0, r)
+        load_words(tab_words, 1, T, "tab_w1", tab_w)
+        load_wm(0, 2)
+        for r in range(4):
+            load_arm_scales(1, r)
+        load_words(tab_words, 2, T, "tab_w2", tab_w)
+        nc.sync.dma_start(out=bs_sb[:], in_=bs.rearrange("(b p t) -> p b t", p=P, t=PACK))
+        load_eps(0)
+        for a in range(KA):
+            load_wm(1, a)
+        load_eps(1)
+        nc.sync.dma_start(out=pay_sb[:], in_=pay.rearrange("(g p t) -> p g t", p=P, t=PACK))
+        for a in range(HB):
+            load_words(tab2_words, a, T2, "tab2_w%d" % a, tab2_w)
+
+        v_sc = held([P, S], U8, "v_sc")
+        ws_sc_d = held([P, H], U8, "ws_sc_d")
+        v_sc0 = [v_sc] + v_sc_low
+        ws_sc0 = [ws_sc_d] + ws_sc_low
+
+        wm_q, wm_s = {}, {}
+
+        def cast_wm(b, a):
+            g = ring.tile([P, PACK, P, PACK], BF16, name="wm_bf%d%d" % (b, a), tag="wm_bf", bufs=3, align_bytes=64)
+            nc.scalar.copy(
+                out=g[:].rearrange("p t m j -> p m j t"),
+                in_=wm_raw[(b, a)][:].rearrange("p j (m t) -> p m j t", t=PACK),
+            )
+            return g
+
+        def quant_wm(b, a, g):
+            wm_q[(b, a)] = held([P, PASS], U32, "wm_q%d%d" % (b, a))
+            wm_s[(b, a)] = held([P, PASS], U8, "wm_s%d%d" % (b, a))
+            nc.vector.quantize_mx(
+                out=wm_q[(b, a)][:].bitcast(FP8X4), scales=wm_s[(b, a)][:], in_=g[:].rearrange("p t m j -> p (t m j)")
+            )
+
+        def bank(n):
+            return psum.tile([P, PASS], F32, name="bank%d" % n, tag="bank%d" % n)
+
+        v_w, ws_d = [], []
+        mean_banks = {}
+
+        def mean_pass(b, a):
+            if a == 0:
+                mean_banks[b] = [bank(4 + jq) for jq in range(4)]
+            for jq in range(4):
+                js = slice(jq * P, (jq + 1) * P)
+                for t in range(PACK):
+                    ms = slice(t * P, (t + 1) * P)
+                    nc.tensor.matmul_mx(
+                        out=mean_banks[b][jq][:, ms],
+                        lhsT=wm_q[(b, a)][:, ms].bitcast(FP8X4),
+                        lhsT_scale=wm_s[(b, a)][:, ms],
+                        rhs=v_w[a][:, js].bitcast(FP8X4),
+                        rhs_scale=v_sc[4 * a : P, js],
+                        start=(a == 0 and t == 0),
+                        stop=(a == KA - 1 and t == PACK - 1),
+                    )
+
+        log_banks = {}
+
+        def log_pass(b, a):
+            if a == 0:
+                log_banks[b] = [bank(t) for t in range(PACK)]
+            for t in range(PACK):
+                c0 = b * PASS + t * P
+                nc.tensor.matmul_mx(
+                    out=log_banks[b][t][:],
+                    lhsT=ws_d[a][:, 2 * c0 : 2 * (c0 + P)].bitcast(FP4X4),
+                    lhsT_scale=ws_sc0[a][:, c0 : c0 + P],
+                    rhs=v_w[a][:].bitcast(FP8X4),
+                    rhs_scale=v_sc0[a][:],
+                    start=(a == 0),
+                    stop=(a == KA - 1),
+                )
+
+        noise = {}
+
+        def exp_stage(b):
+            noise[b] = held([P, PACK, S], F32, "noise%d" % b)
+            for t in range(PACK):
+                nc.scalar.activation(
+                    out=noise[b][:, t, :], in_=log_banks[b][t][:], func=ACT.Exp, bias=bs_sb[:, b, t : t + 1]
+                )
+
+        def eps_stage(b):
+            for t in range(PACK):
+                nc.vector.tensor_tensor(noise[b][:, t, :], noise[b][:, t, :], eps_sb[b][:, t, :], ALU.mult)
+
+        h_q, h_s = {}, {}
+
+        def woven(name):
+            return ring.tile([P, S, PACK], BF16, name=name, tag="woven", bufs=2, align_bytes=64)
+
+        def h_stage(b):
+            hb = woven("h_bf%d" % b)
+            for jq in range(4):
+                js = slice(jq * P, (jq + 1) * P)
+                nc.vector.tensor_tensor(
+                    hb[:, js, :].rearrange("p (c i) t -> p c t i", i=4),
+                    mean_banks[b][jq][:].rearrange("p (t c i) -> p c t i", t=PACK, i=4),
+                    noise[b][:, :, js].rearrange("p t (c i) -> p c t i", i=4),
+                    ALU.add,
+                )
+            h_q[b] = held([P, S], U32, "h_q%d" % b)
+            h_s[b] = held([P, S], U8, "h_s%d" % b)
+            nc.vector.quantize_mx(out=h_q[b][:].bitcast(FP8X4), scales=h_s[b][:], in_=hb[:].rearrange("p j t -> p (j t)"))
+
+        v2_sc = held([P, S2], U8, "v2_sc")
+        v2_sc_d = held([P, S2], U8, "v2_sc_d")
+        nc.vector.tensor_copy(v_sc[:], tab_sc[:].indirect(idx[:]))
+        nc.vector.tensor_copy(
+            ws_sc_d[:].rearrange("p (b t m) -> p b t m", b=HB, t=PACK),
+            ws_sc[:].rearrange("p (b m t) -> p b t m", b=HB, t=PACK),
+        )
+        for a in range(1, KA):
+            nc.gpsimd.dma_start(out=v_sc_low[a - 1][0:112, :].bitcast(I32), in_=v_sc[4 * a : 4 * a + 112, :].bitcast(I32))
+            nc.gpsimd.dma_start(out=ws_sc_low[a - 1][0:112, :].bitcast(I32), in_=ws_sc_d[4 * a : 4 * a + 112, :].bitcast(I32))
+        for a in range(KA):
+            g = cast_wm(0, a)
+            vw = held([P, S], U32, "v_w%d" % a)
+            nc.vector.tensor_copy(vw[:], tab_w[a][:].bitcast(U32).indirect(idx[:]))
+            v_w.append(vw)
+            wd = held([P, 2 * H], U8, "ws_d%d" % a)
+            nc.vector.tensor_copy(
+                wd[:].bitcast(U16).rearrange("p (b t m) -> p b t m", b=HB, t=PACK),
+                ws_w[:, a, :].bitcast(U16).rearrange("p (b m t) -> p b t m", b=HB, t=PACK),
+            )
+            ws_d.append(wd)
+            quant_wm(0, a, g)
+            mean_pass(0, a)
+            log_pass(0, a)
+        nc.vector.tensor_copy(v2_sc[:], tab2_sc[:].indirect(idx2[:]))
+        nc.vector.tensor_copy(
+            v2_sc_d[:].rearrange("p (g t m) -> p g t m", g=YG, t=PACK),
+            v2_sc[:].rearrange("p (g m t) -> p g t m", g=YG, t=PACK),
+        )
+        exp_stage(0)
+        for a in range(KA):
+            log_pass(1, a)
+        eps_stage(0)
+        h_stage(0)
+        exp_stage(1)
+        for a in range(KA):
+            g = cast_wm(1, a)
+            quant_wm(1, a, g)
+            mean_pass(1, a)
+        eps_stage(1)
+        h_stage(1)
+
+        v2_w = {}
+
+        def gather_arms(b, g):
+            w = held([P, PACK, P], U32, "v2_w%d%d" % (b, g))
+            nc.vector.tensor_copy(
+                w[:].rearrange("p t m -> p m t"),
+                tab2_w[b][:].bitcast(U32).indirect(idx2[:, g * LIST_COLS : (g + 1) * LIST_COLS]),
+            )
+            v2_w[(b, g)] = w
+
+        for b in range(HB):
+            for g in range(YG):
+                gather_arms(b, g)
+
+        y_s = held([P, YG, S], U8, "y_s")
+        for g in range(YG):
+            banks = [bank(4 * (g % 2) + t) for t in range(PACK)]
+            for b in range(HB):
+                for t in range(PACK):
+                    c0 = g * PASS + t * P
+                    nc.tensor.matmul_mx(
+                        out=banks[t][:],
+                        lhsT=v2_w[(b, g)][:, t, :].bitcast(FP8X4),
+                        lhsT_scale=v2_sc_d[8 + 4 * b : P, c0 : c0 + P],
+                        rhs=h_q[b][:].bitcast(FP8X4),
+                        rhs_scale=h_s[b][:],
+                        start=(b == 0),
+                        stop=(b == HB - 1),
+                    )
+            y = f32_block("y%d" % g)
+            rows = out_0[g * PASS : (g + 1) * PASS, :].rearrange("(p t) j -> p t j", t=PACK)
+            for t in range(PACK):
+                nc.scalar.activation(out=y[:, t, :], in_=banks[t][:], func=ACT.Copy, scale=pay_sb[:, g, t : t + 1])
+                if t % 2 == 1:
+                    nc.sync.dma_start(out=rows[:, t - 1 : t + 1, :], in_=y[:, t - 1 : t + 1, :])
+            yb = woven("y_bf%d" % g)
+            nc.vector.tensor_copy(
+                yb[:].rearrange("p (c i) t -> p c t i", i=4), y[:].rearrange("p t (c i) -> p c t i", i=4)
+            )
+            y_q = held([P, S], I32, "y_q%d" % g)
+            nc.vector.quantize_mx(out=y_q[:].bitcast(FP8X4), scales=y_s[:, g, :], in_=yb[:].rearrange("p j t -> p (j t)"))
+            nc.sync.dma_start(out=out_1[g].rearrange("p m t -> p (m t)").bitcast(I32), in_=y_q[:])
+        for q in range(4):
+            nc.sync.dma_start(
+                out=out_2[:, 4 * q : 4 * q + 4, :].rearrange("g r m -> r g m").bitcast(I32),
+                in_=y_s[32 * q : 32 * q + 4, :, :].bitcast(I32),
+            )

@@ -44,30 +44,24 @@ def tile_list_thompson_arm_rewards_kernel(
         idx = keep.tile([P, S // 16], U16, name="idx")
         idx2 = keep.tile([P, S2 // 16], U16, name="idx2")
         nc.sync.dma_start(idx[:], offs)
-        nc.sync.dma_start(idx2[:], offs2)
 
-        tab_sc = held([P, T], U8, "tab_sc")
-        ws_sc = held([P, H], U8, "ws_sc")
-        v_sc_low = [held([P, S], U8, "v_sc_low%d" % a) for a in range(1, KA)]
-        ws_sc_low = [held([P, H], U8, "ws_sc_low%d" % a) for a in range(1, KA)]
-        for plane in v_sc_low + ws_sc_low:
-            nc.gpsimd.memset(plane[:].bitcast(I32), 0)
+        tab_sc = held([P, KA, T], U8, "tab_sc")
+        ws_sc = held([P, KA, H], U8, "ws_sc")
         tab2_sc = held([P, T2], U8, "tab2_sc")
         for plane in (tab_sc, ws_sc, tab2_sc):
             nc.vector.memset(plane[:].bitcast(I32), 0)
 
         def load_scales(src, dst):
-            for q in range(4):
-                nc.sync.dma_start(
-                    out=dst[32 * q : 32 * q + 4 * KA, :].bitcast(I32), in_=src[:, 4 * q : 4 * q + 4, :].bitcast(I32)
-                )
+            rows = src.rearrange("a (q r) t -> r q a t", r=4)
+            for r in range(4):
+                nc.sync.dma_start(out=dst[r:P:32, :, :].bitcast(I32), in_=rows[r].bitcast(I32))
 
         def load_arm_scales(b, r):
             rows = tab2_scales[b].rearrange("(q r) t -> r q t", r=4)
             nc.sync.dma_start(out=tab2_sc[8 + 4 * b + r : P : 32, :].bitcast(I32), in_=rows[r].bitcast(I32))
 
         wm_raw = {}
-        tab_w, eps_sb, tab2_w = [], [], []
+        tab_w, ws_w, eps_sb, tab2_w = [], [], [], []
 
         def load_wm(b, a):
             raw = f32_block("wm_raw%d%d" % (b, a))
@@ -77,8 +71,8 @@ def tile_list_thompson_arm_rewards_kernel(
             )
             wm_raw[(b, a)] = raw
 
-        def load_words(src, a, width, name, into):
-            w = held([P, width], I32, name)
+        def load_words(src, a, width, name, into, pool, tag):
+            w = pool.tile([P, width], I32, name=name, tag=tag, bufs=src.shape[0], align_bytes=64)
             nc.sync.dma_start(out=w[:], in_=src[a].rearrange("p n t -> p (n t)").bitcast(I32))
             into.append(w)
 
@@ -89,41 +83,48 @@ def tile_list_thompson_arm_rewards_kernel(
 
         bs_sb = held([P, HB, PACK], F32, "bs_sb")
         pay_sb = held([P, YG, PACK], F32, "pay_sb")
-        ws_w = held([P, KA, H // 2], I32, "ws_w")
+        def load_ws(a):
+            w = held([P, H // 2], I32, "ws_w%d" % a)
+            nc.sync.dma_start(out=w[:], in_=ws_words[a].bitcast(I32))
+            ws_w.append(w)
+
+        def arm_scales(b, rows):
+            for r in rows:
+                load_arm_scales(b, r)
+
+        nc.sync.dma_start(out=bs_sb[:], in_=bs.rearrange("(b p t) -> p b t", p=P, t=PACK))
+        load_ws(0)
+        nc.sync.dma_start(idx2[:], offs2)
+        nc.sync.dma_start(out=pay_sb[:], in_=pay.rearrange("(g p t) -> p g t", p=P, t=PACK))
+        load_ws(1)
+        load_ws(2)
         load_wm(0, 0)
         load_scales(tab_scales, tab_sc)
-        load_words(tab_words, 0, T, "tab_w0", tab_w)
-        load_scales(ws_scales, ws_sc)
-        nc.sync.dma_start(out=ws_w[:], in_=ws_words.rearrange("a p c -> p a c").bitcast(I32))
+        load_words(tab_words, 0, T, "tab_w0", tab_w, ring, "tab_block")
+        arm_scales(0, range(4))
+        load_words(tab_words, 1, T, "tab_w1", tab_w, ring, "tab_block")
+        arm_scales(1, range(4))
         load_wm(0, 1)
-        for r in range(4):
-            load_arm_scales(0, r)
-        load_words(tab_words, 1, T, "tab_w1", tab_w)
+        load_scales(ws_scales, ws_sc)
+        load_words(tab_words, 2, T, "tab_w2", tab_w, ring, "tab_block")
         load_wm(0, 2)
-        for r in range(4):
-            load_arm_scales(1, r)
-        load_words(tab_words, 2, T, "tab_w2", tab_w)
-        nc.sync.dma_start(out=bs_sb[:], in_=bs.rearrange("(b p t) -> p b t", p=P, t=PACK))
         load_eps(0)
-        for a in range(KA):
-            load_wm(1, a)
+        load_words(tab2_words, 0, T2, "tab2_w0", tab2_w, keep, "tab2_block")
+        load_wm(1, 0)
+        load_wm(1, 1)
+        load_wm(1, 2)
         load_eps(1)
-        nc.sync.dma_start(out=pay_sb[:], in_=pay.rearrange("(g p t) -> p g t", p=P, t=PACK))
-        for a in range(HB):
-            load_words(tab2_words, a, T2, "tab2_w%d" % a, tab2_w)
+        load_words(tab2_words, 1, T2, "tab2_w1", tab2_w, keep, "tab2_block")
 
-        v_sc = held([P, S], U8, "v_sc")
-        ws_sc_d = held([P, H], U8, "ws_sc_d")
-        v_sc0 = [v_sc] + v_sc_low
-        ws_sc0 = [ws_sc_d] + ws_sc_low
+        v_sc, ws_sc_d = [], []
 
         wm_q, wm_s = {}, {}
 
         def cast_wm(b, a):
             g = ring.tile([P, PACK, P, PACK], BF16, name="wm_bf%d%d" % (b, a), tag="wm_bf", bufs=3, align_bytes=64)
             nc.scalar.copy(
-                out=g[:].rearrange("p t m j -> p m j t"),
-                in_=wm_raw[(b, a)][:].rearrange("p j (m t) -> p m j t", t=PACK),
+                out=g[:].rearrange("p (u e) m j -> p u m j e", e=2),
+                in_=wm_raw[(b, a)][:].rearrange("p j (m u e) -> p u m j e", u=2, e=2),
             )
             return g
 
@@ -142,7 +143,7 @@ def tile_list_thompson_arm_rewards_kernel(
 
         def mean_pass(b, a):
             if a == 0:
-                mean_banks[b] = [bank(4 + jq) for jq in range(4)]
+                mean_banks[b] = [bank(4 * (1 - b) + jq) for jq in range(4)]
             for jq in range(4):
                 js = slice(jq * P, (jq + 1) * P)
                 for t in range(PACK):
@@ -152,7 +153,7 @@ def tile_list_thompson_arm_rewards_kernel(
                         lhsT=wm_q[(b, a)][:, ms].bitcast(FP8X4),
                         lhsT_scale=wm_s[(b, a)][:, ms],
                         rhs=v_w[a][:, js].bitcast(FP8X4),
-                        rhs_scale=v_sc[4 * a : P, js],
+                        rhs_scale=v_sc[a][:, js],
                         start=(a == 0 and t == 0),
                         stop=(a == KA - 1 and t == PACK - 1),
                     )
@@ -167,9 +168,9 @@ def tile_list_thompson_arm_rewards_kernel(
                 nc.tensor.matmul_mx(
                     out=log_banks[b][t][:],
                     lhsT=ws_d[a][:, 2 * c0 : 2 * (c0 + P)].bitcast(FP4X4),
-                    lhsT_scale=ws_sc0[a][:, c0 : c0 + P],
+                    lhsT_scale=ws_sc_d[a][:, c0 : c0 + P],
                     rhs=v_w[a][:].bitcast(FP8X4),
-                    rhs_scale=v_sc0[a][:],
+                    rhs_scale=v_sc[a][:],
                     start=(a == 0),
                     stop=(a == KA - 1),
                 )
@@ -177,7 +178,7 @@ def tile_list_thompson_arm_rewards_kernel(
         noise = {}
 
         def exp_stage(b):
-            noise[b] = held([P, PACK, S], F32, "noise%d" % b)
+            noise[b] = ring.tile([P, PACK, S], F32, name="noise%d" % b, tag="tab_block", bufs=KA, align_bytes=64)
             for t in range(PACK):
                 nc.scalar.activation(
                     out=noise[b][:, t, :], in_=log_banks[b][t][:], func=ACT.Exp, bias=bs_sb[:, b, t : t + 1]
@@ -208,63 +209,81 @@ def tile_list_thompson_arm_rewards_kernel(
 
         v2_sc = held([P, S2], U8, "v2_sc")
         v2_sc_d = held([P, S2], U8, "v2_sc_d")
-        nc.vector.tensor_copy(v_sc[:], tab_sc[:].indirect(idx[:]))
-        nc.vector.tensor_copy(
-            ws_sc_d[:].rearrange("p (b t m) -> p b t m", b=HB, t=PACK),
-            ws_sc[:].rearrange("p (b m t) -> p b t m", b=HB, t=PACK),
-        )
-        for a in range(1, KA):
-            nc.gpsimd.dma_start(out=v_sc_low[a - 1][0:112, :].bitcast(I32), in_=v_sc[4 * a : 4 * a + 112, :].bitcast(I32))
-            nc.gpsimd.dma_start(out=ws_sc_low[a - 1][0:112, :].bitcast(I32), in_=ws_sc_d[4 * a : 4 * a + 112, :].bitcast(I32))
-        for a in range(KA):
-            g = cast_wm(0, a)
-            vw = held([P, S], U32, "v_w%d" % a)
-            nc.vector.tensor_copy(vw[:], tab_w[a][:].bitcast(U32).indirect(idx[:]))
-            v_w.append(vw)
+
+        def deal_ws(a):
             wd = held([P, 2 * H], U8, "ws_d%d" % a)
             nc.vector.tensor_copy(
                 wd[:].bitcast(U16).rearrange("p (b t m) -> p b t m", b=HB, t=PACK),
-                ws_w[:, a, :].bitcast(U16).rearrange("p (b m t) -> p b t m", b=HB, t=PACK),
+                ws_w[a][:].bitcast(U16).rearrange("p (b m t) -> p b t m", b=HB, t=PACK),
             )
             ws_d.append(wd)
-            quant_wm(0, a, g)
-            mean_pass(0, a)
-            log_pass(0, a)
-        nc.vector.tensor_copy(v2_sc[:], tab2_sc[:].indirect(idx2[:]))
-        nc.vector.tensor_copy(
-            v2_sc_d[:].rearrange("p (g t m) -> p g t m", g=YG, t=PACK),
-            v2_sc[:].rearrange("p (g m t) -> p g t m", g=YG, t=PACK),
-        )
-        exp_stage(0)
-        for a in range(KA):
-            log_pass(1, a)
-        eps_stage(0)
-        h_stage(0)
-        exp_stage(1)
-        for a in range(KA):
-            g = cast_wm(1, a)
-            quant_wm(1, a, g)
-            mean_pass(1, a)
-        eps_stage(1)
-        h_stage(1)
+
+        def deal_ws_scales(a):
+            sd = held([P, H], U8, "ws_sc_d%d" % a)
+            nc.vector.tensor_copy(
+                sd[:].rearrange("p (b t m) -> p b t m", b=HB, t=PACK),
+                ws_sc[:, a, :].rearrange("p (b m t) -> p b t m", b=HB, t=PACK),
+            )
+            ws_sc_d.append(sd)
+
+        def gather_visitors(a):
+            vs = held([P, S], U8, "v_sc%d" % a)
+            nc.vector.tensor_copy(vs[:], tab_sc[:, a, :].indirect(idx[:]))
+            v_sc.append(vs)
+            vw = held([P, S], U32, "v_w%d" % a)
+            nc.vector.tensor_copy(vw[:], tab_w[a][:].bitcast(U32).indirect(idx[:]))
+            v_w.append(vw)
+
+        def arm_scale_stage(g):
+            cols = slice(g * PASS, (g + 1) * PASS)
+            nc.vector.tensor_copy(v2_sc[:, cols], tab2_sc[:].indirect(idx2[:, g * LIST_COLS : (g + 1) * LIST_COLS]))
+            nc.vector.tensor_copy(
+                v2_sc_d[:, cols].rearrange("p (t m) -> p t m", t=PACK),
+                v2_sc[:, cols].rearrange("p (m t) -> p t m", t=PACK),
+            )
 
         v2_w = {}
 
         def gather_arms(b, g):
+            listed = ring.tile([P, PASS], U32, name="listed%d%d" % (b, g), tag="listed", bufs=2, align_bytes=64)
+            nc.vector.tensor_copy(listed[:], tab2_w[b][:].bitcast(U32).indirect(idx2[:, g * LIST_COLS : (g + 1) * LIST_COLS]))
             w = held([P, PACK, P], U32, "v2_w%d%d" % (b, g))
             nc.vector.tensor_copy(
-                w[:].rearrange("p t m -> p m t"),
-                tab2_w[b][:].bitcast(U32).indirect(idx2[:, g * LIST_COLS : (g + 1) * LIST_COLS]),
+                w[:].rearrange("p (u e) m -> p u m e", e=2), listed[:].rearrange("p (m u e) -> p u m e", u=2, e=2)
             )
             v2_w[(b, g)] = w
 
+        def wm_stage(b, a):
+            quant_wm(b, a, cast_wm(b, a))
+            mean_pass(b, a)
+
+        for a in range(KA):
+            deal_ws(a)
+        for a in range(KA):
+            gather_visitors(a)
+            deal_ws_scales(a)
+            log_pass(0, a)
+        exp_stage(0)
+        for a in range(KA):
+            log_pass(1, a)
+        exp_stage(1)
+        for a in range(KA):
+            wm_stage(0, a)
+        eps_stage(0)
+        h_stage(0)
+        for a in range(KA):
+            wm_stage(1, a)
+        eps_stage(1)
+        h_stage(1)
+        for g in range(YG):
+            arm_scale_stage(g)
         for b in range(HB):
             for g in range(YG):
                 gather_arms(b, g)
 
         y_s = held([P, YG, S], U8, "y_s")
         for g in range(YG):
-            banks = [bank(4 * (g % 2) + t) for t in range(PACK)]
+            banks = [bank(4 * (1 - g % 2) + t) for t in range(PACK)]
             for b in range(HB):
                 for t in range(PACK):
                     c0 = g * PASS + t * P

@@ -56,9 +56,8 @@ def tile_list_thompson_arm_rewards_kernel(
             for r in range(4):
                 nc.sync.dma_start(out=dst[r:P:32, :, :].bitcast(I32), in_=rows[r].bitcast(I32))
 
-        def load_arm_scales(b, r):
-            rows = tab2_scales[b].rearrange("(q r) t -> r q t", r=4)
-            nc.sync.dma_start(out=tab2_sc[8 + 4 * b + r : P : 32, :].bitcast(I32), in_=rows[r].bitcast(I32))
+        def load_arm_scales():
+            nc.sync.dma_start(out=tab2_sc[0:P:4, :].bitcast(I32), in_=tab2_scales.rearrange("b q t -> q b t").bitcast(I32))
 
         wm_raw = {}
         tab_w, ws_w, eps_sb, tab2_w = [], [], [], []
@@ -88,25 +87,20 @@ def tile_list_thompson_arm_rewards_kernel(
             nc.sync.dma_start(out=w[:], in_=ws_words[a].bitcast(I32))
             ws_w.append(w)
 
-        def arm_scales(b, rows):
-            for r in rows:
-                load_arm_scales(b, r)
-
         nc.sync.dma_start(out=bs_sb[:], in_=bs.rearrange("(b p t) -> p b t", p=P, t=PACK))
-        load_ws(0)
         nc.sync.dma_start(idx2[:], offs2)
         nc.sync.dma_start(out=pay_sb[:], in_=pay.rearrange("(g p t) -> p g t", p=P, t=PACK))
+        load_ws(0)
         load_ws(1)
         load_ws(2)
         load_wm(0, 0)
         load_scales(tab_scales, tab_sc)
         load_words(tab_words, 0, T, "tab_w0", tab_w, ring, "tab_block")
-        arm_scales(0, range(4))
-        load_words(tab_words, 1, T, "tab_w1", tab_w, ring, "tab_block")
-        arm_scales(1, range(4))
-        load_wm(0, 1)
         load_scales(ws_scales, ws_sc)
+        load_words(tab_words, 1, T, "tab_w1", tab_w, ring, "tab_block")
+        load_wm(0, 1)
         load_words(tab_words, 2, T, "tab_w2", tab_w, ring, "tab_block")
+        load_arm_scales()
         load_wm(0, 2)
         load_eps(0)
         load_words(tab2_words, 0, T2, "tab2_w0", tab2_w, keep, "tab2_block")
@@ -185,8 +179,9 @@ def tile_list_thompson_arm_rewards_kernel(
                 )
 
         def eps_stage(b):
-            for t in range(PACK):
-                nc.vector.tensor_tensor(noise[b][:, t, :], noise[b][:, t, :], eps_sb[b][:, t, :], ALU.mult)
+            for u in range(2):
+                ts = slice(2 * u, 2 * u + 2)
+                nc.vector.tensor_tensor(noise[b][:, ts, :], noise[b][:, ts, :], eps_sb[b][:, ts, :], ALU.mult)
 
         h_q, h_s = {}, {}
 
@@ -198,9 +193,9 @@ def tile_list_thompson_arm_rewards_kernel(
             for jq in range(4):
                 js = slice(jq * P, (jq + 1) * P)
                 nc.vector.tensor_tensor(
-                    hb[:, js, :].rearrange("p (c i) t -> p c t i", i=4),
-                    mean_banks[b][jq][:].rearrange("p (t c i) -> p c t i", t=PACK, i=4),
-                    noise[b][:, :, js].rearrange("p t (c i) -> p c t i", i=4),
+                    hb[:, js, :].rearrange("p (c i) t -> p c t i", i=2),
+                    mean_banks[b][jq][:].rearrange("p (t c i) -> p c t i", t=PACK, i=2),
+                    noise[b][:, :, js].rearrange("p t (c i) -> p c t i", i=2),
                     ALU.add,
                 )
             h_q[b] = held([P, S], U32, "h_q%d" % b)
@@ -234,24 +229,27 @@ def tile_list_thompson_arm_rewards_kernel(
             nc.vector.tensor_copy(vw[:], tab_w[a][:].bitcast(U32).indirect(idx[:]))
             v_w.append(vw)
 
-        def arm_scale_stage(g):
-            cols = slice(g * PASS, (g + 1) * PASS)
-            nc.vector.tensor_copy(v2_sc[:, cols], tab2_sc[:].indirect(idx2[:, g * LIST_COLS : (g + 1) * LIST_COLS]))
+        def arm_scale_stage():
+            nc.vector.tensor_copy(v2_sc[:], tab2_sc[:].indirect(idx2[:]))
             nc.vector.tensor_copy(
-                v2_sc_d[:, cols].rearrange("p (t m) -> p t m", t=PACK),
-                v2_sc[:, cols].rearrange("p (m t) -> p t m", t=PACK),
+                v2_sc_d[:].rearrange("p (g u e m) -> p u g e m", g=YG, u=2, e=2),
+                v2_sc[:].rearrange("p (g m u e) -> p u g e m", g=YG, u=2, e=2),
             )
+            for r in range(1, 4):
+                nc.sync.dma_start(
+                    out=v2_sc_d[r : r + 104 : 4, :].bitcast(I32), in_=v2_sc_d[8 * r : 8 * r + 104 : 4, :].bitcast(I32)
+                )
 
         v2_w = {}
 
-        def gather_arms(b, g):
-            listed = ring.tile([P, PASS], U32, name="listed%d%d" % (b, g), tag="listed", bufs=2, align_bytes=64)
-            nc.vector.tensor_copy(listed[:], tab2_w[b][:].bitcast(U32).indirect(idx2[:, g * LIST_COLS : (g + 1) * LIST_COLS]))
-            w = held([P, PACK, P], U32, "v2_w%d%d" % (b, g))
+        def gather_arms(b, g0, n):
+            w = held([P, n, PACK, P], U32, "v2_w%d%d" % (b, g0))
             nc.vector.tensor_copy(
-                w[:].rearrange("p (u e) m -> p u m e", e=2), listed[:].rearrange("p (m u e) -> p u m e", u=2, e=2)
+                w[:].rearrange("p g t m -> p g m t"),
+                tab2_w[b][:].bitcast(U32).indirect(idx2[:, g0 * LIST_COLS : (g0 + n) * LIST_COLS]),
             )
-            v2_w[(b, g)] = w
+            for g in range(n):
+                v2_w[(b, g0 + g)] = w[:, g, :, :]
 
         def wm_stage(b, a):
             quant_wm(b, a, cast_wm(b, a))
@@ -267,19 +265,18 @@ def tile_list_thompson_arm_rewards_kernel(
         for a in range(KA):
             log_pass(1, a)
         exp_stage(1)
+        arm_scale_stage()
         for a in range(KA):
             wm_stage(0, a)
         eps_stage(0)
         h_stage(0)
+        gather_arms(0, 0, YG)
         for a in range(KA):
             wm_stage(1, a)
         eps_stage(1)
         h_stage(1)
         for g in range(YG):
-            arm_scale_stage(g)
-        for b in range(HB):
-            for g in range(YG):
-                gather_arms(b, g)
+            gather_arms(1, g, 1)
 
         y_s = held([P, YG, S], U8, "y_s")
         for g in range(YG):
@@ -290,7 +287,7 @@ def tile_list_thompson_arm_rewards_kernel(
                     nc.tensor.matmul_mx(
                         out=banks[t][:],
                         lhsT=v2_w[(b, g)][:, t, :].bitcast(FP8X4),
-                        lhsT_scale=v2_sc_d[8 + 4 * b : P, c0 : c0 + P],
+                        lhsT_scale=v2_sc_d[4 * b : P, c0 : c0 + P],
                         rhs=h_q[b][:].bitcast(FP8X4),
                         rhs_scale=h_s[b][:],
                         start=(b == 0),
@@ -304,7 +301,7 @@ def tile_list_thompson_arm_rewards_kernel(
                     nc.sync.dma_start(out=rows[:, t - 1 : t + 1, :], in_=y[:, t - 1 : t + 1, :])
             yb = woven("y_bf%d" % g)
             nc.vector.tensor_copy(
-                yb[:].rearrange("p (c i) t -> p c t i", i=4), y[:].rearrange("p t (c i) -> p c t i", i=4)
+                yb[:].rearrange("p (c i) t -> p c t i", i=2), y[:].rearrange("p t (c i) -> p c t i", i=2)
             )
             y_q = held([P, S], I32, "y_q%d" % g)
             nc.vector.quantize_mx(out=y_q[:].bitcast(FP8X4), scales=y_s[:, g, :], in_=yb[:].rearrange("p j t -> p (j t)"))

@@ -19,10 +19,14 @@ ACT = mybir.ActivationFunctionType
 P = 128
 PACK = 4
 PASS = P * PACK
-KA = K // PASS
-HB = H // PASS
-YG = S2 // PASS
+K_PASSES = K // PASS
+R_PASSES = H // PASS
+I_GROUPS = S2 // PASS
+QUADS = 4
+QUAD_ROWS = 4
+J_PARTS = S // P
 LIST_COLS = PASS // 16
+WM_BLOCK_ON_VECTOR = (0, K_PASSES - 1)
 
 
 def tile_list_thompson_arm_rewards_kernel(
@@ -38,107 +42,150 @@ def tile_list_thompson_arm_rewards_kernel(
         def held(shape, dtype, name):
             return keep.tile(shape, dtype, name=name, align_bytes=64)
 
-        def f32_block(name):
-            return ring.tile([P, PACK, PASS], F32, name=name, tag="f32_block", bufs=6, align_bytes=64)
+        def wm_or_y_block(name):
+            return ring.tile([P, PACK, PASS], F32, name=name, tag="wm_or_y", bufs=R_PASSES * K_PASSES, align_bytes=64)
 
-        idx = keep.tile([P, S // 16], U16, name="idx")
-        idx2 = keep.tile([P, S2 // 16], U16, name="idx2")
-        nc.sync.dma_start(idx[:], offs)
+        def tab_or_noise_block(shape, dtype, name):
+            return ring.tile(shape, dtype, name=name, tag="tab_or_noise", bufs=K_PASSES, align_bytes=64)
 
-        tab_sc = held([P, KA, T], U8, "tab_sc")
-        ws_sc = held([P, KA, H], U8, "ws_sc")
-        tab2_sc = held([P, T2], U8, "tab2_sc")
-        for plane in (tab_sc, ws_sc, tab2_sc):
-            nc.vector.memset(plane[:].bitcast(I32), 0)
-
-        def load_scales(src, dst):
-            rows = src.rearrange("a (q r) t -> r q a t", r=4)
-            for r in range(4):
-                nc.sync.dma_start(out=dst[r:P:32, :, :].bitcast(I32), in_=rows[r].bitcast(I32))
-
-        def load_arm_scales():
-            nc.sync.dma_start(out=tab2_sc[0:P:4, :].bitcast(I32), in_=tab2_scales.rearrange("b q t -> q b t").bitcast(I32))
-
-        wm_raw = {}
-        tab_w, ws_w, eps_sb, tab2_w = [], [], [], []
-
-        def load_wm(b, a):
-            raw = f32_block("wm_raw%d%d" % (b, a))
-            nc.sync.dma_start(
-                out=raw[:],
-                in_=wm[a * PASS : (a + 1) * PASS, b * PASS : (b + 1) * PASS].rearrange("(p j) c -> p j c", j=PACK),
-            )
-            wm_raw[(b, a)] = raw
-
-        def load_words(src, a, width, name, into, pool, tag):
-            w = pool.tile([P, width], I32, name=name, tag=tag, bufs=src.shape[0], align_bytes=64)
-            nc.sync.dma_start(out=w[:], in_=src[a].rearrange("p n t -> p (n t)").bitcast(I32))
-            into.append(w)
-
-        def load_eps(b):
-            e = held([P, PACK, S], F32, "eps%d" % b)
-            nc.sync.dma_start(out=e[:], in_=eps[b * PASS : (b + 1) * PASS, :].rearrange("(p t) j -> p t j", t=PACK))
-            eps_sb.append(e)
-
-        bs_sb = held([P, HB, PACK], F32, "bs_sb")
-        pay_sb = held([P, YG, PACK], F32, "pay_sb")
-        def load_ws(a):
-            w = held([P, H // 2], I32, "ws_w%d" % a)
-            nc.sync.dma_start(out=w[:], in_=ws_words[a].bitcast(I32))
-            ws_w.append(w)
-
-        nc.sync.dma_start(out=bs_sb[:], in_=bs.rearrange("(b p t) -> p b t", p=P, t=PACK))
-        nc.sync.dma_start(idx2[:], offs2)
-        nc.sync.dma_start(out=pay_sb[:], in_=pay.rearrange("(g p t) -> p g t", p=P, t=PACK))
-        load_ws(0)
-        load_ws(1)
-        load_ws(2)
-        load_wm(0, 0)
-        load_scales(tab_scales, tab_sc)
-        load_words(tab_words, 0, T, "tab_w0", tab_w, ring, "tab_block")
-        load_scales(ws_scales, ws_sc)
-        load_words(tab_words, 1, T, "tab_w1", tab_w, ring, "tab_block")
-        load_wm(0, 1)
-        load_words(tab_words, 2, T, "tab_w2", tab_w, ring, "tab_block")
-        load_arm_scales()
-        load_wm(0, 2)
-        load_eps(0)
-        load_words(tab2_words, 0, T2, "tab2_w0", tab2_w, keep, "tab2_block")
-        load_wm(1, 0)
-        load_wm(1, 1)
-        load_wm(1, 2)
-        load_eps(1)
-        load_words(tab2_words, 1, T2, "tab2_w1", tab2_w, keep, "tab2_block")
-
-        v_sc, ws_sc_d = [], []
-
-        wm_q, wm_s = {}, {}
-
-        def cast_wm(b, a):
-            g = ring.tile([P, PACK, P, PACK], BF16, name="wm_bf%d%d" % (b, a), tag="wm_bf", bufs=3, align_bytes=64)
-            nc.scalar.copy(
-                out=g[:].rearrange("p (u e) m j -> p u m j e", e=2),
-                in_=wm_raw[(b, a)][:].rearrange("p j (m u e) -> p u m j e", u=2, e=2),
-            )
-            return g
-
-        def quant_wm(b, a, g):
-            wm_q[(b, a)] = held([P, PASS], U32, "wm_q%d%d" % (b, a))
-            wm_s[(b, a)] = held([P, PASS], U8, "wm_s%d%d" % (b, a))
-            nc.vector.quantize_mx(
-                out=wm_q[(b, a)][:].bitcast(FP8X4), scales=wm_s[(b, a)][:], in_=g[:].rearrange("p t m j -> p (t m j)")
-            )
+        def woven(name):
+            return ring.tile([P, S, PACK], BF16, name=name, tag="woven", bufs=2, align_bytes=64)
 
         def bank(n):
             return psum.tile([P, PASS], F32, name="bank%d" % n, tag="bank%d" % n)
 
-        v_w, ws_d = [], []
-        mean_banks = {}
+        idx = keep.tile([P, S // 16], U16, name="idx")
+        idx2 = keep.tile([P, S2 // 16], U16, name="idx2")
+        bs_sb = held([P, R_PASSES, PACK], F32, "bs_sb")
+        pay_sb = held([P, I_GROUPS, PACK], F32, "pay_sb")
+
+        tab_sc = held([P, K_PASSES, T], U8, "tab_sc")
+        ws_sc = held([P, K_PASSES, H], U8, "ws_sc")
+        tab2_sc = held([P, T2], U8, "tab2_sc")
+        for plane in (tab_sc, ws_sc, tab2_sc):
+            nc.vector.memset(plane[:].bitcast(I32), 0)
+
+        ws_w, tab_w, tab2_w, eps_sb, wm_raw = [], [], [], [], {}
+
+        def load_ws(a):
+            words = held([P, H // 2], I32, "ws_w%d" % a)
+            nc.sync.dma_start(out=words[:], in_=ws_words[a].bitcast(I32))
+            ws_w.append(words)
+
+        def load_scales(src, dst):
+            rows = src.rearrange("a (q r) t -> r q a t", r=QUAD_ROWS)
+            for r in range(QUAD_ROWS):
+                nc.sync.dma_start(out=dst[r:P:32, :, :].bitcast(I32), in_=rows[r].bitcast(I32))
+
+        def load_tab(a):
+            words = tab_or_noise_block([P, T], I32, "tab_w%d" % a)
+            nc.sync.dma_start(out=words[:], in_=tab_words[a].rearrange("p n t -> p (n t)").bitcast(I32))
+            tab_w.append(words)
+
+        def load_tab2(b):
+            words = held([P, T2], I32, "tab2_w%d" % b)
+            nc.sync.dma_start(out=words[:], in_=tab2_words[b].rearrange("p n t -> p (n t)").bitcast(I32))
+            tab2_w.append(words)
+
+        def load_tab2_scales():
+            nc.sync.dma_start(out=tab2_sc[0:P:4, :].bitcast(I32), in_=tab2_scales.rearrange("b q t -> q b t").bitcast(I32))
+
+        def load_wm(b, a):
+            raw = wm_or_y_block("wm_raw%d%d" % (b, a))
+            block = wm[a * PASS : (a + 1) * PASS, b * PASS : (b + 1) * PASS]
+            nc.sync.dma_start(out=raw[:], in_=block.rearrange("(p j) c -> p j c", j=PACK))
+            wm_raw[(b, a)] = raw
+
+        def load_eps(b):
+            rows = held([P, PACK, S], F32, "eps%d" % b)
+            nc.sync.dma_start(out=rows[:], in_=eps[b * PASS : (b + 1) * PASS, :].rearrange("(p t) j -> p t j", t=PACK))
+            eps_sb.append(rows)
+
+        load_ws(0)
+        nc.sync.dma_start(idx[:], offs)
+        load_ws(1)
+        nc.sync.dma_start(out=bs_sb[:], in_=bs.rearrange("(b p t) -> p b t", p=P, t=PACK))
+        load_ws(2)
+        nc.sync.dma_start(idx2[:], offs2)
+        nc.sync.dma_start(out=pay_sb[:], in_=pay.rearrange("(g p t) -> p g t", p=P, t=PACK))
+        load_scales(tab_scales, tab_sc)
+        load_tab(0)
+        load_scales(ws_scales, ws_sc)
+        load_tab(1)
+        load_wm(0, 0)
+        load_tab(2)
+        load_tab2_scales()
+        load_wm(0, 1)
+        load_wm(0, 2)
+        load_eps(0)
+        for a in range(K_PASSES):
+            load_wm(1, a)
+        load_eps(1)
+        for b in range(R_PASSES):
+            load_tab2(b)
+
+        ws_dealt, ws_sc_dealt, v_w, v_sc = [], [], [], []
+
+        def deal_ws(a):
+            dealt = held([P, 2 * H], U8, "ws_dealt%d" % a)
+            nc.vector.tensor_copy(
+                dealt[:].bitcast(U16).rearrange("p (b t m) -> p b t m", b=R_PASSES, t=PACK),
+                ws_w[a][:].bitcast(U16).rearrange("p (b m t) -> p b t m", b=R_PASSES, t=PACK),
+            )
+            ws_dealt.append(dealt)
+
+        def deal_ws_scales(a):
+            dealt = held([P, H], U8, "ws_sc_dealt%d" % a)
+            nc.vector.tensor_copy(
+                dealt[:].rearrange("p (b t m) -> p b t m", b=R_PASSES, t=PACK),
+                ws_sc[:, a, :].rearrange("p (b m t) -> p b t m", b=R_PASSES, t=PACK),
+            )
+            ws_sc_dealt.append(dealt)
+
+        def gather_visitors(a):
+            scales = held([P, S], U8, "v_sc%d" % a)
+            nc.vector.tensor_copy(scales[:], tab_sc[:, a, :].indirect(idx[:]))
+            v_sc.append(scales)
+            words = held([P, S], U32, "v_w%d" % a)
+            nc.vector.tensor_copy(words[:], tab_w[a][:].bitcast(U32).indirect(idx[:]))
+            v_w.append(words)
+
+        wm_q, wm_s = {}, {}
+
+        def quantise_wm(b, a):
+            rounded = ring.tile([P, PACK, P, PACK], BF16, name="wm_bf%d%d" % (b, a), tag="wm_bf", bufs=3, align_bytes=64)
+            copy = nc.vector.tensor_copy if (b, a) == WM_BLOCK_ON_VECTOR else nc.scalar.copy
+            copy(
+                out=rounded[:].rearrange("p (u e) m j -> p u m j e", e=2),
+                in_=wm_raw[(b, a)][:].rearrange("p j (m u e) -> p u m j e", u=2, e=2),
+            )
+            wm_q[(b, a)] = held([P, PASS], U32, "wm_q%d%d" % (b, a))
+            wm_s[(b, a)] = held([P, PASS], U8, "wm_s%d%d" % (b, a))
+            nc.vector.quantize_mx(
+                out=wm_q[(b, a)][:].bitcast(FP8X4), scales=wm_s[(b, a)][:], in_=rounded[:].rearrange("p t m j -> p (t m j)")
+            )
+
+        log_banks, mean_banks, noise = {}, {}, {}
+
+        def log_pass(b, a):
+            if a == 0:
+                log_banks[b] = [bank(t) for t in range(PACK)]
+            for t in range(PACK):
+                c0 = b * PASS + t * P
+                nc.tensor.matmul_mx(
+                    out=log_banks[b][t][:],
+                    lhsT=ws_dealt[a][:, 2 * c0 : 2 * (c0 + P)].bitcast(FP4X4),
+                    lhsT_scale=ws_sc_dealt[a][:, c0 : c0 + P],
+                    rhs=v_w[a][:].bitcast(FP8X4),
+                    rhs_scale=v_sc[a][:],
+                    start=(a == 0),
+                    stop=(a == K_PASSES - 1),
+                )
 
         def mean_pass(b, a):
             if a == 0:
-                mean_banks[b] = [bank(4 * (1 - b) + jq) for jq in range(4)]
-            for jq in range(4):
+                mean_banks[b] = [bank(4 * (1 - b) + jq) for jq in range(J_PARTS)]
+            for jq in range(J_PARTS):
                 js = slice(jq * P, (jq + 1) * P)
                 for t in range(PACK):
                     ms = slice(t * P, (t + 1) * P)
@@ -149,165 +196,105 @@ def tile_list_thompson_arm_rewards_kernel(
                         rhs=v_w[a][:, js].bitcast(FP8X4),
                         rhs_scale=v_sc[a][:, js],
                         start=(a == 0 and t == 0),
-                        stop=(a == KA - 1 and t == PACK - 1),
+                        stop=(a == K_PASSES - 1 and t == PACK - 1),
                     )
 
-        log_banks = {}
-
-        def log_pass(b, a):
-            if a == 0:
-                log_banks[b] = [bank(t) for t in range(PACK)]
-            for t in range(PACK):
-                c0 = b * PASS + t * P
-                nc.tensor.matmul_mx(
-                    out=log_banks[b][t][:],
-                    lhsT=ws_d[a][:, 2 * c0 : 2 * (c0 + P)].bitcast(FP4X4),
-                    lhsT_scale=ws_sc_d[a][:, c0 : c0 + P],
-                    rhs=v_w[a][:].bitcast(FP8X4),
-                    rhs_scale=v_sc[a][:],
-                    start=(a == 0),
-                    stop=(a == KA - 1),
-                )
-
-        noise = {}
-
         def exp_stage(b):
-            noise[b] = ring.tile([P, PACK, S], F32, name="noise%d" % b, tag="tab_block", bufs=KA, align_bytes=64)
+            noise[b] = tab_or_noise_block([P, PACK, S], F32, "noise%d" % b)
             for t in range(PACK):
-                nc.scalar.activation(
-                    out=noise[b][:, t, :], in_=log_banks[b][t][:], func=ACT.Exp, bias=bs_sb[:, b, t : t + 1]
-                )
-
-        def eps_stage(b):
-            for u in range(2):
-                ts = slice(2 * u, 2 * u + 2)
-                nc.vector.tensor_tensor(noise[b][:, ts, :], noise[b][:, ts, :], eps_sb[b][:, ts, :], ALU.mult)
+                nc.scalar.activation(out=noise[b][:, t, :], in_=log_banks[b][t][:], func=ACT.Exp, bias=bs_sb[:, b, t : t + 1])
 
         h_q, h_s = {}, {}
 
-        def woven(name):
-            return ring.tile([P, S, PACK], BF16, name=name, tag="woven", bufs=2, align_bytes=64)
-
         def h_stage(b):
-            hb = woven("h_bf%d" % b)
-            for jq in range(4):
+            for u in range(2):
+                ts = slice(2 * u, 2 * u + 2)
+                nc.vector.tensor_tensor(noise[b][:, ts, :], noise[b][:, ts, :], eps_sb[b][:, ts, :], ALU.mult)
+            h_bf = woven("h_bf%d" % b)
+            for jq in range(J_PARTS):
                 js = slice(jq * P, (jq + 1) * P)
                 nc.vector.tensor_tensor(
-                    hb[:, js, :].rearrange("p (c i) t -> p c t i", i=2),
+                    h_bf[:, js, :].rearrange("p (c i) t -> p c t i", i=2),
                     mean_banks[b][jq][:].rearrange("p (t c i) -> p c t i", t=PACK, i=2),
                     noise[b][:, :, js].rearrange("p t (c i) -> p c t i", i=2),
                     ALU.add,
                 )
             h_q[b] = held([P, S], U32, "h_q%d" % b)
             h_s[b] = held([P, S], U8, "h_s%d" % b)
-            nc.vector.quantize_mx(out=h_q[b][:].bitcast(FP8X4), scales=h_s[b][:], in_=hb[:].rearrange("p j t -> p (j t)"))
+            nc.vector.quantize_mx(out=h_q[b][:].bitcast(FP8X4), scales=h_s[b][:], in_=h_bf[:].rearrange("p j t -> p (j t)"))
 
         v2_sc = held([P, S2], U8, "v2_sc")
-        v2_sc_d = held([P, S2], U8, "v2_sc_d")
+        v2_sc_dealt = held([P, S2], U8, "v2_sc_dealt")
 
-        def deal_ws(a):
-            wd = held([P, 2 * H], U8, "ws_d%d" % a)
-            nc.vector.tensor_copy(
-                wd[:].bitcast(U16).rearrange("p (b t m) -> p b t m", b=HB, t=PACK),
-                ws_w[a][:].bitcast(U16).rearrange("p (b m t) -> p b t m", b=HB, t=PACK),
-            )
-            ws_d.append(wd)
-
-        def deal_ws_scales(a):
-            sd = held([P, H], U8, "ws_sc_d%d" % a)
-            nc.vector.tensor_copy(
-                sd[:].rearrange("p (b t m) -> p b t m", b=HB, t=PACK),
-                ws_sc[:, a, :].rearrange("p (b m t) -> p b t m", b=HB, t=PACK),
-            )
-            ws_sc_d.append(sd)
-
-        def gather_visitors(a):
-            vs = held([P, S], U8, "v_sc%d" % a)
-            nc.vector.tensor_copy(vs[:], tab_sc[:, a, :].indirect(idx[:]))
-            v_sc.append(vs)
-            vw = held([P, S], U32, "v_w%d" % a)
-            nc.vector.tensor_copy(vw[:], tab_w[a][:].bitcast(U32).indirect(idx[:]))
-            v_w.append(vw)
-
-        def arm_scale_stage():
+        def gather_arm_scales():
             nc.vector.tensor_copy(v2_sc[:], tab2_sc[:].indirect(idx2[:]))
             nc.vector.tensor_copy(
-                v2_sc_d[:].rearrange("p (g u e m) -> p u g e m", g=YG, u=2, e=2),
-                v2_sc[:].rearrange("p (g m u e) -> p u g e m", g=YG, u=2, e=2),
+                v2_sc_dealt[:].rearrange("p (g u e m) -> p u g e m", g=I_GROUPS, u=2, e=2),
+                v2_sc[:].rearrange("p (g m u e) -> p u g e m", g=I_GROUPS, u=2, e=2),
             )
-            for r in range(1, 4):
-                nc.sync.dma_start(
-                    out=v2_sc_d[r : r + 104 : 4, :].bitcast(I32), in_=v2_sc_d[8 * r : 8 * r + 104 : 4, :].bitcast(I32)
+            span = 32 * (QUADS - 1) + 4 * R_PASSES
+            for r in range(1, QUAD_ROWS):
+                nc.gpsimd.dma_start(
+                    out=v2_sc_dealt[r : r + span : 4, :].bitcast(I32),
+                    in_=v2_sc_dealt[8 * r : 8 * r + span : 4, :].bitcast(I32),
                 )
 
-        v2_w = {}
-
-        def gather_arms(b, g0, n):
-            w = held([P, n, PACK, P], U32, "v2_w%d%d" % (b, g0))
-            nc.vector.tensor_copy(
-                w[:].rearrange("p g t m -> p g m t"),
-                tab2_w[b][:].bitcast(U32).indirect(idx2[:, g0 * LIST_COLS : (g0 + n) * LIST_COLS]),
-            )
-            for g in range(n):
-                v2_w[(b, g0 + g)] = w[:, g, :, :]
-
-        def wm_stage(b, a):
-            quant_wm(b, a, cast_wm(b, a))
-            mean_pass(b, a)
-
-        for a in range(KA):
+        for a in range(K_PASSES):
             deal_ws(a)
-        for a in range(KA):
+        for a in range(K_PASSES):
             gather_visitors(a)
             deal_ws_scales(a)
             log_pass(0, a)
         exp_stage(0)
-        for a in range(KA):
+        for a in range(K_PASSES):
             log_pass(1, a)
         exp_stage(1)
-        arm_scale_stage()
-        for a in range(KA):
-            wm_stage(0, a)
-        eps_stage(0)
-        h_stage(0)
-        gather_arms(0, 0, YG)
-        for a in range(KA):
-            wm_stage(1, a)
-        eps_stage(1)
-        h_stage(1)
-        for g in range(YG):
-            gather_arms(1, g, 1)
+        gather_arm_scales()
+        for b in range(R_PASSES):
+            for a in range(K_PASSES):
+                quantise_wm(b, a)
+                mean_pass(b, a)
+            h_stage(b)
 
-        y_s = held([P, YG, S], U8, "y_s")
-        for g in range(YG):
-            banks = [bank(4 * (1 - g % 2) + t) for t in range(PACK)]
-            for b in range(HB):
+        def gather_arms(b, g):
+            first_store_slot = (b, g) in ((R_PASSES - 1, 0), (0, I_GROUPS - 1))
+            tag = "v2_w_first_store" if first_store_slot else "v2_w%d%d" % (b, g)
+            words = ring.tile([P, PACK, P], U32, name="v2_w%d%d" % (b, g), tag=tag, bufs=1, align_bytes=64)
+            nc.vector.tensor_copy(
+                words[:].rearrange("p t m -> p m t"),
+                tab2_w[b][:].bitcast(U32).indirect(idx2[:, g * LIST_COLS : (g + 1) * LIST_COLS]),
+            )
+            return words
+
+        y_s = held([P, I_GROUPS, S], U8, "y_s")
+        for g in range(I_GROUPS):
+            y_banks = [bank(4 * (1 - g % 2) + t) for t in range(PACK)]
+            v2_w = [gather_arms(b, g) for b in range(R_PASSES)]
+            for b in range(R_PASSES):
                 for t in range(PACK):
                     c0 = g * PASS + t * P
                     nc.tensor.matmul_mx(
-                        out=banks[t][:],
-                        lhsT=v2_w[(b, g)][:, t, :].bitcast(FP8X4),
-                        lhsT_scale=v2_sc_d[4 * b : P, c0 : c0 + P],
+                        out=y_banks[t][:],
+                        lhsT=v2_w[b][:, t, :].bitcast(FP8X4),
+                        lhsT_scale=v2_sc_dealt[4 * b : P, c0 : c0 + P],
                         rhs=h_q[b][:].bitcast(FP8X4),
                         rhs_scale=h_s[b][:],
                         start=(b == 0),
-                        stop=(b == HB - 1),
+                        stop=(b == R_PASSES - 1),
                     )
-            y = f32_block("y%d" % g)
-            rows = out_0[g * PASS : (g + 1) * PASS, :].rearrange("(p t) j -> p t j", t=PACK)
+            y = wm_or_y_block("y%d" % g)
+            y_rows = out_0[g * PASS : (g + 1) * PASS, :].rearrange("(p t) j -> p t j", t=PACK)
             for t in range(PACK):
-                nc.scalar.activation(out=y[:, t, :], in_=banks[t][:], func=ACT.Copy, scale=pay_sb[:, g, t : t + 1])
+                nc.scalar.activation(out=y[:, t, :], in_=y_banks[t][:], func=ACT.Copy, scale=pay_sb[:, g, t : t + 1])
                 if t % 2 == 1:
-                    nc.sync.dma_start(out=rows[:, t - 1 : t + 1, :], in_=y[:, t - 1 : t + 1, :])
-            yb = woven("y_bf%d" % g)
+                    nc.sync.dma_start(out=y_rows[:, t - 1 : t + 1, :], in_=y[:, t - 1 : t + 1, :])
+            y_bf = woven("y_bf%d" % g)
             nc.vector.tensor_copy(
-                yb[:].rearrange("p (c i) t -> p c t i", i=2), y[:].rearrange("p t (c i) -> p c t i", i=2)
+                y_bf[:].rearrange("p (c i) t -> p c t i", i=2), y[:].rearrange("p t (c i) -> p c t i", i=2)
             )
             y_q = held([P, S], I32, "y_q%d" % g)
-            nc.vector.quantize_mx(out=y_q[:].bitcast(FP8X4), scales=y_s[:, g, :], in_=yb[:].rearrange("p j t -> p (j t)"))
+            nc.vector.quantize_mx(out=y_q[:].bitcast(FP8X4), scales=y_s[:, g, :], in_=y_bf[:].rearrange("p j t -> p (j t)"))
             nc.sync.dma_start(out=out_1[g].rearrange("p m t -> p (m t)").bitcast(I32), in_=y_q[:])
-        for q in range(4):
-            nc.sync.dma_start(
-                out=out_2[:, 4 * q : 4 * q + 4, :].rearrange("g r m -> r g m").bitcast(I32),
-                in_=y_s[32 * q : 32 * q + 4, :, :].bitcast(I32),
-            )
+        y_scale_rows = out_2.rearrange("g (q r) m -> r q g m", r=QUAD_ROWS)
+        for r in range(QUAD_ROWS):
+            nc.sync.dma_start(out=y_scale_rows[r].bitcast(I32), in_=y_s[r:P:32, :, :].bitcast(I32))

@@ -1,6 +1,7 @@
 from contextlib import ExitStack
 
 import concourse.mybir as mybir
+from concourse.masks import make_identity
 
 K, H, T, S, T2, S2 = 1536, 1024, 2048, 512, 4096, 1536
 FLOPS = 2 * (2 * K * H * S + H * S2 * S)
@@ -26,7 +27,9 @@ QUADS = 4
 QUAD_ROWS = 4
 J_PARTS = S // P
 LIST_COLS = PASS // 16
-WM_BLOCK_ON_VECTOR = (0, K_PASSES - 1)
+WM_HALF = 6
+VEC_ROWS = R_PASSES + I_GROUPS
+MOVE_ROWS = 112
 
 
 def tile_list_thompson_arm_rewards_kernel(
@@ -43,7 +46,7 @@ def tile_list_thompson_arm_rewards_kernel(
             return keep.tile(shape, dtype, name=name, align_bytes=64)
 
         def wm_or_y_block(name):
-            return ring.tile([P, PACK, PASS], F32, name=name, tag="wm_or_y", bufs=R_PASSES * K_PASSES, align_bytes=64)
+            return ring.tile([P, PACK, PASS], F32, name=name, tag="wm_or_y", bufs=WM_HALF, align_bytes=64)
 
         def tab_or_noise_block(shape, dtype, name):
             return ring.tile(shape, dtype, name=name, tag="tab_or_noise", bufs=K_PASSES, align_bytes=64)
@@ -56,26 +59,44 @@ def tile_list_thompson_arm_rewards_kernel(
 
         idx = keep.tile([P, S // 16], U16, name="idx")
         idx2 = keep.tile([P, S2 // 16], U16, name="idx2")
-        bs_sb = held([P, R_PASSES, PACK], F32, "bs_sb")
-        pay_sb = held([P, I_GROUPS, PACK], F32, "pay_sb")
+        vec_rows = held([P, PASS], F32, "vec_rows")
+        ident = held([P, P], F32, "ident")
+        vec_cols = held([P, PACK, VEC_ROWS], F32, "vec_cols")
+        nc.gpsimd.memset(vec_rows[:], 0.0)
+        make_identity(nc, ident[:])
 
-        tab_sc = held([P, K_PASSES, T], U8, "tab_sc")
+        def load_vectors():
+            nc.sync.dma_start(out=vec_rows[0:R_PASSES, :], in_=bs.rearrange("(b c) -> b c", c=PASS))
+            nc.sync.dma_start(out=vec_rows[R_PASSES:VEC_ROWS, :], in_=pay.rearrange("(g c) -> g c", c=PASS))
+
+        def turn_vectors():
+            turned = bank(7)
+            for t in range(PACK):
+                nc.tensor.transpose(turned[:, t * P : (t + 1) * P], vec_rows[:, t:PASS:PACK], ident[:])
+            nc.scalar.copy(out=vec_cols[:], in_=turned[:].rearrange("p (t c) -> p t c", t=PACK)[:, :, 0:VEC_ROWS])
+
+        tab_sc = held([P, T], U8, "tab_sc")
         ws_sc = held([P, K_PASSES, H], U8, "ws_sc")
         tab2_sc = held([P, T2], U8, "tab2_sc")
-        for plane in (tab_sc, ws_sc, tab2_sc):
+        v_sc = [held([P, S], U8, "v_sc%d" % a) for a in range(K_PASSES)]
+        ws_sc_dealt = held([P, K_PASSES, H], U8, "ws_sc_dealt")
+        for plane in [tab_sc, ws_sc, tab2_sc] + v_sc[1:]:
             nc.vector.memset(plane[:].bitcast(I32), 0)
 
-        ws_w, tab_w, tab2_w, eps_sb, wm_raw = [], [], [], [], {}
-
-        def load_ws(a):
-            words = held([P, H // 2], I32, "ws_w%d" % a)
-            nc.sync.dma_start(out=words[:], in_=ws_words[a].bitcast(I32))
-            ws_w.append(words)
+        tab_w, tab2_w, eps_sb, wm_raw = [], [], {}, {}
+        ws_w = held([P, K_PASSES, H // 2], I32, "ws_w")
 
         def load_scales(src, dst):
-            rows = src.rearrange("a (q r) t -> r q a t", r=QUAD_ROWS)
+            for q in range(QUADS):
+                nc.sync.dma_start(
+                    out=dst[32 * q : 32 * q + QUAD_ROWS * K_PASSES, :].bitcast(I32),
+                    in_=src[:, QUAD_ROWS * q : QUAD_ROWS * (q + 1), :].bitcast(I32),
+                )
+
+        def load_ws_scales():
+            rows = ws_scales.rearrange("a (q r) t -> r q a t", r=QUAD_ROWS)
             for r in range(QUAD_ROWS):
-                nc.sync.dma_start(out=dst[r:P:32, :, :].bitcast(I32), in_=rows[r].bitcast(I32))
+                nc.sync.dma_start(out=ws_sc[r:P:32, :, :].bitcast(I32), in_=rows[r].bitcast(I32))
 
         def load_tab(a):
             words = tab_or_noise_block([P, T], I32, "tab_w%d" % a)
@@ -94,71 +115,56 @@ def tile_list_thompson_arm_rewards_kernel(
             raw = wm_or_y_block("wm_raw%d%d" % (b, a))
             block = wm[a * PASS : (a + 1) * PASS, b * PASS : (b + 1) * PASS]
             nc.sync.dma_start(out=raw[:], in_=block.rearrange("(p j) c -> p j c", j=PACK))
-            wm_raw[(b, a)] = raw
+            wm_raw[(b, a)] = raw[:]
 
         def load_eps(b):
             rows = held([P, PACK, S], F32, "eps%d" % b)
             nc.sync.dma_start(out=rows[:], in_=eps[b * PASS : (b + 1) * PASS, :].rearrange("(p t) j -> p t j", t=PACK))
-            eps_sb.append(rows)
+            eps_sb[b] = rows
 
-        load_ws(0)
-        nc.sync.dma_start(idx[:], offs)
-        load_ws(1)
-        nc.sync.dma_start(out=bs_sb[:], in_=bs.rearrange("(b p t) -> p b t", p=P, t=PACK))
-        load_ws(2)
-        nc.sync.dma_start(idx2[:], offs2)
-        nc.sync.dma_start(out=pay_sb[:], in_=pay.rearrange("(g p t) -> p g t", p=P, t=PACK))
-        load_scales(tab_scales, tab_sc)
-        load_tab(0)
-        load_scales(ws_scales, ws_sc)
-        load_tab(1)
-        load_wm(0, 0)
-        load_tab(2)
-        load_tab2_scales()
-        load_wm(0, 1)
-        load_wm(0, 2)
-        load_eps(0)
-        for a in range(K_PASSES):
-            load_wm(1, a)
-        load_eps(1)
-        for b in range(R_PASSES):
-            load_tab2(b)
+        def move_planes(planes):
+            for a in range(1, K_PASSES):
+                nc.sync.dma_start(
+                    out=planes[a][0:MOVE_ROWS, :].bitcast(I32),
+                    in_=planes[0][QUAD_ROWS * a : QUAD_ROWS * a + MOVE_ROWS, :].bitcast(I32),
+                )
 
-        ws_dealt, ws_sc_dealt, v_w, v_sc = [], [], [], []
+        ws_dealt = held([P, K_PASSES, 2 * H], U8, "ws_dealt")
+        v_w = []
 
         def deal_ws(a):
-            dealt = held([P, 2 * H], U8, "ws_dealt%d" % a)
             nc.vector.tensor_copy(
-                dealt[:].bitcast(U16).rearrange("p (b t m) -> p b t m", b=R_PASSES, t=PACK),
-                ws_w[a][:].bitcast(U16).rearrange("p (b m t) -> p b t m", b=R_PASSES, t=PACK),
+                ws_dealt[:, a, :].bitcast(U16).rearrange("p (b t m) -> p b t m", b=R_PASSES, t=PACK),
+                ws_w[:, a, :].bitcast(U16).rearrange("p (b m t) -> p b t m", b=R_PASSES, t=PACK),
             )
-            ws_dealt.append(dealt)
 
         def deal_ws_scales(a):
-            dealt = held([P, H], U8, "ws_sc_dealt%d" % a)
             nc.vector.tensor_copy(
-                dealt[:].rearrange("p (b t m) -> p b t m", b=R_PASSES, t=PACK),
+                ws_sc_dealt[:, a, :].rearrange("p (b t m) -> p b t m", b=R_PASSES, t=PACK),
                 ws_sc[:, a, :].rearrange("p (b m t) -> p b t m", b=R_PASSES, t=PACK),
             )
-            ws_sc_dealt.append(dealt)
+
+        def deal_ws_pass(a):
+            deal_ws(a)
+            deal_ws_scales(a)
 
         def gather_visitors(a):
-            scales = held([P, S], U8, "v_sc%d" % a)
-            nc.vector.tensor_copy(scales[:], tab_sc[:, a, :].indirect(idx[:]))
-            v_sc.append(scales)
             words = held([P, S], U32, "v_w%d" % a)
             nc.vector.tensor_copy(words[:], tab_w[a][:].bitcast(U32).indirect(idx[:]))
             v_w.append(words)
 
         wm_q, wm_s = {}, {}
 
-        def quantise_wm(b, a):
-            rounded = ring.tile([P, PACK, P, PACK], BF16, name="wm_bf%d%d" % (b, a), tag="wm_bf", bufs=3, align_bytes=64)
-            copy = nc.vector.tensor_copy if (b, a) == WM_BLOCK_ON_VECTOR else nc.scalar.copy
-            copy(
-                out=rounded[:].rearrange("p (u e) m j -> p u m j e", e=2),
-                in_=wm_raw[(b, a)][:].rearrange("p j (m u e) -> p u m j e", u=2, e=2),
-            )
+        def quantise_wm(b, a, on_scalar):
+            rounded = ring.tile([P, PACK, P, PACK], BF16, name="wm_bf%d%d" % (b, a), tag="wm_bf", bufs=4, align_bytes=64)
+            dst = rounded[:].rearrange("p (u e) m j -> p u m j e", e=2)
+            src = wm_raw[(b, a)].rearrange("p j (m u e) -> p u m j e", u=2, e=2)
+            cut = on_scalar // 64
+            for copy, us in ((nc.scalar.copy, slice(0, cut)), (nc.vector.tensor_copy, slice(cut, 2))):
+                if us.stop - us.start == 2:
+                    copy(out=dst, in_=src)
+                elif us.stop - us.start == 1:
+                    copy(out=dst[:, us.start], in_=src[:, us.start])
             wm_q[(b, a)] = held([P, PASS], U32, "wm_q%d%d" % (b, a))
             wm_s[(b, a)] = held([P, PASS], U8, "wm_s%d%d" % (b, a))
             nc.vector.quantize_mx(
@@ -174,8 +180,8 @@ def tile_list_thompson_arm_rewards_kernel(
                 c0 = b * PASS + t * P
                 nc.tensor.matmul_mx(
                     out=log_banks[b][t][:],
-                    lhsT=ws_dealt[a][:, 2 * c0 : 2 * (c0 + P)].bitcast(FP4X4),
-                    lhsT_scale=ws_sc_dealt[a][:, c0 : c0 + P],
+                    lhsT=ws_dealt[:, a, 2 * c0 : 2 * (c0 + P)].bitcast(FP4X4),
+                    lhsT_scale=ws_sc_dealt[:, a, c0 : c0 + P],
                     rhs=v_w[a][:].bitcast(FP8X4),
                     rhs_scale=v_sc[a][:],
                     start=(a == 0),
@@ -202,14 +208,16 @@ def tile_list_thompson_arm_rewards_kernel(
         def exp_stage(b):
             noise[b] = tab_or_noise_block([P, PACK, S], F32, "noise%d" % b)
             for t in range(PACK):
-                nc.scalar.activation(out=noise[b][:, t, :], in_=log_banks[b][t][:], func=ACT.Exp, bias=bs_sb[:, b, t : t + 1])
+                nc.scalar.activation(out=noise[b][:, t, :], in_=log_banks[b][t][:], func=ACT.Exp, bias=vec_cols[:, t, b : b + 1])
 
         h_q, h_s = {}, {}
 
-        def h_stage(b):
+        def noise_stage(b):
             for u in range(2):
                 ts = slice(2 * u, 2 * u + 2)
                 nc.vector.tensor_tensor(noise[b][:, ts, :], noise[b][:, ts, :], eps_sb[b][:, ts, :], ALU.mult)
+
+        def h_stage(b):
             h_bf = woven("h_bf%d" % b)
             for jq in range(J_PARTS):
                 js = slice(jq * P, (jq + 1) * P)
@@ -227,35 +235,78 @@ def tile_list_thompson_arm_rewards_kernel(
         v2_sc_dealt = held([P, S2], U8, "v2_sc_dealt")
 
         def gather_arm_scales():
-            nc.vector.tensor_copy(v2_sc[:], tab2_sc[:].indirect(idx2[:]))
+            for g in range(I_GROUPS):
+                nc.vector.tensor_copy(
+                    v2_sc[:, g * PASS : (g + 1) * PASS], tab2_sc[:].indirect(idx2[:, g * LIST_COLS : (g + 1) * LIST_COLS])
+                )
             nc.vector.tensor_copy(
                 v2_sc_dealt[:].rearrange("p (g u e m) -> p u g e m", g=I_GROUPS, u=2, e=2),
                 v2_sc[:].rearrange("p (g m u e) -> p u g e m", g=I_GROUPS, u=2, e=2),
             )
+
+        def move_arm_scales():
             span = 32 * (QUADS - 1) + 4 * R_PASSES
             for r in range(1, QUAD_ROWS):
-                nc.gpsimd.dma_start(
+                nc.sync.dma_start(
                     out=v2_sc_dealt[r : r + span : 4, :].bitcast(I32),
                     in_=v2_sc_dealt[8 * r : 8 * r + span : 4, :].bitcast(I32),
                 )
 
-        for a in range(K_PASSES):
-            deal_ws(a)
-        for a in range(K_PASSES):
-            gather_visitors(a)
-            deal_ws_scales(a)
-            log_pass(0, a)
+        nc.sync.dma_start(out=ws_w[:], in_=ws_words.rearrange("a p c -> p a c").bitcast(I32))
+        nc.sync.dma_start(idx[:], offs)
+        load_tab(0)
+        load_vectors()
+        load_scales(tab_scales, tab_sc)
+        load_tab(1)
+        load_ws_scales()
+        load_wm(0, 0)
+        turn_vectors()
+        nc.vector.tensor_copy(v_sc[0][:], tab_sc[:].indirect(idx[:]))
+        deal_ws_pass(0)
+        gather_visitors(0)
+        move_planes(v_sc)
+        load_tab(2)
+        load_tab2_scales()
+        nc.sync.dma_start(idx2[:], offs2)
+        load_wm(0, 1)
+        load_wm(0, 2)
+        load_eps(0)
+        load_wm(1, 0)
+        load_wm(1, 1)
+        log_pass(0, 0)
+        deal_ws_pass(1)
+        gather_visitors(1)
+        log_pass(0, 1)
+        deal_ws_pass(2)
+        gather_visitors(2)
+        log_pass(0, 2)
         exp_stage(0)
-        for a in range(K_PASSES):
-            log_pass(1, a)
+        log_pass(1, 0)
+        log_pass(1, 1)
+        log_pass(1, 2)
         exp_stage(1)
         gather_arm_scales()
-        for b in range(R_PASSES):
-            for a in range(K_PASSES):
-                quantise_wm(b, a)
-                mean_pass(b, a)
-            h_stage(b)
-
+        load_wm(1, 2)
+        load_tab2(0)
+        move_arm_scales()
+        load_eps(1)
+        load_tab2(1)
+        quantise_wm(0, 0, 128)
+        mean_pass(0, 0)
+        quantise_wm(0, 1, 128)
+        mean_pass(0, 1)
+        quantise_wm(0, 2, 0)
+        mean_pass(0, 2)
+        noise_stage(0)
+        h_stage(0)
+        quantise_wm(1, 0, 128)
+        mean_pass(1, 0)
+        quantise_wm(1, 1, 128)
+        mean_pass(1, 1)
+        quantise_wm(1, 2, 128)
+        mean_pass(1, 2)
+        noise_stage(1)
+        h_stage(1)
         def gather_arms(b, g):
             first_store_slot = (b, g) in ((R_PASSES - 1, 0), (0, I_GROUPS - 1))
             tag = "v2_w_first_store" if first_store_slot else "v2_w%d%d" % (b, g)
@@ -267,34 +318,54 @@ def tile_list_thompson_arm_rewards_kernel(
             return words
 
         y_s = held([P, I_GROUPS, S], U8, "y_s")
+        y_q = held([P, I_GROUPS, S], I32, "y_q")
+        ys = {}
+
+        def quantise_y(g):
+            y_bf = woven("y_bf%d" % g)
+            halves = [slice(u * S // 2, (u + 1) * S // 2) for u in range(2)]
+            for u, js in enumerate(halves):
+                copy = nc.scalar.copy if (g, u) in ((2, 1),) else nc.vector.tensor_copy
+                copy(
+                    out=y_bf[:, js, :].rearrange("p (c i) t -> p c t i", i=2),
+                    in_=ys[g][:, :, js].rearrange("p t (c i) -> p c t i", i=2),
+                )
+            for js in halves:
+                nc.vector.quantize_mx(
+                    out=y_q[:, g, js].bitcast(FP8X4), scales=y_s[:, g, js], in_=y_bf[:, js, :].rearrange("p j t -> p (j t)")
+                )
+
+        def store_codes(queue, gs):
+            queue.dma_start(out=out_1[gs].rearrange("g p m t -> p g (m t)").bitcast(I32), in_=y_q[:, gs, :])
+
         for g in range(I_GROUPS):
             y_banks = [bank(4 * (1 - g % 2) + t) for t in range(PACK)]
             v2_w = [gather_arms(b, g) for b in range(R_PASSES)]
-            for b in range(R_PASSES):
-                for t in range(PACK):
-                    c0 = g * PASS + t * P
-                    nc.tensor.matmul_mx(
-                        out=y_banks[t][:],
-                        lhsT=v2_w[b][:, t, :].bitcast(FP8X4),
-                        lhsT_scale=v2_sc_dealt[4 * b : P, c0 : c0 + P],
-                        rhs=h_q[b][:].bitcast(FP8X4),
-                        rhs_scale=h_s[b][:],
-                        start=(b == 0),
-                        stop=(b == R_PASSES - 1),
-                    )
-            y = wm_or_y_block("y%d" % g)
+            steps = [(b, t) for b in range(R_PASSES) for t in range(PACK)]
+            if g == I_GROUPS - 1:
+                steps = [(b, t) for t in range(PACK) for b in range(R_PASSES)]
+            for b, t in steps:
+                c0 = g * PASS + t * P
+                nc.tensor.matmul_mx(
+                    out=y_banks[t][:],
+                    lhsT=v2_w[b][:, t, :].bitcast(FP8X4),
+                    lhsT_scale=v2_sc_dealt[4 * b : P, c0 : c0 + P],
+                    rhs=h_q[b][:].bitcast(FP8X4),
+                    rhs_scale=h_s[b][:],
+                    start=(b == 0),
+                    stop=(b == R_PASSES - 1),
+                )
+            ys[g] = wm_or_y_block("y%d" % g)
             y_rows = out_0[g * PASS : (g + 1) * PASS, :].rearrange("(p t) j -> p t j", t=PACK)
+            rows = [1,1,1][g]
             for t in range(PACK):
-                nc.scalar.activation(out=y[:, t, :], in_=y_banks[t][:], func=ACT.Copy, scale=pay_sb[:, g, t : t + 1])
-                if t % 2 == 1:
-                    nc.sync.dma_start(out=y_rows[:, t - 1 : t + 1, :], in_=y[:, t - 1 : t + 1, :])
-            y_bf = woven("y_bf%d" % g)
-            nc.vector.tensor_copy(
-                y_bf[:].rearrange("p (c i) t -> p c t i", i=2), y[:].rearrange("p t (c i) -> p c t i", i=2)
-            )
-            y_q = held([P, S], I32, "y_q%d" % g)
-            nc.vector.quantize_mx(out=y_q[:].bitcast(FP8X4), scales=y_s[:, g, :], in_=y_bf[:].rearrange("p j t -> p (j t)"))
-            nc.sync.dma_start(out=out_1[g].rearrange("p m t -> p (m t)").bitcast(I32), in_=y_q[:])
+                nc.scalar.activation(
+                    out=ys[g][:, t, :], in_=y_banks[t][:], func=ACT.Copy, scale=vec_cols[:, t, R_PASSES + g : R_PASSES + g + 1]
+                )
+                if (t + 1) % rows == 0:
+                    nc.sync.dma_start(out=y_rows[:, t + 1 - rows : t + 1, :], in_=ys[g][:, t + 1 - rows : t + 1, :])
+            quantise_y(g)
+            store_codes(nc.sync, slice(g, g + 1))
         y_scale_rows = out_2.rearrange("g (q r) m -> r q g m", r=QUAD_ROWS)
         for r in range(QUAD_ROWS):
             nc.sync.dma_start(out=y_scale_rows[r].bitcast(I32), in_=y_s[r:P:32, :, :].bitcast(I32))

@@ -27,7 +27,8 @@ QUADS = 4
 QUAD_ROWS = 4
 J_PARTS = S // P
 LIST_COLS = PASS // 16
-WM_HALF = 6
+WM_SLOTS = 6
+SCALAR_SHARE = 40
 VEC_ROWS = R_PASSES + I_GROUPS
 MOVE_ROWS = 112
 
@@ -46,10 +47,10 @@ def tile_list_thompson_arm_rewards_kernel(
             return keep.tile(shape, dtype, name=name, align_bytes=64)
 
         def wm_or_y_block(name):
-            return ring.tile([P, PACK, PASS], F32, name=name, tag="wm_or_y", bufs=WM_HALF, align_bytes=64)
+            return ring.tile([P, PACK, PASS], F32, name=name, tag="wm_or_y", bufs=WM_SLOTS, align_bytes=64)
 
-        def tab_or_noise_block(shape, dtype, name):
-            return ring.tile(shape, dtype, name=name, tag="tab_or_noise", bufs=K_PASSES, align_bytes=64)
+        def tab_or_noise_block(shape, dtype, name, slot):
+            return ring.tile(shape, dtype, name=name, tag="tab_slot%d" % slot, bufs=1, align_bytes=64)
 
         def woven(name):
             return ring.tile([P, S, PACK], BF16, name=name, tag="woven", bufs=2, align_bytes=64)
@@ -84,7 +85,13 @@ def tile_list_thompson_arm_rewards_kernel(
             nc.vector.memset(plane[:].bitcast(I32), 0)
 
         tab_w, tab2_w, eps_sb, wm_raw = [], [], {}, {}
-        ws_w = held([P, K_PASSES, H // 2], I32, "ws_w")
+        ws_w = {}
+
+        def load_ws(first, last):
+            words = held([P, last - first, H // 2], I32, "ws_w%d" % first)
+            nc.sync.dma_start(out=words[:], in_=ws_words[first:last].rearrange("a p c -> p a c").bitcast(I32))
+            for a in range(first, last):
+                ws_w[a] = words[:, a - first, :]
 
         def load_scales(src, dst):
             for q in range(QUADS):
@@ -99,7 +106,7 @@ def tile_list_thompson_arm_rewards_kernel(
                 nc.sync.dma_start(out=ws_sc[r:P:32, :, :].bitcast(I32), in_=rows[r].bitcast(I32))
 
         def load_tab(a):
-            words = tab_or_noise_block([P, T], I32, "tab_w%d" % a)
+            words = tab_or_noise_block([P, T], I32, "tab_w%d" % a, a)
             nc.sync.dma_start(out=words[:], in_=tab_words[a].rearrange("p n t -> p (n t)").bitcast(I32))
             tab_w.append(words)
 
@@ -116,6 +123,12 @@ def tile_list_thompson_arm_rewards_kernel(
             block = wm[a * PASS : (a + 1) * PASS, b * PASS : (b + 1) * PASS]
             nc.sync.dma_start(out=raw[:], in_=block.rearrange("(p j) c -> p j c", j=PACK))
             wm_raw[(b, a)] = raw[:]
+
+        def load_wm_rows(a):
+            raw = held([P, PACK, H], F32, "wm_rows%d" % a)
+            nc.sync.dma_start(out=raw[:], in_=wm[a * PASS : (a + 1) * PASS, :].rearrange("(p j) c -> p j c", j=PACK))
+            for b in range(R_PASSES):
+                wm_raw[(b, a)] = raw[:, :, b * PASS : (b + 1) * PASS]
 
         def load_eps(b):
             rows = held([P, PACK, S], F32, "eps%d" % b)
@@ -135,7 +148,7 @@ def tile_list_thompson_arm_rewards_kernel(
         def deal_ws(a):
             nc.vector.tensor_copy(
                 ws_dealt[:, a, :].bitcast(U16).rearrange("p (b t m) -> p b t m", b=R_PASSES, t=PACK),
-                ws_w[:, a, :].bitcast(U16).rearrange("p (b m t) -> p b t m", b=R_PASSES, t=PACK),
+                ws_w[a].bitcast(U16).rearrange("p (b m t) -> p b t m", b=R_PASSES, t=PACK),
             )
 
         def deal_ws_scales(a):
@@ -159,13 +172,14 @@ def tile_list_thompson_arm_rewards_kernel(
             rounded = ring.tile([P, PACK, P, PACK], BF16, name="wm_bf%d%d" % (b, a), tag="wm_bf", bufs=4, align_bytes=64)
             dst = rounded[:].rearrange("p (u e) m j -> p u m j e", e=2)
             src = wm_raw[(b, a)].rearrange("p j (m u e) -> p u m j e", u=2, e=2)
-            cut = on_scalar // 64
-            for copy, us in ((nc.scalar.copy, slice(0, cut)), (nc.vector.tensor_copy, slice(cut, 2))):
-                if us.stop - us.start == 2:
-                    copy(out=dst, in_=src)
-                elif us.stop - us.start == 1:
-                    copy(out=dst[:, us.start], in_=src[:, us.start])
-            wm_q[(b, a)] = held([P, PASS], U32, "wm_q%d%d" % (b, a))
+            if on_scalar > 0:
+                nc.scalar.copy(out=dst[:, :, 0:on_scalar], in_=src[:, :, 0:on_scalar])
+            if on_scalar < P:
+                nc.vector.tensor_copy(out=dst[:, :, on_scalar:P], in_=src[:, :, on_scalar:P])
+            if (b, a) == (R_PASSES - 1, K_PASSES - 1):
+                wm_q[(b, a)] = ring.tile([P, PASS], U32, name="wm_q12", tag="wm_q12_then_arms", bufs=1, align_bytes=64)
+            else:
+                wm_q[(b, a)] = held([P, PASS], U32, "wm_q%d%d" % (b, a))
             wm_s[(b, a)] = held([P, PASS], U8, "wm_s%d%d" % (b, a))
             nc.vector.quantize_mx(
                 out=wm_q[(b, a)][:].bitcast(FP8X4), scales=wm_s[(b, a)][:], in_=rounded[:].rearrange("p t m j -> p (t m j)")
@@ -206,7 +220,10 @@ def tile_list_thompson_arm_rewards_kernel(
                     )
 
         def exp_stage(b):
-            noise[b] = tab_or_noise_block([P, PACK, S], F32, "noise%d" % b)
+            if b == 0:
+                noise[b] = tab_or_noise_block([P, PACK, S], F32, "noise%d" % b, 0)
+            else:
+                noise[b] = ring.tile([P, PACK, S], F32, name="noise1", tag="noise1_then_arms", bufs=1, align_bytes=64)
             for t in range(PACK):
                 nc.scalar.activation(out=noise[b][:, t, :], in_=log_banks[b][t][:], func=ACT.Exp, bias=vec_cols[:, t, b : b + 1])
 
@@ -231,17 +248,17 @@ def tile_list_thompson_arm_rewards_kernel(
             h_s[b] = held([P, S], U8, "h_s%d" % b)
             nc.vector.quantize_mx(out=h_q[b][:].bitcast(FP8X4), scales=h_s[b][:], in_=h_bf[:].rearrange("p j t -> p (j t)"))
 
-        v2_sc = held([P, S2], U8, "v2_sc")
         v2_sc_dealt = held([P, S2], U8, "v2_sc_dealt")
 
-        def gather_arm_scales():
-            for g in range(I_GROUPS):
-                nc.vector.tensor_copy(
-                    v2_sc[:, g * PASS : (g + 1) * PASS], tab2_sc[:].indirect(idx2[:, g * LIST_COLS : (g + 1) * LIST_COLS])
-                )
+        def gather_arm_scales(g):
+            if g == I_GROUPS - 1:
+                picked = tab_or_noise_block([P, PASS], U8, "v2_sc%d" % g, K_PASSES - 1)
+            else:
+                picked = held([P, PASS], U8, "v2_sc%d" % g)
+            nc.vector.tensor_copy(picked[:], tab2_sc[:].indirect(idx2[:, g * LIST_COLS : (g + 1) * LIST_COLS]))
             nc.vector.tensor_copy(
-                v2_sc_dealt[:].rearrange("p (g u e m) -> p u g e m", g=I_GROUPS, u=2, e=2),
-                v2_sc[:].rearrange("p (g m u e) -> p u g e m", g=I_GROUPS, u=2, e=2),
+                v2_sc_dealt[:, g * PASS : (g + 1) * PASS].rearrange("p (u e m) -> p u e m", u=2, e=2),
+                picked[:].rearrange("p (m u e) -> p u e m", u=2, e=2),
             )
 
         def move_arm_scales():
@@ -252,32 +269,49 @@ def tile_list_thompson_arm_rewards_kernel(
                     in_=v2_sc_dealt[8 * r : 8 * r + span : 4, :].bitcast(I32),
                 )
 
-        nc.sync.dma_start(out=ws_w[:], in_=ws_words.rearrange("a p c -> p a c").bitcast(I32))
+        v2_w = {}
+
+        def gather_arms(b, g):
+            if b == 0:
+                words = held([P, PACK, P], U32, "v2_w%d%d" % (b, g))
+            else:
+                tag = "noise1_then_arms" if g == 1 else "wm_q12_then_arms"
+                words = ring.tile([P, PACK, P], U32, name="v2_w%d%d" % (b, g), tag=tag, bufs=1, align_bytes=64)
+            nc.vector.tensor_copy(
+                words[:].rearrange("p t m -> p m t"),
+                tab2_w[b][:].bitcast(U32).indirect(idx2[:, g * LIST_COLS : (g + 1) * LIST_COLS]),
+            )
+            v2_w[(b, g)] = words
+
+        load_ws(0, 3)
         nc.sync.dma_start(idx[:], offs)
         load_tab(0)
         load_vectors()
         load_scales(tab_scales, tab_sc)
         load_tab(1)
         load_ws_scales()
+        nc.sync.dma_start(idx2[:], offs2)
+        load_tab2_scales()
         load_wm(0, 0)
         turn_vectors()
         nc.vector.tensor_copy(v_sc[0][:], tab_sc[:].indirect(idx[:]))
-        deal_ws_pass(0)
+        deal_ws(0)
+        deal_ws_scales(0)
         gather_visitors(0)
         move_planes(v_sc)
         load_tab(2)
-        load_tab2_scales()
-        nc.sync.dma_start(idx2[:], offs2)
         load_wm(0, 1)
         load_wm(0, 2)
         load_eps(0)
         load_wm(1, 0)
-        load_wm(1, 1)
+        load_tab2(0)
         log_pass(0, 0)
-        deal_ws_pass(1)
+        deal_ws(1)
+        deal_ws_scales(1)
         gather_visitors(1)
         log_pass(0, 1)
-        deal_ws_pass(2)
+        deal_ws(2)
+        deal_ws_scales(2)
         gather_visitors(2)
         log_pass(0, 2)
         exp_stage(0)
@@ -285,10 +319,12 @@ def tile_list_thompson_arm_rewards_kernel(
         log_pass(1, 1)
         log_pass(1, 2)
         exp_stage(1)
-        gather_arm_scales()
-        load_wm(1, 2)
-        load_tab2(0)
+        gather_arm_scales(0)
+        gather_arm_scales(1)
+        gather_arm_scales(2)
         move_arm_scales()
+        load_wm(1, 1)
+        load_wm(1, 2)
         load_eps(1)
         load_tab2(1)
         quantise_wm(0, 0, 128)
@@ -301,38 +337,34 @@ def tile_list_thompson_arm_rewards_kernel(
         h_stage(0)
         quantise_wm(1, 0, 128)
         mean_pass(1, 0)
+        gather_arms(0, 0)
+        gather_arms(0, 1)
+        gather_arms(0, 2)
         quantise_wm(1, 1, 128)
         mean_pass(1, 1)
-        quantise_wm(1, 2, 128)
+        quantise_wm(1, 2, 64)
         mean_pass(1, 2)
         noise_stage(1)
         h_stage(1)
-        def gather_arms(b, g):
-            first_store_slot = (b, g) in ((R_PASSES - 1, 0), (0, I_GROUPS - 1))
-            tag = "v2_w_first_store" if first_store_slot else "v2_w%d%d" % (b, g)
-            words = ring.tile([P, PACK, P], U32, name="v2_w%d%d" % (b, g), tag=tag, bufs=1, align_bytes=64)
-            nc.vector.tensor_copy(
-                words[:].rearrange("p t m -> p m t"),
-                tab2_w[b][:].bitcast(U32).indirect(idx2[:, g * LIST_COLS : (g + 1) * LIST_COLS]),
-            )
-            return words
-
         y_s = held([P, I_GROUPS, S], U8, "y_s")
         y_q = held([P, I_GROUPS, S], I32, "y_q")
         ys = {}
 
         def quantise_y(g):
-            y_bf = woven("y_bf%d" % g)
             halves = [slice(u * S // 2, (u + 1) * S // 2) for u in range(2)]
+            y_bf = []
             for u, js in enumerate(halves):
+                tag = "y_bf%d%d" % (g % 2, u)
+                half = ring.tile([P, S // 2, PACK], BF16, name="y_bf%d%d" % (g, u), tag=tag, bufs=1, align_bytes=64)
                 copy = nc.scalar.copy if (g, u) in ((2, 1),) else nc.vector.tensor_copy
                 copy(
-                    out=y_bf[:, js, :].rearrange("p (c i) t -> p c t i", i=2),
+                    out=half[:].rearrange("p (c i) t -> p c t i", i=2),
                     in_=ys[g][:, :, js].rearrange("p t (c i) -> p c t i", i=2),
                 )
-            for js in halves:
+                y_bf.append(half)
+            for u, js in enumerate(halves):
                 nc.vector.quantize_mx(
-                    out=y_q[:, g, js].bitcast(FP8X4), scales=y_s[:, g, js], in_=y_bf[:, js, :].rearrange("p j t -> p (j t)")
+                    out=y_q[:, g, js].bitcast(FP8X4), scales=y_s[:, g, js], in_=y_bf[u][:].rearrange("p j t -> p (j t)")
                 )
 
         def store_codes(queue, gs):
@@ -340,7 +372,7 @@ def tile_list_thompson_arm_rewards_kernel(
 
         for g in range(I_GROUPS):
             y_banks = [bank(4 * (1 - g % 2) + t) for t in range(PACK)]
-            v2_w = [gather_arms(b, g) for b in range(R_PASSES)]
+            gather_arms(1, g)
             steps = [(b, t) for b in range(R_PASSES) for t in range(PACK)]
             if g == I_GROUPS - 1:
                 steps = [(b, t) for t in range(PACK) for b in range(R_PASSES)]
@@ -348,7 +380,7 @@ def tile_list_thompson_arm_rewards_kernel(
                 c0 = g * PASS + t * P
                 nc.tensor.matmul_mx(
                     out=y_banks[t][:],
-                    lhsT=v2_w[b][:, t, :].bitcast(FP8X4),
+                    lhsT=v2_w[(b, g)][:, t, :].bitcast(FP8X4),
                     lhsT_scale=v2_sc_dealt[4 * b : P, c0 : c0 + P],
                     rhs=h_q[b][:].bitcast(FP8X4),
                     rhs_scale=h_s[b][:],
@@ -357,15 +389,16 @@ def tile_list_thompson_arm_rewards_kernel(
                 )
             ys[g] = wm_or_y_block("y%d" % g)
             y_rows = out_0[g * PASS : (g + 1) * PASS, :].rearrange("(p t) j -> p t j", t=PACK)
-            rows = [1,1,1][g]
+            rows = 1 if g == 0 else 2
             for t in range(PACK):
                 nc.scalar.activation(
                     out=ys[g][:, t, :], in_=y_banks[t][:], func=ACT.Copy, scale=vec_cols[:, t, R_PASSES + g : R_PASSES + g + 1]
                 )
                 if (t + 1) % rows == 0:
                     nc.sync.dma_start(out=y_rows[:, t + 1 - rows : t + 1, :], in_=ys[g][:, t + 1 - rows : t + 1, :])
+        for g in range(I_GROUPS):
             quantise_y(g)
-            store_codes(nc.sync, slice(g, g + 1))
+            store_codes(nc.scalar if g < I_GROUPS - 1 else nc.sync, slice(g, g + 1))
         y_scale_rows = out_2.rearrange("g (q r) m -> r q g m", r=QUAD_ROWS)
         for r in range(QUAD_ROWS):
             nc.sync.dma_start(out=y_scale_rows[r].bitcast(I32), in_=y_s[r:P:32, :, :].bitcast(I32))

@@ -46,8 +46,8 @@ def tile_list_thompson_arm_rewards_kernel(
         def held(shape, dtype, name):
             return keep.tile(shape, dtype, name=name, align_bytes=64)
 
-        def wm_or_y_block(name):
-            return ring.tile([P, PACK, PASS], F32, name=name, tag="wm_or_y", bufs=WM_SLOTS, align_bytes=64)
+        def wm_or_y_block(name, slot):
+            return ring.tile([P, PACK, PASS], F32, name=name, tag="wm_slot%d" % slot, bufs=1, align_bytes=64)
 
         def tab_or_noise_block(shape, dtype, name, slot):
             return ring.tile(shape, dtype, name=name, tag="tab_slot%d" % slot, bufs=1, align_bytes=64)
@@ -77,11 +77,11 @@ def tile_list_thompson_arm_rewards_kernel(
             nc.scalar.copy(out=vec_cols[:], in_=turned[:].rearrange("p (t c) -> p t c", t=PACK)[:, :, 0:VEC_ROWS])
 
         tab_sc = held([P, T], U8, "tab_sc")
-        ws_sc = held([P, K_PASSES, H], U8, "ws_sc")
+        ws_sc = ring.tile([P, K_PASSES, H], U8, name="ws_sc", tag="ws_sc", bufs=1, align_bytes=64)
         tab2_sc = held([P, T2], U8, "tab2_sc")
         v_sc = [held([P, S], U8, "v_sc%d" % a) for a in range(K_PASSES)]
         ws_sc_dealt = held([P, K_PASSES, H], U8, "ws_sc_dealt")
-        for plane in [tab_sc, ws_sc, tab2_sc] + v_sc[1:]:
+        for plane in [tab2_sc, tab_sc, ws_sc] + v_sc[1:]:
             nc.vector.memset(plane[:].bitcast(I32), 0)
 
         tab_w, tab2_w, eps_sb, wm_raw = [], [], {}, {}
@@ -119,7 +119,7 @@ def tile_list_thompson_arm_rewards_kernel(
             nc.sync.dma_start(out=tab2_sc[0:P:4, :].bitcast(I32), in_=tab2_scales.rearrange("b q t -> q b t").bitcast(I32))
 
         def load_wm(b, a):
-            raw = wm_or_y_block("wm_raw%d%d" % (b, a))
+            raw = wm_or_y_block("wm_raw%d%d" % (b, a), K_PASSES * b + a)
             block = wm[a * PASS : (a + 1) * PASS, b * PASS : (b + 1) * PASS]
             nc.sync.dma_start(out=raw[:], in_=block.rearrange("(p j) c -> p j c", j=PACK))
             wm_raw[(b, a)] = raw[:]
@@ -130,10 +130,12 @@ def tile_list_thompson_arm_rewards_kernel(
             for b in range(R_PASSES):
                 wm_raw[(b, a)] = raw[:, :, b * PASS : (b + 1) * PASS]
 
-        def load_eps(b):
-            rows = held([P, PACK, S], F32, "eps%d" % b)
-            nc.sync.dma_start(out=rows[:], in_=eps[b * PASS : (b + 1) * PASS, :].rearrange("(p t) j -> p t j", t=PACK))
-            eps_sb[b] = rows
+        def load_eps(b, first, last):
+            rows = held([P, 2 * (last - first), S], F32, "eps%d%d" % (b, first))
+            src = eps[b * PASS : (b + 1) * PASS, :].rearrange("(p t) j -> p t j", t=PACK)
+            nc.sync.dma_start(out=rows[:], in_=src[:, 2 * first : 2 * last, :])
+            for u in range(first, last):
+                eps_sb[(b, u)] = rows[:, 2 * (u - first) : 2 * (u - first + 1), :]
 
         def move_planes(planes):
             for a in range(1, K_PASSES):
@@ -176,10 +178,7 @@ def tile_list_thompson_arm_rewards_kernel(
                 nc.scalar.copy(out=dst[:, :, 0:on_scalar], in_=src[:, :, 0:on_scalar])
             if on_scalar < P:
                 nc.vector.tensor_copy(out=dst[:, :, on_scalar:P], in_=src[:, :, on_scalar:P])
-            if (b, a) == (R_PASSES - 1, K_PASSES - 1):
-                wm_q[(b, a)] = ring.tile([P, PASS], U32, name="wm_q12", tag="wm_q12_then_arms", bufs=1, align_bytes=64)
-            else:
-                wm_q[(b, a)] = held([P, PASS], U32, "wm_q%d%d" % (b, a))
+            wm_q[(b, a)] = held([P, PASS], U32, "wm_q%d%d" % (b, a))
             wm_s[(b, a)] = held([P, PASS], U8, "wm_s%d%d" % (b, a))
             nc.vector.quantize_mx(
                 out=wm_q[(b, a)][:].bitcast(FP8X4), scales=wm_s[(b, a)][:], in_=rounded[:].rearrange("p t m j -> p (t m j)")
@@ -189,7 +188,7 @@ def tile_list_thompson_arm_rewards_kernel(
 
         def log_pass(b, a):
             if a == 0:
-                log_banks[b] = [bank(t) for t in range(PACK)]
+                log_banks[b] = [bank(4 * b + t) for t in range(PACK)]
             for t in range(PACK):
                 c0 = b * PASS + t * P
                 nc.tensor.matmul_mx(
@@ -204,7 +203,7 @@ def tile_list_thompson_arm_rewards_kernel(
 
         def mean_pass(b, a):
             if a == 0:
-                mean_banks[b] = [bank(4 * (1 - b) + jq) for jq in range(J_PARTS)]
+                mean_banks[b] = [bank(4 * b + jq) for jq in range(J_PARTS)]
             for jq in range(J_PARTS):
                 js = slice(jq * P, (jq + 1) * P)
                 for t in range(PACK):
@@ -221,9 +220,9 @@ def tile_list_thompson_arm_rewards_kernel(
 
         def exp_stage(b):
             if b == 0:
-                noise[b] = tab_or_noise_block([P, PACK, S], F32, "noise%d" % b, 0)
+                noise[b] = tab_or_noise_block([P, PACK, S], F32, "noise%d" % b, b)
             else:
-                noise[b] = ring.tile([P, PACK, S], F32, name="noise1", tag="noise1_then_arms", bufs=1, align_bytes=64)
+                noise[b] = wm_or_y_block("noise%d" % b, K_PASSES - 1)
             for t in range(PACK):
                 nc.scalar.activation(out=noise[b][:, t, :], in_=log_banks[b][t][:], func=ACT.Exp, bias=vec_cols[:, t, b : b + 1])
 
@@ -232,7 +231,7 @@ def tile_list_thompson_arm_rewards_kernel(
         def noise_stage(b):
             for u in range(2):
                 ts = slice(2 * u, 2 * u + 2)
-                nc.vector.tensor_tensor(noise[b][:, ts, :], noise[b][:, ts, :], eps_sb[b][:, ts, :], ALU.mult)
+                nc.vector.tensor_tensor(noise[b][:, ts, :], noise[b][:, ts, :], eps_sb[(b, u)], ALU.mult)
 
         def h_stage(b):
             h_bf = woven("h_bf%d" % b)
@@ -251,10 +250,8 @@ def tile_list_thompson_arm_rewards_kernel(
         v2_sc_dealt = held([P, S2], U8, "v2_sc_dealt")
 
         def gather_arm_scales(g):
-            if g == I_GROUPS - 1:
-                picked = tab_or_noise_block([P, PASS], U8, "v2_sc%d" % g, K_PASSES - 1)
-            else:
-                picked = held([P, PASS], U8, "v2_sc%d" % g)
+            tag = ("v2_sc0", "ws_sc", "tab_slot2")[g]
+            picked = ring.tile([P, PASS], U8, name="v2_sc%d" % g, tag=tag, bufs=1, align_bytes=64)
             nc.vector.tensor_copy(picked[:], tab2_sc[:].indirect(idx2[:, g * LIST_COLS : (g + 1) * LIST_COLS]))
             nc.vector.tensor_copy(
                 v2_sc_dealt[:, g * PASS : (g + 1) * PASS].rearrange("p (u e m) -> p u e m", u=2, e=2),
@@ -272,80 +269,79 @@ def tile_list_thompson_arm_rewards_kernel(
         v2_w = {}
 
         def gather_arms(b, g):
-            if b == 0:
-                words = held([P, PACK, P], U32, "v2_w%d%d" % (b, g))
-            else:
-                tag = "noise1_then_arms" if g == 1 else "wm_q12_then_arms"
-                words = ring.tile([P, PACK, P], U32, name="v2_w%d%d" % (b, g), tag=tag, bufs=1, align_bytes=64)
+            first_store_slot = (b, g) in ((R_PASSES - 1, 0), (0, I_GROUPS - 1))
+            tag = "v2_w_first_store" if first_store_slot else "v2_w%d%d" % (b, g)
+            words = ring.tile([P, PACK, P], U32, name="v2_w%d%d" % (b, g), tag=tag, bufs=1, align_bytes=64)
             nc.vector.tensor_copy(
                 words[:].rearrange("p t m -> p m t"),
                 tab2_w[b][:].bitcast(U32).indirect(idx2[:, g * LIST_COLS : (g + 1) * LIST_COLS]),
             )
             v2_w[(b, g)] = words
 
-        load_ws(0, 3)
+        load_ws(0, 1)
+        nc.sync.dma_start(idx2[:], offs2)
+        load_tab2_scales()
+        load_ws(1, 3)
         nc.sync.dma_start(idx[:], offs)
         load_tab(0)
         load_vectors()
         load_scales(tab_scales, tab_sc)
         load_tab(1)
         load_ws_scales()
-        nc.sync.dma_start(idx2[:], offs2)
-        load_tab2_scales()
         load_wm(0, 0)
         turn_vectors()
-        nc.vector.tensor_copy(v_sc[0][:], tab_sc[:].indirect(idx[:]))
         deal_ws(0)
-        deal_ws_scales(0)
+        gather_arm_scales(0)
+        deal_ws(1)
+        deal_ws(2)
         gather_visitors(0)
+        nc.vector.tensor_copy(v_sc[0][:], tab_sc[:].indirect(idx[:]))
         move_planes(v_sc)
         load_tab(2)
         load_wm(0, 1)
         load_wm(0, 2)
-        load_eps(0)
+        load_eps(0, 0, 1)
+        load_eps(0, 1, 2)
         load_wm(1, 0)
-        load_tab2(0)
+        load_wm(1, 1)
+        deal_ws_scales(0)
         log_pass(0, 0)
-        deal_ws(1)
-        deal_ws_scales(1)
         gather_visitors(1)
+        deal_ws_scales(1)
         log_pass(0, 1)
-        deal_ws(2)
         deal_ws_scales(2)
+        gather_arm_scales(1)
         gather_visitors(2)
         log_pass(0, 2)
         exp_stage(0)
+        quantise_wm(0, 0, 128)
+        gather_arm_scales(2)
+        move_arm_scales()
+        load_wm(1, 2)
+        load_eps(1, 0, 2)
+        load_tab2(0)
+        load_tab2(1)
+        quantise_wm(0, 1, 0)
+        quantise_wm(0, 2, 128)
         log_pass(1, 0)
         log_pass(1, 1)
         log_pass(1, 2)
         exp_stage(1)
-        gather_arm_scales(0)
-        gather_arm_scales(1)
-        gather_arm_scales(2)
-        move_arm_scales()
-        load_wm(1, 1)
-        load_wm(1, 2)
-        load_eps(1)
-        load_tab2(1)
-        quantise_wm(0, 0, 128)
         mean_pass(0, 0)
-        quantise_wm(0, 1, 128)
         mean_pass(0, 1)
-        quantise_wm(0, 2, 0)
         mean_pass(0, 2)
         noise_stage(0)
         h_stage(0)
         quantise_wm(1, 0, 128)
         mean_pass(1, 0)
-        gather_arms(0, 0)
-        gather_arms(0, 1)
-        gather_arms(0, 2)
-        quantise_wm(1, 1, 128)
+        quantise_wm(1, 1, 64)
         mean_pass(1, 1)
-        quantise_wm(1, 2, 64)
+        quantise_wm(1, 2, 128)
         mean_pass(1, 2)
         noise_stage(1)
         h_stage(1)
+        gather_arms(0, 0)
+        gather_arms(0, 1)
         y_s = held([P, I_GROUPS, S], U8, "y_s")
         y_q = held([P, I_GROUPS, S], I32, "y_q")
         ys = {}
@@ -371,11 +367,14 @@ def tile_list_thompson_arm_rewards_kernel(
             queue.dma_start(out=out_1[gs].rearrange("g p m t -> p g (m t)").bitcast(I32), in_=y_q[:, gs, :])
 
         for g in range(I_GROUPS):
-            y_banks = [bank(4 * (1 - g % 2) + t) for t in range(PACK)]
+            y_banks = [bank(4 * (g % 2) + t) for t in range(PACK)]
+            if g == I_GROUPS - 1:
+                gather_arms(0, g)
             gather_arms(1, g)
             steps = [(b, t) for b in range(R_PASSES) for t in range(PACK)]
-            if g == I_GROUPS - 1:
-                steps = [(b, t) for t in range(PACK) for b in range(R_PASSES)]
+            if g > 0:
+                steps = [(b, t) for t in range(PACK) for b in reversed(range(R_PASSES))]
+            first = steps[0][0]
             for b, t in steps:
                 c0 = g * PASS + t * P
                 nc.tensor.matmul_mx(
@@ -384,10 +383,10 @@ def tile_list_thompson_arm_rewards_kernel(
                     lhsT_scale=v2_sc_dealt[4 * b : P, c0 : c0 + P],
                     rhs=h_q[b][:].bitcast(FP8X4),
                     rhs_scale=h_s[b][:],
-                    start=(b == 0),
-                    stop=(b == R_PASSES - 1),
+                    start=(b == first),
+                    stop=(b != first),
                 )
-            ys[g] = wm_or_y_block("y%d" % g)
+            ys[g] = wm_or_y_block("y%d" % g, (0, 1, 3)[g])
             y_rows = out_0[g * PASS : (g + 1) * PASS, :].rearrange("(p t) j -> p t j", t=PACK)
             rows = 1 if g == 0 else 2
             for t in range(PACK):
@@ -398,7 +397,7 @@ def tile_list_thompson_arm_rewards_kernel(
                     nc.sync.dma_start(out=y_rows[:, t + 1 - rows : t + 1, :], in_=ys[g][:, t + 1 - rows : t + 1, :])
         for g in range(I_GROUPS):
             quantise_y(g)
-            store_codes(nc.scalar if g < I_GROUPS - 1 else nc.sync, slice(g, g + 1))
+            store_codes(nc.scalar if g == 0 else nc.sync, slice(g, g + 1))
         y_scale_rows = out_2.rearrange("g (q r) m -> r q g m", r=QUAD_ROWS)
         for r in range(QUAD_ROWS):
             nc.sync.dma_start(out=y_scale_rows[r].bitcast(I32), in_=y_s[r:P:32, :, :].bitcast(I32))

@@ -79,9 +79,10 @@ def tile_list_thompson_arm_rewards_kernel(
         tab_sc = held([P, T], U8, "tab_sc")
         ws_sc = ring.tile([P, K_PASSES, H], U8, name="ws_sc", tag="ws_sc", bufs=1, align_bytes=64)
         tab2_sc = held([P, T2], U8, "tab2_sc")
+        v_sc_picked = held([P, S], U8, "v_sc_picked")
         v_sc = [held([P, S], U8, "v_sc%d" % a) for a in range(K_PASSES)]
         ws_sc_dealt = held([P, K_PASSES, H], U8, "ws_sc_dealt")
-        for plane in [tab2_sc, tab_sc, ws_sc] + v_sc[1:]:
+        for plane in [tab2_sc, tab_sc, ws_sc] + v_sc:
             nc.vector.memset(plane[:].bitcast(I32), 0)
 
         tab_w, tab2_w, eps_sb, wm_raw = [], [], {}, {}
@@ -93,12 +94,10 @@ def tile_list_thompson_arm_rewards_kernel(
             for a in range(first, last):
                 ws_w[a] = words[:, a - first, :]
 
-        def load_scales(src, dst):
-            for q in range(QUADS):
-                nc.sync.dma_start(
-                    out=dst[32 * q : 32 * q + QUAD_ROWS * K_PASSES, :].bitcast(I32),
-                    in_=src[:, QUAD_ROWS * q : QUAD_ROWS * (q + 1), :].bitcast(I32),
-                )
+        def load_tab_scales():
+            rows = tab_scales.rearrange("a q t -> q a t").bitcast(I32)
+            nc.sync.dma_start(out=tab_sc[0:P:4, :].bitcast(I32), in_=rows[:, 0:K_PASSES:2, :])
+            nc.sync.dma_start(out=tab_sc[2:P:8, :].bitcast(I32), in_=rows[:, 1, :])
 
         def load_ws_scales():
             rows = ws_scales.rearrange("a (q r) t -> r q a t", r=QUAD_ROWS)
@@ -137,11 +136,10 @@ def tile_list_thompson_arm_rewards_kernel(
             for u in range(first, last):
                 eps_sb[(b, u)] = rows[:, 2 * (u - first) : 2 * (u - first + 1), :]
 
-        def move_planes(planes):
-            for a in range(1, K_PASSES):
+        def move_plane(a):
+            for r in range(QUAD_ROWS):
                 nc.sync.dma_start(
-                    out=planes[a][0:MOVE_ROWS, :].bitcast(I32),
-                    in_=planes[0][QUAD_ROWS * a : QUAD_ROWS * a + MOVE_ROWS, :].bitcast(I32),
+                    out=v_sc[a][r:P:32, :].bitcast(I32), in_=v_sc_picked[8 * r + 2 * a : P : 32, :].bitcast(I32)
                 )
 
         ws_dealt = held([P, K_PASSES, 2 * H], U8, "ws_dealt")
@@ -281,29 +279,31 @@ def tile_list_thompson_arm_rewards_kernel(
         load_ws(0, 1)
         nc.sync.dma_start(idx2[:], offs2)
         load_tab2_scales()
-        load_ws(1, 3)
         nc.sync.dma_start(idx[:], offs)
+        load_tab_scales()
+        load_ws(1, 3)
         load_tab(0)
         load_vectors()
-        load_scales(tab_scales, tab_sc)
-        load_tab(1)
         load_ws_scales()
-        load_wm(0, 0)
+        load_tab(1)
         turn_vectors()
         deal_ws(0)
-        gather_arm_scales(0)
-        deal_ws(1)
-        deal_ws(2)
-        gather_visitors(0)
-        nc.vector.tensor_copy(v_sc[0][:], tab_sc[:].indirect(idx[:]))
-        move_planes(v_sc)
+        nc.vector.tensor_copy(v_sc_picked[:], tab_sc[:].indirect(idx[:]))
+        move_plane(0)
+        load_wm(0, 0)
+        move_plane(1)
         load_tab(2)
+        move_plane(2)
         load_wm(0, 1)
         load_wm(0, 2)
         load_eps(0, 0, 1)
         load_eps(0, 1, 2)
         load_wm(1, 0)
         load_wm(1, 1)
+        gather_arm_scales(0)
+        deal_ws(1)
+        deal_ws(2)
+        gather_visitors(0)
         deal_ws_scales(0)
         log_pass(0, 0)
         gather_visitors(1)
@@ -400,4 +400,5 @@ def tile_list_thompson_arm_rewards_kernel(
             store_codes(nc.scalar if g == 0 else nc.sync, slice(g, g + 1))
         y_scale_rows = out_2.rearrange("g (q r) m -> r q g m", r=QUAD_ROWS)
         for r in range(QUAD_ROWS):
-            nc.sync.dma_start(out=y_scale_rows[r].bitcast(I32), in_=y_s[r:P:32, :, :].bitcast(I32))
+            queue = nc.sync if r < QUAD_ROWS // 2 else nc.scalar
+            queue.dma_start(out=y_scale_rows[r].bitcast(I32), in_=y_s[r:P:32, :, :].bitcast(I32))

@@ -352,11 +352,14 @@ def tile_list_thompson_arm_rewards_kernel(
             for u, js in enumerate(halves):
                 tag = "y_bf%d%d" % (g % 2, u)
                 half = ring.tile([P, S // 2, PACK], BF16, name="y_bf%d%d" % (g, u), tag=tag, bufs=1, align_bytes=64)
-                copy = nc.scalar.copy if (g, u) in ((2, 1),) else nc.vector.tensor_copy
-                copy(
-                    out=half[:].rearrange("p (c i) t -> p c t i", i=2),
-                    in_=ys[g][:, :, js].rearrange("p t (c i) -> p c t i", i=2),
-                )
+                dst = half[:].rearrange("p (c i) t -> p c t i", i=2)
+                src = ys[g][:, :, js].rearrange("p t (c i) -> p c t i", i=2)
+                if (g, u) == (0, 1):
+                    nc.gpsimd.tensor_scalar(out=dst, in0=src, scalar1=1.0, scalar2=-0.0, op0=ALU.mult, op1=ALU.add)
+                elif (g, u) == (I_GROUPS - 1, 1):
+                    nc.scalar.copy(out=dst, in_=src)
+                else:
+                    nc.vector.tensor_copy(out=dst, in_=src)
                 y_bf.append(half)
             for u, js in enumerate(halves):
                 nc.vector.quantize_mx(

@@ -23,14 +23,15 @@ PASS = P * PACK
 K_PASSES = K // PASS
 R_PASSES = H // PASS
 I_GROUPS = S2 // PASS
-QUADS = 4
 QUAD_ROWS = 4
 J_PARTS = S // P
 LIST_COLS = PASS // 16
-WM_SLOTS = 6
-SCALAR_SHARE = 40
 VEC_ROWS = R_PASSES + I_GROUPS
-MOVE_ROWS = 112
+ALL_ON_SCALAR, ALL_ON_VECTOR = P, 0
+SHARED_BLOCK = 64
+ROUNDED_SLOTS = 4
+LAST_WEAVE = 104
+Y_SLOTS = (0, 1, 3)
 
 
 def tile_list_thompson_arm_rewards_kernel(
@@ -123,12 +124,6 @@ def tile_list_thompson_arm_rewards_kernel(
             nc.sync.dma_start(out=raw[:], in_=block.rearrange("(p j) c -> p j c", j=PACK))
             wm_raw[(b, a)] = raw[:]
 
-        def load_wm_rows(a):
-            raw = held([P, PACK, H], F32, "wm_rows%d" % a)
-            nc.sync.dma_start(out=raw[:], in_=wm[a * PASS : (a + 1) * PASS, :].rearrange("(p j) c -> p j c", j=PACK))
-            for b in range(R_PASSES):
-                wm_raw[(b, a)] = raw[:, :, b * PASS : (b + 1) * PASS]
-
         def load_eps(b, first, last):
             rows = held([P, 2 * (last - first), S], F32, "eps%d%d" % (b, first))
             src = eps[b * PASS : (b + 1) * PASS, :].rearrange("(p t) j -> p t j", t=PACK)
@@ -157,9 +152,8 @@ def tile_list_thompson_arm_rewards_kernel(
                 ws_sc[:, a, :].rearrange("p (b m t) -> p b t m", b=R_PASSES, t=PACK),
             )
 
-        def deal_ws_pass(a):
-            deal_ws(a)
-            deal_ws_scales(a)
+        def gather_visitor_scales():
+            nc.vector.tensor_copy(v_sc_picked[:], tab_sc[:].indirect(idx[:]))
 
         def gather_visitors(a):
             words = held([P, S], U32, "v_w%d" % a)
@@ -169,7 +163,9 @@ def tile_list_thompson_arm_rewards_kernel(
         wm_q, wm_s = {}, {}
 
         def quantise_wm(b, a, on_scalar):
-            rounded = ring.tile([P, PACK, P, PACK], BF16, name="wm_bf%d%d" % (b, a), tag="wm_bf", bufs=4, align_bytes=64)
+            rounded = ring.tile(
+                [P, PACK, P, PACK], BF16, name="wm_bf%d%d" % (b, a), tag="wm_bf", bufs=ROUNDED_SLOTS, align_bytes=64
+            )
             dst = rounded[:].rearrange("p (u e) m j -> p u m j e", e=2)
             src = wm_raw[(b, a)].rearrange("p j (m u e) -> p u m j e", u=2, e=2)
             if on_scalar > 0:
@@ -257,12 +253,12 @@ def tile_list_thompson_arm_rewards_kernel(
             )
 
         def move_arm_scales():
-            span = 32 * (QUADS - 1) + 4 * R_PASSES
-            for r in range(1, QUAD_ROWS):
-                nc.sync.dma_start(
-                    out=v2_sc_dealt[r : r + span : 4, :].bitcast(I32),
-                    in_=v2_sc_dealt[8 * r : 8 * r + span : 4, :].bitcast(I32),
-                )
+            for b in range(R_PASSES):
+                for r in range(1, QUAD_ROWS):
+                    nc.sync.dma_start(
+                        out=v2_sc_dealt[r + 4 * b : P : 32, :].bitcast(I32),
+                        in_=v2_sc_dealt[8 * r + 4 * b : P : 32, :].bitcast(I32),
+                    )
 
         v2_w = {}
 
@@ -281,14 +277,14 @@ def tile_list_thompson_arm_rewards_kernel(
         load_tab2_scales()
         nc.sync.dma_start(idx[:], offs)
         load_tab_scales()
-        load_ws(1, 3)
+        load_ws(1, K_PASSES)
         load_tab(0)
         load_vectors()
         load_ws_scales()
         load_tab(1)
         turn_vectors()
         deal_ws(0)
-        nc.vector.tensor_copy(v_sc_picked[:], tab_sc[:].indirect(idx[:]))
+        gather_visitor_scales()
         move_plane(0)
         load_wm(0, 0)
         move_plane(1)
@@ -314,34 +310,33 @@ def tile_list_thompson_arm_rewards_kernel(
         gather_visitors(2)
         log_pass(0, 2)
         exp_stage(0)
-        quantise_wm(0, 0, 128)
+        quantise_wm(0, 0, ALL_ON_SCALAR)
         gather_arm_scales(2)
         move_arm_scales()
         load_wm(1, 2)
         load_eps(1, 0, 2)
         load_tab2(0)
         load_tab2(1)
-        quantise_wm(0, 1, 0)
-        quantise_wm(0, 2, 128)
-        log_pass(1, 0)
-        log_pass(1, 1)
-        log_pass(1, 2)
+        quantise_wm(0, 1, ALL_ON_VECTOR)
+        quantise_wm(0, 2, ALL_ON_SCALAR)
+        for a in range(K_PASSES):
+            log_pass(1, a)
         exp_stage(1)
-        mean_pass(0, 0)
-        mean_pass(0, 1)
-        mean_pass(0, 2)
+        for a in range(K_PASSES):
+            mean_pass(0, a)
         noise_stage(0)
         h_stage(0)
-        quantise_wm(1, 0, 128)
+        quantise_wm(1, 0, ALL_ON_SCALAR)
         mean_pass(1, 0)
-        quantise_wm(1, 1, 64)
+        quantise_wm(1, 1, SHARED_BLOCK)
         mean_pass(1, 1)
-        quantise_wm(1, 2, 128)
+        quantise_wm(1, 2, ALL_ON_SCALAR)
         mean_pass(1, 2)
         noise_stage(1)
         h_stage(1)
         gather_arms(0, 0)
         gather_arms(0, 1)
+
         y_s = held([P, I_GROUPS, S], U8, "y_s")
         y_q = held([P, I_GROUPS, S], I32, "y_q")
         ys = {}
@@ -357,7 +352,8 @@ def tile_list_thompson_arm_rewards_kernel(
                 if (g, u) == (0, 1):
                     nc.gpsimd.tensor_scalar(out=dst, in0=src, scalar1=1.0, scalar2=-0.0, op0=ALU.mult, op1=ALU.add)
                 elif (g, u) == (I_GROUPS - 1, 1):
-                    nc.scalar.copy(out=dst, in_=src)
+                    nc.scalar.copy(out=dst[:, 0:LAST_WEAVE], in_=src[:, 0:LAST_WEAVE])
+                    nc.vector.tensor_copy(out=dst[:, LAST_WEAVE:], in_=src[:, LAST_WEAVE:])
                 else:
                     nc.vector.tensor_copy(out=dst, in_=src)
                 y_bf.append(half)
@@ -365,9 +361,6 @@ def tile_list_thompson_arm_rewards_kernel(
                 nc.vector.quantize_mx(
                     out=y_q[:, g, js].bitcast(FP8X4), scales=y_s[:, g, js], in_=y_bf[u][:].rearrange("p j t -> p (j t)")
                 )
-
-        def store_codes(queue, gs):
-            queue.dma_start(out=out_1[gs].rearrange("g p m t -> p g (m t)").bitcast(I32), in_=y_q[:, gs, :])
 
         for g in range(I_GROUPS):
             y_banks = [bank(4 * (g % 2) + t) for t in range(PACK)]
@@ -389,7 +382,7 @@ def tile_list_thompson_arm_rewards_kernel(
                     start=(b == first),
                     stop=(b != first),
                 )
-            ys[g] = wm_or_y_block("y%d" % g, (0, 1, 3)[g])
+            ys[g] = wm_or_y_block("y%d" % g, Y_SLOTS[g])
             y_rows = out_0[g * PASS : (g + 1) * PASS, :].rearrange("(p t) j -> p t j", t=PACK)
             rows = 1 if g == 0 else 2
             for t in range(PACK):
@@ -400,7 +393,9 @@ def tile_list_thompson_arm_rewards_kernel(
                     nc.sync.dma_start(out=y_rows[:, t + 1 - rows : t + 1, :], in_=ys[g][:, t + 1 - rows : t + 1, :])
         for g in range(I_GROUPS):
             quantise_y(g)
-            store_codes(nc.scalar if g == 0 else nc.sync, slice(g, g + 1))
+            gs = slice(g, g + 1)
+            queue = nc.scalar if g == 0 else nc.sync
+            queue.dma_start(out=out_1[gs].rearrange("g p m t -> p g (m t)").bitcast(I32), in_=y_q[:, gs, :])
         y_scale_rows = out_2.rearrange("g (q r) m -> r q g m", r=QUAD_ROWS)
         for r in range(QUAD_ROWS):
             queue = nc.sync if r < QUAD_ROWS // 2 else nc.scalar

@@ -28,10 +28,11 @@ J_PARTS = S // P
 LIST_COLS = PASS // 16
 VEC_ROWS = R_PASSES + I_GROUPS
 ALL_ON_SCALAR, ALL_ON_VECTOR = P, 0
-SHARED_BLOCK = 64
-ROUNDED_SLOTS = 4
+LAST_BLOCK_SHARE = 48
+ROUNDED_SLOTS = ("wm_bf0", "wm_bf1", "bs", "bs", "eps01", "eps10")
+FIRST_ROW = (0, 2, 64)
+ARM_PLANE = 8
 LAST_WEAVE = 104
-Y_SLOTS = (0, 1, 3)
 
 
 def tile_list_thompson_arm_rewards_kernel(
@@ -47,47 +48,47 @@ def tile_list_thompson_arm_rewards_kernel(
         def held(shape, dtype, name):
             return keep.tile(shape, dtype, name=name, align_bytes=64)
 
-        def wm_or_y_block(name, slot):
-            return ring.tile([P, PACK, PASS], F32, name=name, tag="wm_slot%d" % slot, bufs=1, align_bytes=64)
-
-        def tab_or_noise_block(shape, dtype, name, slot):
-            return ring.tile(shape, dtype, name=name, tag="tab_slot%d" % slot, bufs=1, align_bytes=64)
-
-        def woven(name):
-            return ring.tile([P, S, PACK], BF16, name=name, tag="woven", bufs=2, align_bytes=64)
+        def in_slot(shape, dtype, name, slot):
+            return ring.tile(shape, dtype, name=name, tag=slot, bufs=1, align_bytes=64)
 
         def bank(n):
             return psum.tile([P, PASS], F32, name="bank%d" % n, tag="bank%d" % n)
 
         idx = keep.tile([P, S // 16], U16, name="idx")
         idx2 = keep.tile([P, S2 // 16], U16, name="idx2")
+
+        tab_sc = held([P, T], U8, "tab_sc")
+        ws_sc = held([P, H], U8, "ws_sc")
+        tab2_sc = held([P, T2], U8, "tab2_sc")
+        plane_tiles = [held([P, 2, S + H], U8, "planes01"), held([P, 1, S + H], U8, "planes2")]
+        planes = [plane_tiles[a // 2][:, a % 2, :] for a in range(K_PASSES)]
+        arm_planes = held([P, R_PASSES, S2], U8, "arm_planes")
+        for cleared in [tab_sc, ws_sc, tab2_sc] + plane_tiles + [arm_planes]:
+            nc.vector.memset(cleared[:].bitcast(I32), 0)
+
         vec_rows = held([P, PASS], F32, "vec_rows")
         ident = held([P, P], F32, "ident")
-        vec_cols = held([P, PACK, VEC_ROWS], F32, "vec_cols")
+        bs_cols = in_slot([P, PACK, R_PASSES], F32, "bs_cols", "bs")
+        pay_cols = held([P, PACK, I_GROUPS], F32, "pay_cols")
         nc.gpsimd.memset(vec_rows[:], 0.0)
         make_identity(nc, ident[:])
 
-        def load_vectors():
-            nc.sync.dma_start(out=vec_rows[0:R_PASSES, :], in_=bs.rearrange("(b c) -> b c", c=PASS))
-            nc.sync.dma_start(out=vec_rows[R_PASSES:VEC_ROWS, :], in_=pay.rearrange("(g c) -> g c", c=PASS))
+        tab_w, tab2_w, ws_w, eps_sb, wm_raw = [], [], {}, {}, {}
 
         def turn_vectors():
             turned = bank(7)
             for t in range(PACK):
                 nc.tensor.transpose(turned[:, t * P : (t + 1) * P], vec_rows[:, t:PASS:PACK], ident[:])
-            nc.scalar.copy(out=vec_cols[:], in_=turned[:].rearrange("p (t c) -> p t c", t=PACK)[:, :, 0:VEC_ROWS])
+            cols = turned[:].rearrange("p (t c) -> p t c", t=PACK)
+            nc.scalar.copy(out=bs_cols[:], in_=cols[:, :, 0:R_PASSES])
+            nc.scalar.copy(out=pay_cols[:], in_=cols[:, :, R_PASSES:VEC_ROWS])
 
-        tab_sc = held([P, T], U8, "tab_sc")
-        ws_sc = ring.tile([P, K_PASSES, H], U8, name="ws_sc", tag="ws_sc", bufs=1, align_bytes=64)
-        tab2_sc = held([P, T2], U8, "tab2_sc")
-        v_sc_picked = held([P, S], U8, "v_sc_picked")
-        v_sc = [held([P, S], U8, "v_sc%d" % a) for a in range(K_PASSES)]
-        ws_sc_dealt = held([P, K_PASSES, H], U8, "ws_sc_dealt")
-        for plane in [tab2_sc, tab_sc, ws_sc] + v_sc:
-            nc.vector.memset(plane[:].bitcast(I32), 0)
-
-        tab_w, tab2_w, eps_sb, wm_raw = [], [], {}, {}
-        ws_w = {}
+        def load_scale_rows(rows, scales):
+            for a in range(K_PASSES):
+                nc.sync.dma_start(
+                    out=rows[FIRST_ROW[a] : FIRST_ROW[a] // 64 * 64 + 64 : 4, :].bitcast(I32),
+                    in_=scales[a].rearrange("(q r) t -> r q t", r=QUAD_ROWS).bitcast(I32),
+                )
 
         def load_ws(first, last):
             words = held([P, last - first, H // 2], I32, "ws_w%d" % first)
@@ -95,18 +96,8 @@ def tile_list_thompson_arm_rewards_kernel(
             for a in range(first, last):
                 ws_w[a] = words[:, a - first, :]
 
-        def load_tab_scales():
-            rows = tab_scales.rearrange("a q t -> q a t").bitcast(I32)
-            nc.sync.dma_start(out=tab_sc[0:P:4, :].bitcast(I32), in_=rows[:, 0:K_PASSES:2, :])
-            nc.sync.dma_start(out=tab_sc[2:P:8, :].bitcast(I32), in_=rows[:, 1, :])
-
-        def load_ws_scales():
-            rows = ws_scales.rearrange("a (q r) t -> r q a t", r=QUAD_ROWS)
-            for r in range(QUAD_ROWS):
-                nc.sync.dma_start(out=ws_sc[r:P:32, :, :].bitcast(I32), in_=rows[r].bitcast(I32))
-
         def load_tab(a):
-            words = tab_or_noise_block([P, T], I32, "tab_w%d" % a, a)
+            words = in_slot([P, T], I32, "tab_w%d" % a, "tab%d" % a)
             nc.sync.dma_start(out=words[:], in_=tab_words[a].rearrange("p n t -> p (n t)").bitcast(I32))
             tab_w.append(words)
 
@@ -116,119 +107,137 @@ def tile_list_thompson_arm_rewards_kernel(
             tab2_w.append(words)
 
         def load_tab2_scales():
-            nc.sync.dma_start(out=tab2_sc[0:P:4, :].bitcast(I32), in_=tab2_scales.rearrange("b q t -> q b t").bitcast(I32))
+            for b in range(R_PASSES):
+                nc.sync.dma_start(
+                    out=tab2_sc[4 * b : P : 8, :].bitcast(I32),
+                    in_=tab2_scales[b].rearrange("(q r) t -> r q t", r=QUAD_ROWS).bitcast(I32),
+                )
 
         def load_wm(b, a):
-            raw = wm_or_y_block("wm_raw%d%d" % (b, a), K_PASSES * b + a)
+            raw = in_slot([P, PACK, PASS], F32, "wm_raw%d%d" % (b, a), "wm%d" % (K_PASSES * b + a))
             block = wm[a * PASS : (a + 1) * PASS, b * PASS : (b + 1) * PASS]
             nc.sync.dma_start(out=raw[:], in_=block.rearrange("(p j) c -> p j c", j=PACK))
             wm_raw[(b, a)] = raw[:]
 
-        def load_eps(b, first, last):
-            rows = held([P, 2 * (last - first), S], F32, "eps%d%d" % (b, first))
+        def load_eps(b, u):
+            rows = in_slot([P, 2, S], F32, "eps%d%d" % (b, u), "eps%d%d" % (b, u))
             src = eps[b * PASS : (b + 1) * PASS, :].rearrange("(p t) j -> p t j", t=PACK)
-            nc.sync.dma_start(out=rows[:], in_=src[:, 2 * first : 2 * last, :])
-            for u in range(first, last):
-                eps_sb[(b, u)] = rows[:, 2 * (u - first) : 2 * (u - first + 1), :]
+            nc.sync.dma_start(out=rows[:], in_=src[:, 2 * u : 2 * u + 2, :])
+            eps_sb[(b, u)] = rows
 
-        def move_plane(a):
-            for r in range(QUAD_ROWS):
-                nc.sync.dma_start(
-                    out=v_sc[a][r:P:32, :].bitcast(I32), in_=v_sc_picked[8 * r + 2 * a : P : 32, :].bitcast(I32)
-                )
-
-        ws_dealt = held([P, K_PASSES, 2 * H], U8, "ws_dealt")
+        ws_dealt = [held([P, 2 * H], U8, "ws_dealt%d" % a) for a in range(K_PASSES)]
+        v_sc_picked = held([P, S], U8, "v_sc_picked")
+        staged = held([P, S + H], U8, "staged")
         v_w = []
 
         def deal_ws(a):
-            nc.vector.tensor_copy(
-                ws_dealt[:, a, :].bitcast(U16).rearrange("p (b t m) -> p b t m", b=R_PASSES, t=PACK),
-                ws_w[a].bitcast(U16).rearrange("p (b m t) -> p b t m", b=R_PASSES, t=PACK),
+            nc.scalar.copy(
+                out=ws_dealt[a][:].bitcast(U16).rearrange("p (b t m) -> p b t m", b=R_PASSES, t=PACK),
+                in_=ws_w[a].bitcast(U16).rearrange("p (b m t) -> p b t m", b=R_PASSES, t=PACK),
             )
 
-        def deal_ws_scales(a):
-            nc.vector.tensor_copy(
-                ws_sc_dealt[:, a, :].rearrange("p (b t m) -> p b t m", b=R_PASSES, t=PACK),
-                ws_sc[:, a, :].rearrange("p (b m t) -> p b t m", b=R_PASSES, t=PACK),
-            )
-
-        def gather_visitor_scales():
+        def stage_scales():
             nc.vector.tensor_copy(v_sc_picked[:], tab_sc[:].indirect(idx[:]))
+            nc.vector.tensor_copy(
+                staged[:, S:].rearrange("p (b t m) -> p b t m", b=R_PASSES, t=PACK),
+                ws_sc[:].rearrange("p (b m t) -> p b t m", b=R_PASSES, t=PACK),
+            )
+            nc.vector.tensor_copy(staged[:, 0:S].bitcast(I32), v_sc_picked[:].bitcast(I32))
+
+        def move_planes(first, last):
+            for r in range(QUAD_ROWS):
+                p0 = FIRST_ROW[first] + 16 * r
+                nc.sync.dma_start(
+                    out=plane_tiles[first // 2][r:P:32, :, :].bitcast(I32),
+                    in_=staged[p0 : p0 + 16 : 4 // (last - first), :].bitcast(I32),
+                )
 
         def gather_visitors(a):
             words = held([P, S], U32, "v_w%d" % a)
             nc.vector.tensor_copy(words[:], tab_w[a][:].bitcast(U32).indirect(idx[:]))
             v_w.append(words)
 
-        wm_q, wm_s = {}, {}
+        v2_sc = held([P, S2], U8, "v2_sc")
 
-        def quantise_wm(b, a, on_scalar):
-            rounded = ring.tile(
-                [P, PACK, P, PACK], BF16, name="wm_bf%d%d" % (b, a), tag="wm_bf", bufs=ROUNDED_SLOTS, align_bytes=64
+        def gather_arm_scales(g, picked):
+            nc.vector.tensor_copy(picked[:], tab2_sc[:].indirect(idx2[:, g * LIST_COLS : (g + 1) * LIST_COLS]))
+            nc.vector.tensor_copy(
+                v2_sc[:, g * PASS : (g + 1) * PASS].rearrange("p (u e m) -> p u e m", u=2, e=2),
+                picked[:].rearrange("p (m u e) -> p u e m", u=2, e=2),
             )
-            dst = rounded[:].rearrange("p (u e) m j -> p u m j e", e=2)
+
+        def move_arm_scales():
+            for r in range(QUAD_ROWS):
+                nc.sync.dma_start(
+                    out=arm_planes[ARM_PLANE + r : P : 32, :, :].bitcast(I32),
+                    in_=v2_sc[32 * r : 32 * (r + 1) : 4, :].bitcast(I32),
+                )
+
+        rounded, wm_q, wm_s = {}, {}, {}
+
+        def round_wm(b, a, on_scalar):
+            rounded[(b, a)] = in_slot([P, PACK, P, PACK], BF16, "wm_bf%d%d" % (b, a), ROUNDED_SLOTS[K_PASSES * b + a])
+            dst = rounded[(b, a)][:].rearrange("p (u e) m j -> p u m j e", e=2)
             src = wm_raw[(b, a)].rearrange("p j (m u e) -> p u m j e", u=2, e=2)
             if on_scalar > 0:
                 nc.scalar.copy(out=dst[:, :, 0:on_scalar], in_=src[:, :, 0:on_scalar])
             if on_scalar < P:
                 nc.vector.tensor_copy(out=dst[:, :, on_scalar:P], in_=src[:, :, on_scalar:P])
+
+        def quantise_wm(b, a):
             wm_q[(b, a)] = held([P, PASS], U32, "wm_q%d%d" % (b, a))
             wm_s[(b, a)] = held([P, PASS], U8, "wm_s%d%d" % (b, a))
             nc.vector.quantize_mx(
-                out=wm_q[(b, a)][:].bitcast(FP8X4), scales=wm_s[(b, a)][:], in_=rounded[:].rearrange("p t m j -> p (t m j)")
+                out=wm_q[(b, a)][:].bitcast(FP8X4),
+                scales=wm_s[(b, a)][:],
+                in_=rounded[(b, a)][:].rearrange("p t m j -> p (t m j)"),
             )
 
-        log_banks, mean_banks, noise = {}, {}, {}
+        mean_banks, noise, h_q, h_s = {}, {}, {}, {}
 
-        def log_pass(b, a):
-            if a == 0:
-                log_banks[b] = [bank(4 * b + t) for t in range(PACK)]
-            for t in range(PACK):
+        def log_stage(b):
+            banks = [bank(4 * b + t) for t in range(PACK)]
+            steps = [(a, t) for a in range(K_PASSES) for t in range(PACK)]
+            if b == 1:
+                steps = [(a, t) for t in range(PACK) for a in reversed(range(K_PASSES))]
+            first, last = steps[0][0], steps[-1][0]
+            for a, t in steps:
                 c0 = b * PASS + t * P
                 nc.tensor.matmul_mx(
-                    out=log_banks[b][t][:],
-                    lhsT=ws_dealt[:, a, 2 * c0 : 2 * (c0 + P)].bitcast(FP4X4),
-                    lhsT_scale=ws_sc_dealt[:, a, c0 : c0 + P],
+                    out=banks[t][:],
+                    lhsT=ws_dealt[a][:, 2 * c0 : 2 * (c0 + P)].bitcast(FP4X4),
+                    lhsT_scale=planes[a][:, S + c0 : S + c0 + P],
                     rhs=v_w[a][:].bitcast(FP8X4),
-                    rhs_scale=v_sc[a][:],
-                    start=(a == 0),
-                    stop=(a == K_PASSES - 1),
+                    rhs_scale=planes[a][:, 0:S],
+                    start=(a == first),
+                    stop=(a == last),
                 )
+            noise[b] = in_slot([P, PACK, S], F32, "noise%d" % b, "tab%d" % b)
+            for t in range(PACK):
+                nc.scalar.activation(out=noise[b][:, t, :], in_=banks[t][:], func=ACT.Exp, bias=bs_cols[:, t, b : b + 1])
 
         def mean_pass(b, a):
             if a == 0:
                 mean_banks[b] = [bank(4 * b + jq) for jq in range(J_PARTS)]
             for jq in range(J_PARTS):
-                js = slice(jq * P, (jq + 1) * P)
                 for t in range(PACK):
                     ms = slice(t * P, (t + 1) * P)
                     nc.tensor.matmul_mx(
                         out=mean_banks[b][jq][:, ms],
                         lhsT=wm_q[(b, a)][:, ms].bitcast(FP8X4),
                         lhsT_scale=wm_s[(b, a)][:, ms],
-                        rhs=v_w[a][:, js].bitcast(FP8X4),
-                        rhs_scale=v_sc[a][:, js],
+                        rhs=v_w[a][:, jq * P : (jq + 1) * P].bitcast(FP8X4),
+                        rhs_scale=planes[a][:, jq * P : (jq + 1) * P],
                         start=(a == 0 and t == 0),
                         stop=(a == K_PASSES - 1 and t == PACK - 1),
                     )
 
-        def exp_stage(b):
-            if b == 0:
-                noise[b] = tab_or_noise_block([P, PACK, S], F32, "noise%d" % b, b)
-            else:
-                noise[b] = wm_or_y_block("noise%d" % b, K_PASSES - 1)
-            for t in range(PACK):
-                nc.scalar.activation(out=noise[b][:, t, :], in_=log_banks[b][t][:], func=ACT.Exp, bias=vec_cols[:, t, b : b + 1])
-
-        h_q, h_s = {}, {}
-
-        def noise_stage(b):
-            for u in range(2):
-                ts = slice(2 * u, 2 * u + 2)
-                nc.vector.tensor_tensor(noise[b][:, ts, :], noise[b][:, ts, :], eps_sb[(b, u)], ALU.mult)
+        def times_eps(b, u):
+            ts = slice(2 * u, 2 * u + 2)
+            nc.vector.tensor_tensor(noise[b][:, ts, :], noise[b][:, ts, :], eps_sb[(b, u)][:], ALU.mult)
 
         def h_stage(b):
-            h_bf = woven("h_bf%d" % b)
+            h_bf = in_slot([P, S, PACK], BF16, "h_bf%d" % b, "h_bf%d" % b)
             for jq in range(J_PARTS):
                 js = slice(jq * P, (jq + 1) * P)
                 nc.vector.tensor_tensor(
@@ -241,99 +250,64 @@ def tile_list_thompson_arm_rewards_kernel(
             h_s[b] = held([P, S], U8, "h_s%d" % b)
             nc.vector.quantize_mx(out=h_q[b][:].bitcast(FP8X4), scales=h_s[b][:], in_=h_bf[:].rearrange("p j t -> p (j t)"))
 
-        v2_sc_dealt = held([P, S2], U8, "v2_sc_dealt")
-
-        def gather_arm_scales(g):
-            tag = ("v2_sc0", "ws_sc", "tab_slot2")[g]
-            picked = ring.tile([P, PASS], U8, name="v2_sc%d" % g, tag=tag, bufs=1, align_bytes=64)
-            nc.vector.tensor_copy(picked[:], tab2_sc[:].indirect(idx2[:, g * LIST_COLS : (g + 1) * LIST_COLS]))
-            nc.vector.tensor_copy(
-                v2_sc_dealt[:, g * PASS : (g + 1) * PASS].rearrange("p (u e m) -> p u e m", u=2, e=2),
-                picked[:].rearrange("p (m u e) -> p u e m", u=2, e=2),
-            )
-
-        def move_arm_scales():
-            for b in range(R_PASSES):
-                for r in range(1, QUAD_ROWS):
-                    nc.sync.dma_start(
-                        out=v2_sc_dealt[r + 4 * b : P : 32, :].bitcast(I32),
-                        in_=v2_sc_dealt[8 * r + 4 * b : P : 32, :].bitcast(I32),
-                    )
-
         v2_w = {}
 
         def gather_arms(b, g):
             first_store_slot = (b, g) in ((R_PASSES - 1, 0), (0, I_GROUPS - 1))
-            tag = "v2_w_first_store" if first_store_slot else "v2_w%d%d" % (b, g)
-            words = ring.tile([P, PACK, P], U32, name="v2_w%d%d" % (b, g), tag=tag, bufs=1, align_bytes=64)
+            words = in_slot([P, PACK, P], U32, "v2_w%d%d" % (b, g), "v2_w_first" if first_store_slot else "v2_w%d%d" % (b, g))
             nc.vector.tensor_copy(
                 words[:].rearrange("p t m -> p m t"),
                 tab2_w[b][:].bitcast(U32).indirect(idx2[:, g * LIST_COLS : (g + 1) * LIST_COLS]),
             )
             v2_w[(b, g)] = words
 
-        load_ws(0, 1)
+        nc.sync.dma_start(idx[:], offs)
+        load_ws(0, 2)
+        load_scale_rows(tab_sc, tab_scales)
+        load_scale_rows(ws_sc, ws_scales)
+        load_tab(0)
         nc.sync.dma_start(idx2[:], offs2)
         load_tab2_scales()
-        nc.sync.dma_start(idx[:], offs)
-        load_tab_scales()
-        load_ws(1, K_PASSES)
-        load_tab(0)
-        load_vectors()
-        load_ws_scales()
+        load_ws(2, 3)
         load_tab(1)
-        turn_vectors()
-        deal_ws(0)
-        gather_visitor_scales()
-        move_plane(0)
-        load_wm(0, 0)
-        move_plane(1)
+        nc.sync.dma_start(out=vec_rows[0:R_PASSES, :], in_=bs.rearrange("(b c) -> b c", c=PASS))
+        nc.sync.dma_start(out=vec_rows[R_PASSES:VEC_ROWS, :], in_=pay.rearrange("(g c) -> g c", c=PASS))
+        stage_scales()
+        move_planes(0, 2)
         load_tab(2)
-        move_plane(2)
-        load_wm(0, 1)
-        load_wm(0, 2)
-        load_eps(0, 0, 1)
-        load_eps(0, 1, 2)
-        load_wm(1, 0)
-        load_wm(1, 1)
-        gather_arm_scales(0)
-        deal_ws(1)
-        deal_ws(2)
+        move_planes(2, 3)
+        for a in range(K_PASSES):
+            deal_ws(a)
         gather_visitors(0)
-        deal_ws_scales(0)
-        log_pass(0, 0)
+        gather_arm_scales(0, held([P, PASS], U8, "arm_sc0"))
         gather_visitors(1)
-        deal_ws_scales(1)
-        log_pass(0, 1)
-        deal_ws_scales(2)
-        gather_arm_scales(1)
+        gather_arm_scales(1, in_slot([P, PASS], U8, "arm_sc1", "tab1"))
         gather_visitors(2)
-        log_pass(0, 2)
-        exp_stage(0)
-        quantise_wm(0, 0, ALL_ON_SCALAR)
-        gather_arm_scales(2)
-        move_arm_scales()
-        load_wm(1, 2)
-        load_eps(1, 0, 2)
+        gather_arm_scales(2, in_slot([P, PASS], U8, "arm_sc2", "tab2"))
+        for b in range(R_PASSES):
+            load_wm(b, 0)
+            load_wm(b, 1)
+            load_eps(b, 0)
+            if b == 0:
+                move_arm_scales()
+            load_wm(b, 2)
+            load_eps(b, 1)
         load_tab2(0)
         load_tab2(1)
-        quantise_wm(0, 1, ALL_ON_VECTOR)
-        quantise_wm(0, 2, ALL_ON_SCALAR)
-        for a in range(K_PASSES):
-            log_pass(1, a)
-        exp_stage(1)
-        for a in range(K_PASSES):
-            mean_pass(0, a)
-        noise_stage(0)
-        h_stage(0)
-        quantise_wm(1, 0, ALL_ON_SCALAR)
-        mean_pass(1, 0)
-        quantise_wm(1, 1, SHARED_BLOCK)
-        mean_pass(1, 1)
-        quantise_wm(1, 2, ALL_ON_SCALAR)
-        mean_pass(1, 2)
-        noise_stage(1)
-        h_stage(1)
+        turn_vectors()
+        log_stage(0)
+        log_stage(1)
+        for b in range(R_PASSES):
+            for a in range(K_PASSES - 1):
+                round_wm(b, a, ALL_ON_VECTOR if b == 0 else ALL_ON_SCALAR)
+                quantise_wm(b, a)
+                mean_pass(b, a)
+            times_eps(b, 0)
+            round_wm(b, K_PASSES - 1, LAST_BLOCK_SHARE)
+            quantise_wm(b, K_PASSES - 1)
+            mean_pass(b, K_PASSES - 1)
+            times_eps(b, 1)
+            h_stage(b)
         gather_arms(0, 0)
         gather_arms(0, 1)
 
@@ -345,8 +319,7 @@ def tile_list_thompson_arm_rewards_kernel(
             halves = [slice(u * S // 2, (u + 1) * S // 2) for u in range(2)]
             y_bf = []
             for u, js in enumerate(halves):
-                tag = "y_bf%d%d" % (g % 2, u)
-                half = ring.tile([P, S // 2, PACK], BF16, name="y_bf%d%d" % (g, u), tag=tag, bufs=1, align_bytes=64)
+                half = in_slot([P, S // 2, PACK], BF16, "y_bf%d%d" % (g, u), "y_bf%d%d" % (g % 2, u))
                 dst = half[:].rearrange("p (c i) t -> p c t i", i=2)
                 src = ys[g][:, :, js].rearrange("p t (c i) -> p c t i", i=2)
                 if (g, u) == (0, 1):
@@ -376,19 +349,17 @@ def tile_list_thompson_arm_rewards_kernel(
                 nc.tensor.matmul_mx(
                     out=y_banks[t][:],
                     lhsT=v2_w[(b, g)][:, t, :].bitcast(FP8X4),
-                    lhsT_scale=v2_sc_dealt[4 * b : P, c0 : c0 + P],
+                    lhsT_scale=arm_planes[ARM_PLANE:P, b, c0 : c0 + P],
                     rhs=h_q[b][:].bitcast(FP8X4),
                     rhs_scale=h_s[b][:],
                     start=(b == first),
                     stop=(b != first),
                 )
-            ys[g] = wm_or_y_block("y%d" % g, Y_SLOTS[g])
+            ys[g] = in_slot([P, PACK, S], F32, "y%d" % g, "wm%d" % g)
             y_rows = out_0[g * PASS : (g + 1) * PASS, :].rearrange("(p t) j -> p t j", t=PACK)
             rows = 1 if g == 0 else 2
             for t in range(PACK):
-                nc.scalar.activation(
-                    out=ys[g][:, t, :], in_=y_banks[t][:], func=ACT.Copy, scale=vec_cols[:, t, R_PASSES + g : R_PASSES + g + 1]
-                )
+                nc.scalar.activation(out=ys[g][:, t, :], in_=y_banks[t][:], func=ACT.Copy, scale=pay_cols[:, t, g : g + 1])
                 if (t + 1) % rows == 0:
                     nc.sync.dma_start(out=y_rows[:, t + 1 - rows : t + 1, :], in_=ys[g][:, t + 1 - rows : t + 1, :])
         for g in range(I_GROUPS):

@@ -30,7 +30,6 @@ VEC_ROWS = R_PASSES + I_GROUPS
 ALL_ON_SCALAR, ALL_ON_VECTOR = P, 0
 LAST_BLOCK_SHARE = 48
 ROUNDED_SLOTS = ("wm_bf0", "wm_bf1", "bs", "bs", "eps01", "eps10")
-FIRST_ROW = (0, 2, 64)
 ARM_PLANE = 8
 LAST_WEAVE = 104
 
@@ -60,10 +59,8 @@ def tile_list_thompson_arm_rewards_kernel(
         tab_sc = held([P, T], U8, "tab_sc")
         ws_sc = held([P, H], U8, "ws_sc")
         tab2_sc = held([P, T2], U8, "tab2_sc")
-        plane_tiles = [held([P, 2, S + H], U8, "planes01"), held([P, 1, S + H], U8, "planes2")]
-        planes = [plane_tiles[a // 2][:, a % 2, :] for a in range(K_PASSES)]
-        arm_planes = held([P, R_PASSES, S2], U8, "arm_planes")
-        for cleared in [tab_sc, ws_sc, tab2_sc] + plane_tiles + [arm_planes]:
+        planes = [held([P, S + H], U8, "planes%d" % a) for a in range(K_PASSES)]
+        for cleared in [tab_sc, ws_sc, tab2_sc] + planes:
             nc.vector.memset(cleared[:].bitcast(I32), 0)
 
         vec_rows = held([P, PASS], F32, "vec_rows")
@@ -84,11 +81,9 @@ def tile_list_thompson_arm_rewards_kernel(
             nc.scalar.copy(out=pay_cols[:], in_=cols[:, :, R_PASSES:VEC_ROWS])
 
         def load_scale_rows(rows, scales):
-            for a in range(K_PASSES):
-                nc.sync.dma_start(
-                    out=rows[FIRST_ROW[a] : FIRST_ROW[a] // 64 * 64 + 64 : 4, :].bitcast(I32),
-                    in_=scales[a].rearrange("(q r) t -> r q t", r=QUAD_ROWS).bitcast(I32),
-                )
+            by_block = scales.rearrange("a q t -> q a t").bitcast(I32)
+            nc.sync.dma_start(out=rows[0:P:4, :].bitcast(I32), in_=by_block[:, 0:K_PASSES:2, :])
+            nc.sync.dma_start(out=rows[2:P:8, :].bitcast(I32), in_=by_block[:, 1, :])
 
         def load_ws(first, last):
             words = held([P, last - first, H // 2], I32, "ws_w%d" % first)
@@ -107,11 +102,7 @@ def tile_list_thompson_arm_rewards_kernel(
             tab2_w.append(words)
 
         def load_tab2_scales():
-            for b in range(R_PASSES):
-                nc.sync.dma_start(
-                    out=tab2_sc[4 * b : P : 8, :].bitcast(I32),
-                    in_=tab2_scales[b].rearrange("(q r) t -> r q t", r=QUAD_ROWS).bitcast(I32),
-                )
+            nc.sync.dma_start(out=tab2_sc[1:P:4, :].bitcast(I32), in_=tab2_scales.rearrange("b q t -> q b t").bitcast(I32))
 
         def load_wm(b, a):
             raw = in_slot([P, PACK, PASS], F32, "wm_raw%d%d" % (b, a), "wm%d" % (K_PASSES * b + a))
@@ -144,13 +135,9 @@ def tile_list_thompson_arm_rewards_kernel(
             )
             nc.vector.tensor_copy(staged[:, 0:S].bitcast(I32), v_sc_picked[:].bitcast(I32))
 
-        def move_planes(first, last):
+        def move_planes(a):
             for r in range(QUAD_ROWS):
-                p0 = FIRST_ROW[first] + 16 * r
-                nc.sync.dma_start(
-                    out=plane_tiles[first // 2][r:P:32, :, :].bitcast(I32),
-                    in_=staged[p0 : p0 + 16 : 4 // (last - first), :].bitcast(I32),
-                )
+                nc.sync.dma_start(out=planes[a][r:P:32, :].bitcast(I32), in_=staged[8 * r + 2 * a : P : 32, :].bitcast(I32))
 
         def gather_visitors(a):
             words = held([P, S], U32, "v_w%d" % a)
@@ -166,11 +153,11 @@ def tile_list_thompson_arm_rewards_kernel(
                 picked[:].rearrange("p (m u e) -> p u e m", u=2, e=2),
             )
 
-        def move_arm_scales():
-            for r in range(QUAD_ROWS):
+        def move_arm_scales(b):
+            for r in (0, 2, 3):
                 nc.sync.dma_start(
-                    out=arm_planes[ARM_PLANE + r : P : 32, :, :].bitcast(I32),
-                    in_=v2_sc[32 * r : 32 * (r + 1) : 4, :].bitcast(I32),
+                    out=v2_sc[ARM_PLANE + 4 * b + r : P : 32, :].bitcast(I32),
+                    in_=v2_sc[8 * r + 4 * b + 1 : P : 32, :].bitcast(I32),
                 )
 
         rounded, wm_q, wm_s = {}, {}, {}
@@ -262,20 +249,23 @@ def tile_list_thompson_arm_rewards_kernel(
             v2_w[(b, g)] = words
 
         nc.sync.dma_start(idx[:], offs)
-        load_ws(0, 2)
+        load_ws(0, 1)
         load_scale_rows(tab_sc, tab_scales)
         load_scale_rows(ws_sc, ws_scales)
         load_tab(0)
         nc.sync.dma_start(idx2[:], offs2)
         load_tab2_scales()
+        load_ws(1, 2)
         load_ws(2, 3)
         load_tab(1)
         nc.sync.dma_start(out=vec_rows[0:R_PASSES, :], in_=bs.rearrange("(b c) -> b c", c=PASS))
         nc.sync.dma_start(out=vec_rows[R_PASSES:VEC_ROWS, :], in_=pay.rearrange("(g c) -> g c", c=PASS))
         stage_scales()
-        move_planes(0, 2)
+        move_planes(0)
         load_tab(2)
-        move_planes(2, 3)
+        move_planes(1)
+        load_wm(0, 0)
+        move_planes(2)
         for a in range(K_PASSES):
             deal_ws(a)
         gather_visitors(0)
@@ -285,12 +275,12 @@ def tile_list_thompson_arm_rewards_kernel(
         gather_visitors(2)
         gather_arm_scales(2, in_slot([P, PASS], U8, "arm_sc2", "tab2"))
         for b in range(R_PASSES):
-            load_wm(b, 0)
+            if b > 0:
+                load_wm(b, 0)
             load_wm(b, 1)
             load_eps(b, 0)
-            if b == 0:
-                move_arm_scales()
             load_wm(b, 2)
+            move_arm_scales(b)
             load_eps(b, 1)
         load_tab2(0)
         load_tab2(1)
@@ -349,7 +339,7 @@ def tile_list_thompson_arm_rewards_kernel(
                 nc.tensor.matmul_mx(
                     out=y_banks[t][:],
                     lhsT=v2_w[(b, g)][:, t, :].bitcast(FP8X4),
-                    lhsT_scale=arm_planes[ARM_PLANE:P, b, c0 : c0 + P],
+                    lhsT_scale=v2_sc[ARM_PLANE + 4 * b : P, c0 : c0 + P],
                     rhs=h_q[b][:].bitcast(FP8X4),
                     rhs_scale=h_s[b][:],
                     start=(b == first),

@@ -240,8 +240,7 @@ def tile_list_thompson_arm_rewards_kernel(
         v2_w = {}
 
         def gather_arms(b, g):
-            first_store_slot = (b, g) in ((R_PASSES - 1, 0), (0, I_GROUPS - 1))
-            words = in_slot([P, PACK, P], U32, "v2_w%d%d" % (b, g), "v2_w_first" if first_store_slot else "v2_w%d%d" % (b, g))
+            words = held([P, PACK, P], U32, "v2_w%d%d" % (b, g))
             nc.vector.tensor_copy(
                 words[:].rearrange("p t m -> p m t"),
                 tab2_w[b][:].bitcast(U32).indirect(idx2[:, g * LIST_COLS : (g + 1) * LIST_COLS]),
@@ -298,8 +297,8 @@ def tile_list_thompson_arm_rewards_kernel(
             mean_pass(b, K_PASSES - 1)
             times_eps(b, 1)
             h_stage(b)
-        gather_arms(0, 0)
-        gather_arms(0, 1)
+        for g in range(I_GROUPS):
+            gather_arms(0, g)
 
         y_s = held([P, I_GROUPS, S], U8, "y_s")
         y_q = held([P, I_GROUPS, S], I32, "y_q")
@@ -327,8 +326,6 @@ def tile_list_thompson_arm_rewards_kernel(
 
         for g in range(I_GROUPS):
             y_banks = [bank(4 * (g % 2) + t) for t in range(PACK)]
-            if g == I_GROUPS - 1:
-                gather_arms(0, g)
             gather_arms(1, g)
             steps = [(b, t) for b in range(R_PASSES) for t in range(PACK)]
             if g > 0:

@@ -31,6 +31,7 @@ ALL_ON_SCALAR, ALL_ON_VECTOR = P, 0
 LAST_BLOCK_SHARE = 48
 ROUNDED_SLOTS = ("wm_bf0", "wm_bf1", "bs", "bs", "eps01", "eps10")
 ARM_PLANE = 8
+VECTOR_BANK = (1, 3)
 LAST_WEAVE = 104
 
 
@@ -97,7 +98,7 @@ def tile_list_thompson_arm_rewards_kernel(
             tab_w.append(words)
 
         def load_tab2(b):
-            words = held([P, T2], I32, "tab2_w%d" % b)
+            words = in_slot([P, T2], I32, "tab2_w%d" % b, "tab2_w%d" % b)
             nc.sync.dma_start(out=words[:], in_=tab2_words[b].rearrange("p n t -> p (n t)").bitcast(I32))
             tab2_w.append(words)
 
@@ -180,7 +181,7 @@ def tile_list_thompson_arm_rewards_kernel(
                 in_=rounded[(b, a)][:].rearrange("p t m j -> p (t m j)"),
             )
 
-        mean_banks, noise, h_q, h_s = {}, {}, {}, {}
+        mean_banks, noise, h_bf, h_q, h_s = {}, {}, {}, {}, {}
 
         def log_stage(b):
             banks = [bank(4 * b + t) for t in range(PACK)]
@@ -223,19 +224,21 @@ def tile_list_thompson_arm_rewards_kernel(
             ts = slice(2 * u, 2 * u + 2)
             nc.vector.tensor_tensor(noise[b][:, ts, :], noise[b][:, ts, :], eps_sb[(b, u)][:], ALU.mult)
 
-        def h_stage(b):
-            h_bf = in_slot([P, S, PACK], BF16, "h_bf%d" % b, "h_bf%d" % b)
+        def add_mean(b):
+            h_bf[b] = held([P, S, PACK], BF16, "h_bf%d" % b)
             for jq in range(J_PARTS):
                 js = slice(jq * P, (jq + 1) * P)
                 nc.vector.tensor_tensor(
-                    h_bf[:, js, :].rearrange("p (c i) t -> p c t i", i=2),
+                    h_bf[b][:, js, :].rearrange("p (c i) t -> p c t i", i=2),
                     mean_banks[b][jq][:].rearrange("p (t c i) -> p c t i", t=PACK, i=2),
                     noise[b][:, :, js].rearrange("p t (c i) -> p c t i", i=2),
                     ALU.add,
                 )
-            h_q[b] = held([P, S], U32, "h_q%d" % b)
+
+        def quantise_h(b):
+            h_q[b] = in_slot([P, S], U32, "h_q%d" % b, "h_q0" if b == 0 else "tab2_w0")
             h_s[b] = held([P, S], U8, "h_s%d" % b)
-            nc.vector.quantize_mx(out=h_q[b][:].bitcast(FP8X4), scales=h_s[b][:], in_=h_bf[:].rearrange("p j t -> p (j t)"))
+            nc.vector.quantize_mx(out=h_q[b][:].bitcast(FP8X4), scales=h_s[b][:], in_=h_bf[b][:].rearrange("p j t -> p (j t)"))
 
         v2_w = {}
 
@@ -247,8 +250,8 @@ def tile_list_thompson_arm_rewards_kernel(
             )
             v2_w[(b, g)] = words
 
-        nc.sync.dma_start(idx[:], offs)
         load_ws(0, 1)
+        nc.sync.dma_start(idx[:], offs)
         load_scale_rows(tab_sc, tab_scales)
         load_scale_rows(ws_sc, ws_scales)
         load_tab(0)
@@ -296,64 +299,82 @@ def tile_list_thompson_arm_rewards_kernel(
             quantise_wm(b, K_PASSES - 1)
             mean_pass(b, K_PASSES - 1)
             times_eps(b, 1)
-            h_stage(b)
+            add_mean(b)
+            if b == 0:
+                quantise_h(b)
         for g in range(I_GROUPS):
             gather_arms(0, g)
+        quantise_h(1)
 
         y_s = held([P, I_GROUPS, S], U8, "y_s")
         y_q = held([P, I_GROUPS, S], I32, "y_q")
-        ys = {}
+        y_banks, ys, y_bf = {}, {}, {}
+        halves = [slice(u * S // 2, (u + 1) * S // 2) for u in range(2)]
 
-        def quantise_y(g):
-            halves = [slice(u * S // 2, (u + 1) * S // 2) for u in range(2)]
-            y_bf = []
-            for u, js in enumerate(halves):
-                half = in_slot([P, S // 2, PACK], BF16, "y_bf%d%d" % (g, u), "y_bf%d%d" % (g % 2, u))
-                dst = half[:].rearrange("p (c i) t -> p c t i", i=2)
-                src = ys[g][:, :, js].rearrange("p t (c i) -> p c t i", i=2)
-                if (g, u) == (0, 1):
-                    nc.gpsimd.tensor_scalar(out=dst, in0=src, scalar1=1.0, scalar2=-0.0, op0=ALU.mult, op1=ALU.add)
-                elif (g, u) == (I_GROUPS - 1, 1):
-                    nc.scalar.copy(out=dst[:, 0:LAST_WEAVE], in_=src[:, 0:LAST_WEAVE])
-                    nc.vector.tensor_copy(out=dst[:, LAST_WEAVE:], in_=src[:, LAST_WEAVE:])
-                else:
-                    nc.vector.tensor_copy(out=dst, in_=src)
-                y_bf.append(half)
-            for u, js in enumerate(halves):
-                nc.vector.quantize_mx(
-                    out=y_q[:, g, js].bitcast(FP8X4), scales=y_s[:, g, js], in_=y_bf[u][:].rearrange("p j t -> p (j t)")
-                )
+        def y_pass(b, g, t):
+            if b == 0:
+                y_banks[(g, t)] = bank(4 * (g % 2) + t)
+            c0 = g * PASS + t * P
+            nc.tensor.matmul_mx(
+                out=y_banks[(g, t)][:],
+                lhsT=v2_w[(b, g)][:, t, :].bitcast(FP8X4),
+                lhsT_scale=v2_sc[ARM_PLANE + 4 * b : P, c0 : c0 + P],
+                rhs=h_q[b][:].bitcast(FP8X4),
+                rhs_scale=h_s[b][:],
+                start=(b == 0),
+                stop=(b == R_PASSES - 1),
+            )
 
-        for g in range(I_GROUPS):
-            y_banks = [bank(4 * (g % 2) + t) for t in range(PACK)]
-            gather_arms(1, g)
-            steps = [(b, t) for b in range(R_PASSES) for t in range(PACK)]
-            if g > 0:
-                steps = [(b, t) for t in range(PACK) for b in reversed(range(R_PASSES))]
-            first = steps[0][0]
-            for b, t in steps:
-                c0 = g * PASS + t * P
-                nc.tensor.matmul_mx(
-                    out=y_banks[t][:],
-                    lhsT=v2_w[(b, g)][:, t, :].bitcast(FP8X4),
-                    lhsT_scale=v2_sc[ARM_PLANE + 4 * b : P, c0 : c0 + P],
-                    rhs=h_q[b][:].bitcast(FP8X4),
-                    rhs_scale=h_s[b][:],
-                    start=(b == first),
-                    stop=(b != first),
-                )
+        def store_y(g):
             ys[g] = in_slot([P, PACK, S], F32, "y%d" % g, "wm%d" % g)
             y_rows = out_0[g * PASS : (g + 1) * PASS, :].rearrange("(p t) j -> p t j", t=PACK)
             rows = 1 if g == 0 else 2
             for t in range(PACK):
-                nc.scalar.activation(out=ys[g][:, t, :], in_=y_banks[t][:], func=ACT.Copy, scale=pay_cols[:, t, g : g + 1])
+                pay_col = pay_cols[:, t, g : g + 1]
+                if (g, t) != VECTOR_BANK:
+                    nc.scalar.activation(out=ys[g][:, t, :], in_=y_banks[(g, t)][:], func=ACT.Copy, scale=pay_col)
+                else:
+                    nc.vector.tensor_scalar(ys[g][:, t, :], y_banks[(g, t)][:], pay_col, None, ALU.mult)
                 if (t + 1) % rows == 0:
                     nc.sync.dma_start(out=y_rows[:, t + 1 - rows : t + 1, :], in_=ys[g][:, t + 1 - rows : t + 1, :])
-        for g in range(I_GROUPS):
-            quantise_y(g)
+
+        def weave_y(g):
+            for u, js in enumerate(halves):
+                y_bf[(g, u)] = held([P, S // 2, PACK], BF16, "y_bf%d%d" % (g, u))
+                dst = y_bf[(g, u)][:].rearrange("p (c i) t -> p c t i", i=2)
+                src = ys[g][:, :, js].rearrange("p t (c i) -> p c t i", i=2)
+                if (g, u) == (I_GROUPS - 1, 1):
+                    nc.scalar.copy(out=dst[:, 0:LAST_WEAVE], in_=src[:, 0:LAST_WEAVE])
+                    nc.vector.tensor_copy(out=dst[:, LAST_WEAVE:], in_=src[:, LAST_WEAVE:])
+                else:
+                    nc.vector.tensor_copy(out=dst, in_=src)
+
+        def quantise_y(g):
+            for u, js in enumerate(halves):
+                nc.vector.quantize_mx(
+                    out=y_q[:, g, js].bitcast(FP8X4), scales=y_s[:, g, js], in_=y_bf[(g, u)][:].rearrange("p j t -> p (j t)")
+                )
             gs = slice(g, g + 1)
             queue = nc.scalar if g == 0 else nc.sync
             queue.dma_start(out=out_1[gs].rearrange("g p m t -> p g (m t)").bitcast(I32), in_=y_q[:, gs, :])
+
+        for g in range(2):
+            for t in range(PACK):
+                y_pass(0, g, t)
+        for g in range(2):
+            gather_arms(1, g)
+            for t in range(PACK):
+                y_pass(1, g, t)
+        gather_arms(1, 2)
+        store_y(0)
+        store_y(1)
+        for t in range(PACK):
+            y_pass(0, 2, t)
+            y_pass(1, 2, t)
+        store_y(2)
+        for g in range(I_GROUPS):
+            weave_y(g)
+            quantise_y(g)
         y_scale_rows = out_2.rearrange("g (q r) m -> r q g m", r=QUAD_ROWS)
         for r in range(QUAD_ROWS):
             queue = nc.sync if r < QUAD_ROWS // 2 else nc.scalar

@@ -31,7 +31,7 @@ ALL_ON_SCALAR, ALL_ON_VECTOR = P, 0
 LAST_BLOCK_SHARE = 48
 ROUNDED_SLOTS = ("wm_bf0", "wm_bf1", "bs", "bs", "eps01", "eps10")
 ARM_PLANE = 8
-VECTOR_BANK = (1, 3)
+VECTOR_BANK = (1, 1)
 LAST_WEAVE = 104
 
 

@@ -302,7 +302,7 @@ def tile_list_thompson_arm_rewards_kernel(
             add_mean(b)
             if b == 0:
                 quantise_h(b)
-        for g in range(I_GROUPS):
+        for g in (0, 2, 1):
             gather_arms(0, g)
         quantise_h(1)
 

@@ -28,7 +28,7 @@ J_PARTS = S // P
 LIST_COLS = PASS // 16
 VEC_ROWS = R_PASSES + I_GROUPS
 ALL_ON_SCALAR, ALL_ON_VECTOR = P, 0
-LAST_BLOCK_SHARE = 48
+LAST_BLOCK_SHARE = 44
 ROUNDED_SLOTS = ("wm_bf0", "wm_bf1", "bs", "bs", "eps01", "eps10")
 ARM_PLANE = 8
 VECTOR_BANK = (1, 1)
@@ -98,7 +98,7 @@ def tile_list_thompson_arm_rewards_kernel(
             tab_w.append(words)
 
         def load_tab2(b):
-            words = in_slot([P, T2], I32, "tab2_w%d" % b, "tab2_w%d" % b)
+            words = held([P, T2], I32, "tab2_w%d" % b)
             nc.sync.dma_start(out=words[:], in_=tab2_words[b].rearrange("p n t -> p (n t)").bitcast(I32))
             tab2_w.append(words)
 
@@ -161,6 +161,13 @@ def tile_list_thompson_arm_rewards_kernel(
                     in_=v2_sc[8 * r + 4 * b + 1 : P : 32, :].bitcast(I32),
                 )
 
+        def quantise_in_halves(codes, scales, values):
+            for u in range(2):
+                cols = slice(u * PASS // 2, (u + 1) * PASS // 2)
+                nc.vector.quantize_mx(
+                    out=codes[:, cols].bitcast(FP8X4), scales=scales[:, cols], in_=values[:, PACK * cols.start : PACK * cols.stop]
+                )
+
         rounded, wm_q, wm_s = {}, {}, {}
 
         def round_wm(b, a, on_scalar):
@@ -170,16 +177,13 @@ def tile_list_thompson_arm_rewards_kernel(
             if on_scalar > 0:
                 nc.scalar.copy(out=dst[:, :, 0:on_scalar], in_=src[:, :, 0:on_scalar])
             if on_scalar < P:
-                nc.vector.tensor_copy(out=dst[:, :, on_scalar:P], in_=src[:, :, on_scalar:P])
+                for u in range(2):
+                    nc.vector.tensor_copy(out=dst[:, u, on_scalar:P], in_=src[:, u, on_scalar:P])
 
         def quantise_wm(b, a):
             wm_q[(b, a)] = held([P, PASS], U32, "wm_q%d%d" % (b, a))
             wm_s[(b, a)] = held([P, PASS], U8, "wm_s%d%d" % (b, a))
-            nc.vector.quantize_mx(
-                out=wm_q[(b, a)][:].bitcast(FP8X4),
-                scales=wm_s[(b, a)][:],
-                in_=rounded[(b, a)][:].rearrange("p t m j -> p (t m j)"),
-            )
+            quantise_in_halves(wm_q[(b, a)], wm_s[(b, a)], rounded[(b, a)][:].rearrange("p t m j -> p (t m j)"))
 
         mean_banks, noise, h_bf, h_q, h_s = {}, {}, {}, {}, {}
 
@@ -220,9 +224,12 @@ def tile_list_thompson_arm_rewards_kernel(
                         stop=(a == K_PASSES - 1 and t == PACK - 1),
                     )
 
+        halves = [slice(u * S // 2, (u + 1) * S // 2) for u in range(2)]
+
         def times_eps(b, u):
             ts = slice(2 * u, 2 * u + 2)
-            nc.vector.tensor_tensor(noise[b][:, ts, :], noise[b][:, ts, :], eps_sb[(b, u)][:], ALU.mult)
+            for js in [slice(0, S)] if u == 0 else halves:
+                nc.vector.tensor_tensor(noise[b][:, ts, js], noise[b][:, ts, js], eps_sb[(b, u)][:, :, js], ALU.mult)
 
         def add_mean(b):
             h_bf[b] = held([P, S, PACK], BF16, "h_bf%d" % b)
@@ -236,9 +243,9 @@ def tile_list_thompson_arm_rewards_kernel(
                 )
 
         def quantise_h(b):
-            h_q[b] = in_slot([P, S], U32, "h_q%d" % b, "h_q0" if b == 0 else "tab2_w0")
+            h_q[b] = held([P, S], U32, "h_q%d" % b)
             h_s[b] = held([P, S], U8, "h_s%d" % b)
-            nc.vector.quantize_mx(out=h_q[b][:].bitcast(FP8X4), scales=h_s[b][:], in_=h_bf[b][:].rearrange("p j t -> p (j t)"))
+            quantise_in_halves(h_q[b], h_s[b], h_bf[b][:].rearrange("p j t -> p (j t)"))
 
         v2_w = {}
 
@@ -300,16 +307,13 @@ def tile_list_thompson_arm_rewards_kernel(
             mean_pass(b, K_PASSES - 1)
             times_eps(b, 1)
             add_mean(b)
-            if b == 0:
-                quantise_h(b)
+            quantise_h(b)
         for g in (0, 2, 1):
             gather_arms(0, g)
-        quantise_h(1)
 
         y_s = held([P, I_GROUPS, S], U8, "y_s")
         y_q = held([P, I_GROUPS, S], I32, "y_q")
         y_banks, ys, y_bf = {}, {}, {}
-        halves = [slice(u * S // 2, (u + 1) * S // 2) for u in range(2)]
 
         def y_pass(b, g, t):
             if b == 0:
@@ -354,9 +358,9 @@ def tile_list_thompson_arm_rewards_kernel(
                 nc.vector.quantize_mx(
                     out=y_q[:, g, js].bitcast(FP8X4), scales=y_s[:, g, js], in_=y_bf[(g, u)][:].rearrange("p j t -> p (j t)")
                 )
-            gs = slice(g, g + 1)
-            queue = nc.scalar if g == 0 else nc.sync
-            queue.dma_start(out=out_1[gs].rearrange("g p m t -> p g (m t)").bitcast(I32), in_=y_q[:, gs, :])
+
+        def store_codes(gs):
+            nc.sync.dma_start(out=out_1[gs].rearrange("g p m t -> p g (m t)").bitcast(I32), in_=y_q[:, gs, :])
 
         for g in range(2):
             for t in range(PACK):
@@ -375,6 +379,8 @@ def tile_list_thompson_arm_rewards_kernel(
         for g in range(I_GROUPS):
             weave_y(g)
             quantise_y(g)
+        store_codes(slice(0, I_GROUPS - 1))
+        store_codes(slice(I_GROUPS - 1, I_GROUPS))
         y_scale_rows = out_2.rearrange("g (q r) m -> r q g m", r=QUAD_ROWS)
         for r in range(QUAD_ROWS):
             queue = nc.sync if r < QUAD_ROWS // 2 else nc.scalar

@@ -44,12 +44,14 @@ def tile_list_thompson_arm_rewards_kernel(
         keep = ctx.enter_context(tc.tile_pool(name="keep", bufs=1))
         ring = ctx.enter_context(tc.tile_pool(name="ring", bufs=1))
         psum = ctx.enter_context(tc.psum_pool(name="psum", bufs=1))
+        pools = {}
 
         def held(shape, dtype, name):
             return keep.tile(shape, dtype, name=name, align_bytes=64)
 
         def in_slot(shape, dtype, name, slot):
-            return ring.tile(shape, dtype, name=name, tag=slot, bufs=1, align_bytes=64)
+            pool = ring if slot in ("tab0", "tab1", "bs") else pools["late"]
+            return pool.tile(shape, dtype, name=name, tag=slot, bufs=1, align_bytes=64)
 
         def bank(n):
             return psum.tile([P, PASS], F32, name="bank%d" % n, tag="bank%d" % n)
@@ -57,12 +59,8 @@ def tile_list_thompson_arm_rewards_kernel(
         idx = keep.tile([P, S // 16], U16, name="idx")
         idx2 = keep.tile([P, S2 // 16], U16, name="idx2")
 
-        tab_sc = held([P, T], U8, "tab_sc")
-        ws_sc = held([P, H], U8, "ws_sc")
         tab2_sc = held([P, T2], U8, "tab2_sc")
         planes = [held([P, S + H], U8, "planes%d" % a) for a in range(K_PASSES)]
-        for cleared in [tab_sc, ws_sc, tab2_sc] + planes:
-            nc.vector.memset(cleared[:].bitcast(I32), 0)
 
         vec_rows = held([P, PASS], F32, "vec_rows")
         ident = held([P, P], F32, "ident")
@@ -98,7 +96,7 @@ def tile_list_thompson_arm_rewards_kernel(
             tab_w.append(words)
 
         def load_tab2(b):
-            words = held([P, T2], I32, "tab2_w%d" % b)
+            words = in_slot([P, T2], I32, "tab2_w%d" % b, "arms%d" % b)
             nc.sync.dma_start(out=words[:], in_=tab2_words[b].rearrange("p n t -> p (n t)").bitcast(I32))
             tab2_w.append(words)
 
@@ -118,7 +116,6 @@ def tile_list_thompson_arm_rewards_kernel(
             eps_sb[(b, u)] = rows
 
         ws_dealt = [held([P, 2 * H], U8, "ws_dealt%d" % a) for a in range(K_PASSES)]
-        v_sc_picked = held([P, S], U8, "v_sc_picked")
         staged = held([P, S + H], U8, "staged")
         v_w = []
 
@@ -128,7 +125,7 @@ def tile_list_thompson_arm_rewards_kernel(
                 in_=ws_w[a].bitcast(U16).rearrange("p (b m t) -> p b t m", b=R_PASSES, t=PACK),
             )
 
-        def stage_scales():
+        def stage_scales(tab_sc, ws_sc, v_sc_picked):
             nc.vector.tensor_copy(v_sc_picked[:], tab_sc[:].indirect(idx[:]))
             nc.vector.tensor_copy(
                 staged[:, S:].rearrange("p (b t m) -> p b t m", b=R_PASSES, t=PACK),
@@ -180,10 +177,14 @@ def tile_list_thompson_arm_rewards_kernel(
                 for u in range(2):
                     nc.vector.tensor_copy(out=dst[:, u, on_scalar:P], in_=src[:, u, on_scalar:P])
 
-        def quantise_wm(b, a):
+        def quantise_wm(b, a, in_halves):
             wm_q[(b, a)] = held([P, PASS], U32, "wm_q%d%d" % (b, a))
             wm_s[(b, a)] = held([P, PASS], U8, "wm_s%d%d" % (b, a))
-            quantise_in_halves(wm_q[(b, a)], wm_s[(b, a)], rounded[(b, a)][:].rearrange("p t m j -> p (t m j)"))
+            values = rounded[(b, a)][:].rearrange("p t m j -> p (t m j)")
+            if in_halves:
+                quantise_in_halves(wm_q[(b, a)], wm_s[(b, a)], values)
+            else:
+                nc.vector.quantize_mx(out=wm_q[(b, a)][:].bitcast(FP8X4), scales=wm_s[(b, a)][:], in_=values)
 
         mean_banks, noise, h_bf, h_q, h_s = {}, {}, {}, {}, {}
 
@@ -257,19 +258,24 @@ def tile_list_thompson_arm_rewards_kernel(
             )
             v2_w[(b, g)] = words
 
-        load_ws(0, 1)
-        nc.sync.dma_start(idx[:], offs)
-        load_scale_rows(tab_sc, tab_scales)
-        load_scale_rows(ws_sc, ws_scales)
-        load_tab(0)
-        nc.sync.dma_start(idx2[:], offs2)
-        load_tab2_scales()
-        load_ws(1, 2)
-        load_ws(2, 3)
-        load_tab(1)
-        nc.sync.dma_start(out=vec_rows[0:R_PASSES, :], in_=bs.rearrange("(b c) -> b c", c=PASS))
-        nc.sync.dma_start(out=vec_rows[R_PASSES:VEC_ROWS, :], in_=pay.rearrange("(g c) -> g c", c=PASS))
-        stage_scales()
+        with tc.tile_pool(name="head", bufs=1) as head:
+            tab_sc = head.tile([P, T], U8, name="tab_sc", align_bytes=64)
+            ws_sc = head.tile([P, H], U8, name="ws_sc", align_bytes=64)
+            v_sc_picked = head.tile([P, S], U8, name="v_sc_picked", align_bytes=64)
+            for cleared in [tab_sc, ws_sc, tab2_sc] + planes:
+                nc.vector.memset(cleared[:].bitcast(I32), 0)
+            load_ws(0, K_PASSES)
+            nc.sync.dma_start(idx[:], offs)
+            load_scale_rows(tab_sc, tab_scales)
+            load_scale_rows(ws_sc, ws_scales)
+            load_tab(0)
+            nc.sync.dma_start(idx2[:], offs2)
+            load_tab2_scales()
+            nc.sync.dma_start(out=vec_rows[0:R_PASSES, :], in_=bs.rearrange("(b c) -> b c", c=PASS))
+            nc.sync.dma_start(out=vec_rows[R_PASSES:VEC_ROWS, :], in_=pay.rearrange("(g c) -> g c", c=PASS))
+            load_tab(1)
+            stage_scales(tab_sc, ws_sc, v_sc_picked)
+        pools["late"] = ctx.enter_context(tc.tile_pool(name="late", bufs=1))
         move_planes(0)
         load_tab(2)
         move_planes(1)
@@ -299,11 +305,11 @@ def tile_list_thompson_arm_rewards_kernel(
         for b in range(R_PASSES):
             for a in range(K_PASSES - 1):
                 round_wm(b, a, ALL_ON_VECTOR if b == 0 else ALL_ON_SCALAR)
-                quantise_wm(b, a)
+                quantise_wm(b, a, b == 0)
                 mean_pass(b, a)
             times_eps(b, 0)
             round_wm(b, K_PASSES - 1, LAST_BLOCK_SHARE)
-            quantise_wm(b, K_PASSES - 1)
+            quantise_wm(b, K_PASSES - 1, True)
             mean_pass(b, K_PASSES - 1)
             times_eps(b, 1)
             add_mean(b)

@@ -30,6 +30,7 @@ VEC_ROWS = R_PASSES + I_GROUPS
 ALL_ON_SCALAR, ALL_ON_VECTOR = P, 0
 LAST_BLOCK_SHARE = 44
 ROUNDED_SLOTS = ("wm_bf0", "wm_bf1", "bs", "bs", "eps01", "eps10")
+ROW_OFFSETS = (0, 6, 4)
 ARM_PLANE = 8
 VECTOR_BANK = (1, 1)
 LAST_WEAVE = 104
@@ -82,7 +83,7 @@ def tile_list_thompson_arm_rewards_kernel(
         def load_scale_rows(rows, scales):
             by_block = scales.rearrange("a q t -> q a t").bitcast(I32)
             nc.sync.dma_start(out=rows[0:P:4, :].bitcast(I32), in_=by_block[:, 0:K_PASSES:2, :])
-            nc.sync.dma_start(out=rows[2:P:8, :].bitcast(I32), in_=by_block[:, 1, :])
+            nc.sync.dma_start(out=rows[ROW_OFFSETS[1] : P : 8, :].bitcast(I32), in_=by_block[:, 1, :])
 
         def load_ws(first, last):
             words = held([P, last - first, H // 2], I32, "ws_w%d" % first)
@@ -116,7 +117,7 @@ def tile_list_thompson_arm_rewards_kernel(
             eps_sb[(b, u)] = rows
 
         ws_dealt = [held([P, 2 * H], U8, "ws_dealt%d" % a) for a in range(K_PASSES)]
-        staged = held([P, S + H], U8, "staged")
+        staged = planes[0]
         v_w = []
 
         def deal_ws(a):
@@ -134,8 +135,9 @@ def tile_list_thompson_arm_rewards_kernel(
             nc.vector.tensor_copy(staged[:, 0:S].bitcast(I32), v_sc_picked[:].bitcast(I32))
 
         def move_planes(a):
-            for r in range(QUAD_ROWS):
-                nc.sync.dma_start(out=planes[a][r:P:32, :].bitcast(I32), in_=staged[8 * r + 2 * a : P : 32, :].bitcast(I32))
+            for r in range(1 if a == 0 else 0, QUAD_ROWS):
+                src = staged[8 * r + ROW_OFFSETS[a] : P : 32, :]
+                nc.sync.dma_start(out=planes[a][r:P:32, :].bitcast(I32), in_=src.bitcast(I32))
 
         def gather_visitors(a):
             words = held([P, S], U32, "v_w%d" % a)
@@ -262,7 +264,7 @@ def tile_list_thompson_arm_rewards_kernel(
             tab_sc = head.tile([P, T], U8, name="tab_sc", align_bytes=64)
             ws_sc = head.tile([P, H], U8, name="ws_sc", align_bytes=64)
             v_sc_picked = head.tile([P, S], U8, name="v_sc_picked", align_bytes=64)
-            for cleared in [tab_sc, ws_sc, tab2_sc] + planes:
+            for cleared in [tab_sc, ws_sc, tab2_sc] + planes[1:]:
                 nc.vector.memset(cleared[:].bitcast(I32), 0)
             load_ws(0, K_PASSES)
             nc.sync.dma_start(idx[:], offs)

from contextlib import ExitStack

import concourse.mybir as mybir
from concourse.masks import make_identity

K, H, T, S, T2, S2 = 1536, 1024, 2048, 512, 4096, 1536
FLOPS = 2 * (2 * K * H * S + H * S2 * S)

F32 = mybir.dt.float32
BF16 = mybir.dt.bfloat16
I32 = mybir.dt.int32
U32 = mybir.dt.uint32
U16 = mybir.dt.uint16
U8 = mybir.dt.uint8
FP8X4 = mybir.dt.float8_e4m3fn_x4
FP4X4 = mybir.dt.float4_e2m1fn_x4
ALU = mybir.AluOpType
ACT = mybir.ActivationFunctionType

P = 128
PACK = 4
PASS = P * PACK
K_PASSES = K // PASS
R_PASSES = H // PASS
I_GROUPS = S2 // PASS
QUAD_ROWS = 4
J_PARTS = S // P
LIST_COLS = PASS // 16
VEC_ROWS = R_PASSES + I_GROUPS
ALL_ON_SCALAR, ALL_ON_VECTOR = P, 0
LAST_BLOCK_SHARE = 44
ROUNDED_SLOTS = ("wm_bf0", "wm_bf1", "bs", "bs", "eps01", "eps10")
ROW_OFFSETS = (0, 6, 4)
ARM_PLANE = 8
VECTOR_BANK = (1, 1)
LAST_WEAVE = 104


def tile_list_thompson_arm_rewards_kernel(
    tc, tab_words, tab_scales, offs, tab2_words, tab2_scales, offs2, wm, ws_words, ws_scales, bs, eps, pay,
    out_0, out_1, out_2,
):
    nc = tc.nc
    with ExitStack() as ctx:
        keep = ctx.enter_context(tc.tile_pool(name="keep", bufs=1))
        ring = ctx.enter_context(tc.tile_pool(name="ring", bufs=1))
        psum = ctx.enter_context(tc.psum_pool(name="psum", bufs=1))
        pools = {}

        def held(shape, dtype, name):
            return keep.tile(shape, dtype, name=name, align_bytes=64)

        def in_slot(shape, dtype, name, slot):
            pool = ring if slot in ("tab0", "tab1", "bs") else pools["late"]
            return pool.tile(shape, dtype, name=name, tag=slot, bufs=1, align_bytes=64)

        def bank(n):
            return psum.tile([P, PASS], F32, name="bank%d" % n, tag="bank%d" % n)

        idx = keep.tile([P, S // 16], U16, name="idx")
        idx2 = keep.tile([P, S2 // 16], U16, name="idx2")

        tab2_sc = held([P, T2], U8, "tab2_sc")
        planes = [held([P, S + H], U8, "planes%d" % a) for a in range(K_PASSES)]

        vec_rows = held([P, PASS], F32, "vec_rows")
        ident = held([P, P], F32, "ident")
        bs_cols = in_slot([P, PACK, R_PASSES], F32, "bs_cols", "bs")
        pay_cols = held([P, PACK, I_GROUPS], F32, "pay_cols")
        nc.gpsimd.memset(vec_rows[:], 0.0)
        make_identity(nc, ident[:])

        tab_w, tab2_w, ws_w, eps_sb, wm_raw = [], [], {}, {}, {}

        def turn_vectors():
            turned = bank(7)
            for t in range(PACK):
                nc.tensor.transpose(turned[:, t * P : (t + 1) * P], vec_rows[:, t:PASS:PACK], ident[:])
            cols = turned[:].rearrange("p (t c) -> p t c", t=PACK)
            nc.scalar.copy(out=bs_cols[:], in_=cols[:, :, 0:R_PASSES])
            nc.scalar.copy(out=pay_cols[:], in_=cols[:, :, R_PASSES:VEC_ROWS])

        def load_scale_rows(rows, scales):
            by_block = scales.rearrange("a q t -> q a t").bitcast(I32)
            nc.sync.dma_start(out=rows[0:P:4, :].bitcast(I32), in_=by_block[:, 0:K_PASSES:2, :])
            nc.sync.dma_start(out=rows[ROW_OFFSETS[1] : P : 8, :].bitcast(I32), in_=by_block[:, 1, :])

        def load_ws(first, last):
            words = held([P, last - first, H // 2], I32, "ws_w%d" % first)
            nc.sync.dma_start(out=words[:], in_=ws_words[first:last].rearrange("a p c -> p a c").bitcast(I32))
            for a in range(first, last):
                ws_w[a] = words[:, a - first, :]

        def load_tab(a):
            words = in_slot([P, T], I32, "tab_w%d" % a, "tab%d" % a)
            nc.sync.dma_start(out=words[:], in_=tab_words[a].rearrange("p n t -> p (n t)").bitcast(I32))
            tab_w.append(words)

        def load_tab2(b):
            words = in_slot([P, T2], I32, "tab2_w%d" % b, "arms%d" % b)
            nc.sync.dma_start(out=words[:], in_=tab2_words[b].rearrange("p n t -> p (n t)").bitcast(I32))
            tab2_w.append(words)

        def load_tab2_scales():
            nc.sync.dma_start(out=tab2_sc[1:P:4, :].bitcast(I32), in_=tab2_scales.rearrange("b q t -> q b t").bitcast(I32))

        def load_wm(b, a):
            raw = in_slot([P, PACK, PASS], F32, "wm_raw%d%d" % (b, a), "wm%d" % (K_PASSES * b + a))
            block = wm[a * PASS : (a + 1) * PASS, b * PASS : (b + 1) * PASS]
            nc.sync.dma_start(out=raw[:], in_=block.rearrange("(p j) c -> p j c", j=PACK))
            wm_raw[(b, a)] = raw[:]

        def load_eps(b, u):
            rows = in_slot([P, 2, S], F32, "eps%d%d" % (b, u), "eps%d%d" % (b, u))
            src = eps[b * PASS : (b + 1) * PASS, :].rearrange("(p t) j -> p t j", t=PACK)
            nc.sync.dma_start(out=rows[:], in_=src[:, 2 * u : 2 * u + 2, :])
            eps_sb[(b, u)] = rows

        ws_dealt = [held([P, 2 * H], U8, "ws_dealt%d" % a) for a in range(K_PASSES)]
        staged = planes[0]
        v_w = []

        def deal_ws(a):
            nc.scalar.copy(
                out=ws_dealt[a][:].bitcast(U16).rearrange("p (b t m) -> p b t m", b=R_PASSES, t=PACK),
                in_=ws_w[a].bitcast(U16).rearrange("p (b m t) -> p b t m", b=R_PASSES, t=PACK),
            )

        def stage_scales(tab_sc, ws_sc, v_sc_picked):
            nc.vector.tensor_copy(v_sc_picked[:], tab_sc[:].indirect(idx[:]))
            nc.vector.tensor_copy(
                staged[:, S:].rearrange("p (b t m) -> p b t m", b=R_PASSES, t=PACK),
                ws_sc[:].rearrange("p (b m t) -> p b t m", b=R_PASSES, t=PACK),
            )
            nc.vector.tensor_copy(staged[:, 0:S].bitcast(I32), v_sc_picked[:].bitcast(I32))

        def move_planes(a):
            for r in range(1 if a == 0 else 0, QUAD_ROWS):
                src = staged[8 * r + ROW_OFFSETS[a] : P : 32, :]
                nc.sync.dma_start(out=planes[a][r:P:32, :].bitcast(I32), in_=src.bitcast(I32))

        def gather_visitors(a):
            words = held([P, S], U32, "v_w%d" % a)
            nc.vector.tensor_copy(words[:], tab_w[a][:].bitcast(U32).indirect(idx[:]))
            v_w.append(words)

        v2_sc = held([P, S2], U8, "v2_sc")

        def gather_arm_scales(g, picked):
            nc.vector.tensor_copy(picked[:], tab2_sc[:].indirect(idx2[:, g * LIST_COLS : (g + 1) * LIST_COLS]))
            nc.vector.tensor_copy(
                v2_sc[:, g * PASS : (g + 1) * PASS].rearrange("p (u e m) -> p u e m", u=2, e=2),
                picked[:].rearrange("p (m u e) -> p u e m", u=2, e=2),
            )

        def move_arm_scales(b):
            for r in (0, 2, 3):
                nc.sync.dma_start(
                    out=v2_sc[ARM_PLANE + 4 * b + r : P : 32, :].bitcast(I32),
                    in_=v2_sc[8 * r + 4 * b + 1 : P : 32, :].bitcast(I32),
                )

        def quantise_in_halves(codes, scales, values):
            for u in range(2):
                cols = slice(u * PASS // 2, (u + 1) * PASS // 2)
                nc.vector.quantize_mx(
                    out=codes[:, cols].bitcast(FP8X4), scales=scales[:, cols], in_=values[:, PACK * cols.start : PACK * cols.stop]
                )

        rounded, wm_q, wm_s = {}, {}, {}

        def round_wm(b, a, on_scalar):
            rounded[(b, a)] = in_slot([P, PACK, P, PACK], BF16, "wm_bf%d%d" % (b, a), ROUNDED_SLOTS[K_PASSES * b + a])
            dst = rounded[(b, a)][:].rearrange("p (u e) m j -> p u m j e", e=2)
            src = wm_raw[(b, a)].rearrange("p j (m u e) -> p u m j e", u=2, e=2)
            if on_scalar > 0:
                nc.scalar.copy(out=dst[:, :, 0:on_scalar], in_=src[:, :, 0:on_scalar])
            if on_scalar < P:
                for u in range(2):
                    nc.vector.tensor_copy(out=dst[:, u, on_scalar:P], in_=src[:, u, on_scalar:P])

        def quantise_wm(b, a, in_halves):
            wm_q[(b, a)] = held([P, PASS], U32, "wm_q%d%d" % (b, a))
            wm_s[(b, a)] = held([P, PASS], U8, "wm_s%d%d" % (b, a))
            values = rounded[(b, a)][:].rearrange("p t m j -> p (t m j)")
            if in_halves:
                quantise_in_halves(wm_q[(b, a)], wm_s[(b, a)], values)
            else:
                nc.vector.quantize_mx(out=wm_q[(b, a)][:].bitcast(FP8X4), scales=wm_s[(b, a)][:], in_=values)

        mean_banks, noise, h_bf, h_q, h_s = {}, {}, {}, {}, {}

        def log_stage(b):
            banks = [bank(4 * b + t) for t in range(PACK)]
            steps = [(a, t) for a in range(K_PASSES) for t in range(PACK)]
            if b == 1:
                steps = [(a, t) for t in range(PACK) for a in reversed(range(K_PASSES))]
            first, last = steps[0][0], steps[-1][0]
            for a, t in steps:
                c0 = b * PASS + t * P
                nc.tensor.matmul_mx(
                    out=banks[t][:],
                    lhsT=ws_dealt[a][:, 2 * c0 : 2 * (c0 + P)].bitcast(FP4X4),
                    lhsT_scale=planes[a][:, S + c0 : S + c0 + P],
                    rhs=v_w[a][:].bitcast(FP8X4),
                    rhs_scale=planes[a][:, 0:S],
                    start=(a == first),
                    stop=(a == last),
                )
            noise[b] = in_slot([P, PACK, S], F32, "noise%d" % b, "tab%d" % b)
            for t in range(PACK):
                nc.scalar.activation(out=noise[b][:, t, :], in_=banks[t][:], func=ACT.Exp, bias=bs_cols[:, t, b : b + 1])

        def mean_pass(b, a):
            if a == 0:
                mean_banks[b] = [bank(4 * b + jq) for jq in range(J_PARTS)]
            for jq in range(J_PARTS):
                for t in range(PACK):
                    ms = slice(t * P, (t + 1) * P)
                    nc.tensor.matmul_mx(
                        out=mean_banks[b][jq][:, ms],
                        lhsT=wm_q[(b, a)][:, ms].bitcast(FP8X4),
                        lhsT_scale=wm_s[(b, a)][:, ms],
                        rhs=v_w[a][:, jq * P : (jq + 1) * P].bitcast(FP8X4),
                        rhs_scale=planes[a][:, jq * P : (jq + 1) * P],
                        start=(a == 0 and t == 0),
                        stop=(a == K_PASSES - 1 and t == PACK - 1),
                    )

        halves = [slice(u * S // 2, (u + 1) * S // 2) for u in range(2)]

        def times_eps(b, u):
            ts = slice(2 * u, 2 * u + 2)
            for js in [slice(0, S)] if u == 0 else halves:
                nc.vector.tensor_tensor(noise[b][:, ts, js], noise[b][:, ts, js], eps_sb[(b, u)][:, :, js], ALU.mult)

        def add_mean(b):
            h_bf[b] = held([P, S, PACK], BF16, "h_bf%d" % b)
            for jq in range(J_PARTS):
                js = slice(jq * P, (jq + 1) * P)
                nc.vector.tensor_tensor(
                    h_bf[b][:, js, :].rearrange("p (c i) t -> p c t i", i=2),
                    mean_banks[b][jq][:].rearrange("p (t c i) -> p c t i", t=PACK, i=2),
                    noise[b][:, :, js].rearrange("p t (c i) -> p c t i", i=2),
                    ALU.add,
                )

        def quantise_h(b):
            h_q[b] = held([P, S], U32, "h_q%d" % b)
            h_s[b] = held([P, S], U8, "h_s%d" % b)
            quantise_in_halves(h_q[b], h_s[b], h_bf[b][:].rearrange("p j t -> p (j t)"))

        v2_w = {}

        def gather_arms(b, g):
            words = held([P, PACK, P], U32, "v2_w%d%d" % (b, g))
            nc.vector.tensor_copy(
                words[:].rearrange("p t m -> p m t"),
                tab2_w[b][:].bitcast(U32).indirect(idx2[:, g * LIST_COLS : (g + 1) * LIST_COLS]),
            )
            v2_w[(b, g)] = words

        with tc.tile_pool(name="head", bufs=1) as head:
            tab_sc = head.tile([P, T], U8, name="tab_sc", align_bytes=64)
            ws_sc = head.tile([P, H], U8, name="ws_sc", align_bytes=64)
            v_sc_picked = head.tile([P, S], U8, name="v_sc_picked", align_bytes=64)
            for cleared in [tab_sc, ws_sc, tab2_sc] + planes[1:]:
                nc.vector.memset(cleared[:].bitcast(I32), 0)
            load_ws(0, K_PASSES)
            nc.sync.dma_start(idx[:], offs)
            load_scale_rows(tab_sc, tab_scales)
            load_scale_rows(ws_sc, ws_scales)
            load_tab(0)
            nc.sync.dma_start(idx2[:], offs2)
            load_tab2_scales()
            nc.sync.dma_start(out=vec_rows[0:R_PASSES, :], in_=bs.rearrange("(b c) -> b c", c=PASS))
            nc.sync.dma_start(out=vec_rows[R_PASSES:VEC_ROWS, :], in_=pay.rearrange("(g c) -> g c", c=PASS))
            load_tab(1)
            stage_scales(tab_sc, ws_sc, v_sc_picked)
        pools["late"] = ctx.enter_context(tc.tile_pool(name="late", bufs=1))
        move_planes(0)
        load_tab(2)
        move_planes(1)
        load_wm(0, 0)
        move_planes(2)
        for a in range(K_PASSES):
            deal_ws(a)
        gather_visitors(0)
        gather_arm_scales(0, held([P, PASS], U8, "arm_sc0"))
        gather_visitors(1)
        gather_arm_scales(1, in_slot([P, PASS], U8, "arm_sc1", "tab1"))
        gather_visitors(2)
        gather_arm_scales(2, in_slot([P, PASS], U8, "arm_sc2", "tab2"))
        for b in range(R_PASSES):
            if b > 0:
                load_wm(b, 0)
            load_wm(b, 1)
            load_eps(b, 0)
            load_wm(b, 2)
            move_arm_scales(b)
            load_eps(b, 1)
        load_tab2(0)
        load_tab2(1)
        turn_vectors()
        log_stage(0)
        log_stage(1)
        for b in range(R_PASSES):
            for a in range(K_PASSES - 1):
                round_wm(b, a, ALL_ON_VECTOR if b == 0 else ALL_ON_SCALAR)
                quantise_wm(b, a, b == 0)
                mean_pass(b, a)
            times_eps(b, 0)
            round_wm(b, K_PASSES - 1, LAST_BLOCK_SHARE)
            quantise_wm(b, K_PASSES - 1, True)
            mean_pass(b, K_PASSES - 1)
            times_eps(b, 1)
            add_mean(b)
            quantise_h(b)
        for g in (0, 2, 1):
            gather_arms(0, g)

        y_s = held([P, I_GROUPS, S], U8, "y_s")
        y_q = held([P, I_GROUPS, S], I32, "y_q")
        y_banks, ys, y_bf = {}, {}, {}

        def y_pass(b, g, t):
            if b == 0:
                y_banks[(g, t)] = bank(4 * (g % 2) + t)
            c0 = g * PASS + t * P
            nc.tensor.matmul_mx(
                out=y_banks[(g, t)][:],
                lhsT=v2_w[(b, g)][:, t, :].bitcast(FP8X4),
                lhsT_scale=v2_sc[ARM_PLANE + 4 * b : P, c0 : c0 + P],
                rhs=h_q[b][:].bitcast(FP8X4),
                rhs_scale=h_s[b][:],
                start=(b == 0),
                stop=(b == R_PASSES - 1),
            )

        def store_y(g):
            ys[g] = in_slot([P, PACK, S], F32, "y%d" % g, "wm%d" % g)
            y_rows = out_0[g * PASS : (g + 1) * PASS, :].rearrange("(p t) j -> p t j", t=PACK)
            rows = 1 if g == 0 else 2
            for t in range(PACK):
                pay_col = pay_cols[:, t, g : g + 1]
                if (g, t) != VECTOR_BANK:
                    nc.scalar.activation(out=ys[g][:, t, :], in_=y_banks[(g, t)][:], func=ACT.Copy, scale=pay_col)
                else:
                    nc.vector.tensor_scalar(ys[g][:, t, :], y_banks[(g, t)][:], pay_col, None, ALU.mult)
                if (t + 1) % rows == 0:
                    nc.sync.dma_start(out=y_rows[:, t + 1 - rows : t + 1, :], in_=ys[g][:, t + 1 - rows : t + 1, :])

        def weave_y(g):
            for u, js in enumerate(halves):
                y_bf[(g, u)] = held([P, S // 2, PACK], BF16, "y_bf%d%d" % (g, u))
                dst = y_bf[(g, u)][:].rearrange("p (c i) t -> p c t i", i=2)
                src = ys[g][:, :, js].rearrange("p t (c i) -> p c t i", i=2)
                if (g, u) == (I_GROUPS - 1, 1):
                    nc.scalar.copy(out=dst[:, 0:LAST_WEAVE], in_=src[:, 0:LAST_WEAVE])
                    nc.vector.tensor_copy(out=dst[:, LAST_WEAVE:], in_=src[:, LAST_WEAVE:])
                else:
                    nc.vector.tensor_copy(out=dst, in_=src)

        def quantise_y(g):
            for u, js in enumerate(halves):
                nc.vector.quantize_mx(
                    out=y_q[:, g, js].bitcast(FP8X4), scales=y_s[:, g, js], in_=y_bf[(g, u)][:].rearrange("p j t -> p (j t)")
                )

        def store_codes(gs):
            nc.sync.dma_start(out=out_1[gs].rearrange("g p m t -> p g (m t)").bitcast(I32), in_=y_q[:, gs, :])

        for g in range(2):
            for t in range(PACK):
                y_pass(0, g, t)
        for g in range(2):
            gather_arms(1, g)
            for t in range(PACK):
                y_pass(1, g, t)
        gather_arms(1, 2)
        store_y(0)
        store_y(1)
        for t in range(PACK):
            y_pass(0, 2, t)
            y_pass(1, 2, t)
        store_y(2)
        for g in range(I_GROUPS):
            weave_y(g)
            quantise_y(g)
        store_codes(slice(0, I_GROUPS - 1))
        store_codes(slice(I_GROUPS - 1, I_GROUPS))
        y_scale_rows = out_2.rearrange("g (q r) m -> r q g m", r=QUAD_ROWS)
        for r in range(QUAD_ROWS):
            queue = nc.sync if r < QUAD_ROWS // 2 else nc.scalar
            queue.dma_start(out=y_scale_rows[r].bitcast(I32), in_=y_s[r:P:32, :, :].bitcast(I32))
